import numpy as np, ml_dtypes
CORES = [242,247,114,119]
N = 4
BF = ml_dtypes.bfloat16
def gentries(a):
    return np.ascontiguousarray(a.reshape(8, 16, -1).transpose(0, 2, 1)).reshape(8, -1)
def gtable(e):
    e = np.asarray(e); return np.ascontiguousarray(e.reshape(8, -1, 16).transpose(0, 2, 1)).reshape(128, -1).astype(np.int32)
V, G, CAP, Q, C, CL, RO = 1792, 512, 80, (64, 64, 128), 3, 4, 3
W = V + (N - 1) * G
def ghosted(xs):
    return np.stack([np.concatenate([xs[a]] + [xs[(a - d) % N][:, :, :G] for d in range(1, N)], axis=2) for a in range(N)])
def drawn(n, t, sd):
    r = []
    for c in range(C):
        if n[c] >= Q[c]:
            st = 4096 // Q[c]; b = (41 * t + 13 * n[0] + sd[c]) & (st - 1)
            r.append(V * c + (((np.arange(Q[c]) * st + b) * n[c]) >> 12))
    return np.concatenate(r)
def move(w, nb, s):
    m = np.add.reduce(w[:, nb[:, s]], axis=1) >> 4
    w[:, s] = w[:, s] + np.minimum(np.maximum(m - w[:, s], -CL), CL)
def hand(w, s):
    for a in range(N):
        for g in range(8):
            lo = np.sort(s[a][g]); lo = lo[lo < G][:CAP]
            for d in range(1, N): w[(a + d) % N, g][:, V + (d - 1) * G + lo] = w[a, g][:, lo]
def touched(nb, s):
    return np.unique(np.concatenate([s, nb[0, s]]))
def energy(w, nb, s):
    return np.sum(np.abs(w[:, nb[:, s]] - w[:, None, s]), axis=(0, 1))
def lay(n):
    return np.concatenate([V * c + np.arange(n[c]) for c in range(C)])
def force(rng, c, k):
    cuts = np.sort(rng.integers(0, V - k + 1, C - 2)); p = np.diff(np.concatenate([np.array([0]), cuts, np.array([V - k])]))
    return np.insert(p, c, k)
def parts(rng):
    amp = rng.choice(np.array([3, 12, 40, 127]), (N, 8, 1, V)); xs = 128 + rng.integers(-127, 128, (N, 8, 16, V)) * amp // 127
    nbr = rng.integers(0, W, (N, 8, 16, V)); nbr[:, :, 0] = np.argsort(rng.random((N, 8, V)), axis=2)
    z = np.zeros((N, 8, 1), np.int64); n = np.diff(np.concatenate([z, np.sort(rng.integers(0, V + 1, (N, 8, C - 1)), axis=2), z + V], axis=2), axis=2)
    o = np.argsort(rng.random((N, 8, V)), axis=2); sd = rng.integers(0, 4096, (N, 8, C))
    return xs, nbr, n, o, sd
def quant(rng, xs, nbr):
    w = ghosted(xs); th = np.zeros((N, 8, C - 1), np.int64)
    for a in range(N):
        for g in range(8): th[a, g] = np.sort(energy(w[a, g], nbr[a, g], rng.integers(0, V, 256)))[np.sort(rng.integers(16, 240, C - 1))]
    return th
def watched(rng, g, t, xs, nbr, n, o, th, sd):
    one = V * np.eye(C, dtype=np.int64)[C - 1]
    for a in range(0, N, 2):
        n[a, g] = V // C; n[a, g, C - 1] += V - C * (V // C)
        if t > 0: n[a, g] = one; th[a, g] = 0
        at = [np.searchsorted(lay(n[a, g]), drawn(n[a, g], u, sd[a, g])) for u in range(t + 1)]
        p = at[t]; early = np.concatenate([np.zeros(0, np.int64)] + at[:t]); m = np.ones(V, bool); m[p] = False; m[early] = False
        lo = rng.permutation(G); hi = G + rng.permutation(V - G); q = o[a, g]
        q[p] = lo[:len(p)]; q[early] = hi[:len(early)]; q[m] = rng.permutation(np.concatenate([lo[len(p):], hi[len(early):]]))
        xs[a, g] = 200; xs[a, g][:, :G] = 100; nbr[a, g, 0] = np.arange(V); nbr[a, g, 1:] = rng.integers(G, V, (15, V))
        z = np.sort(q[p]); still = rng.random(len(z)) < 0.5; still[CAP - 1:CAP + 1] = False
        nbr[a, g, 1:][:, z[still]] = z[still]
        b = a + 1; n[b, g] = one; xs[b, g] = 200; th[b, g] = 240 * (100 - CL)
        come = o[b, g][np.searchsorted(lay(one), drawn(one, t, sd[b, g]))]
        nbr[b, g, 0] = np.arange(V); nbr[b, g, 1:] = V + rng.choice(z, V)
        nbr[b, g, 1:][:, come] = V + rng.permutation(z[:len(come)])
def pack(xs, nbr, n, o, th, sd):
    pl = np.zeros((N, 8, V), np.int64)
    for a in range(N):
        for g in range(8): pl[a, g, o[a, g]] = lay(n[a, g])
    return {"x": np.ascontiguousarray(xs.reshape(N, 128, V)).astype(np.float32).astype(BF), "nb": np.ascontiguousarray(nbr.reshape(N, 128, V)).astype(np.int32),
            "plc": np.stack([gtable(p) for p in pl]), "th": th.astype(np.int32), "sd": sd.astype(np.int32)}
def setup_inputs(rng):
    xs, nbr, n, o, sd = parts(rng)
    for a in range(N): n[a, (3 * a + 2) % 8] = force(rng, a % C, int(rng.integers(0, Q[a % C])))
    return pack(xs, nbr, n, o, quant(rng, xs, nbr), sd)
def setup_inputs_room(rng):
    xs, nbr, n, o, sd = parts(rng)
    for a in range(N):
        for g in range(8):
            if a == 0:
                n[a, g] = V // C; n[a, g, C - 1] += V - C * (V // C); k = (CAP, CAP + 1, 2 * CAP, CAP - 1, 1, 0, CAP, CAP + 1)[g]
            else:
                c = (g + a) % C; n[a, g] = force(rng, c, (Q[c] - 1, Q[c], Q[c] + 1, 0)[(g + g // 4) % 4]); k = int(rng.choice(np.array([0, 1, CAP - 1, CAP, CAP + 1, 2 * CAP])))
            p = np.searchsorted(lay(n[a, g]), drawn(n[a, g], 0, sd[a, g])); k = min(k, len(p)); h = len(p) - k
            lo = rng.permutation(G); hi = G + rng.permutation(V - G); m = np.ones(V, bool); m[p] = False; q = o[a, g]
            q[p] = rng.permutation(np.concatenate([lo[:k], hi[:h]])); q[m] = rng.permutation(np.concatenate([lo[k:], hi[h:]]))
    return pack(xs, nbr, n, o, quant(rng, xs, nbr), sd)
def setup_inputs_ties(rng):
    xs, nbr, n, o, sd = parts(rng); xs[:, ::2] = 100 + rng.integers(0, 4, (N, 4, 16, V)); xs[:, 4] = 77
    for a in range(N):
        q = rng.permutation(V); lo = q[:V // 2]; hi = q[V // 2:]; xs[a, 6] = 0; xs[a, 6][:, hi] = 255
        nbr[a, 6, 0][lo] = hi; nbr[a, 6, 0][hi] = np.roll(lo, -1)
        nbr[a, 6, 1:][:, lo] = rng.choice(hi, (15, V // 2)); nbr[a, 6, 1:][:, hi] = rng.choice(lo, (15, V // 2))
    w = ghosted(xs); s = [[o[a, g][np.searchsorted(lay(n[a, g]), drawn(n[a, g], 0, sd[a, g]))] for g in range(8)] for a in range(N)]; th = np.zeros((N, 8, C - 1), np.int64)
    for a in range(N):
        for g in range(8): move(w[a, g], nbr[a, g], s[a][g])
    hand(w, s)
    for a in range(N):
        for g in range(8):
            e = energy(w[a, g], nbr[a, g], touched(nbr[a, g], s[a][g])); th[a, g] = e[rng.integers(0, len(e), C - 1)] + rng.integers(0, 2, C - 1)
    th[:, 1] = th[:, 1, :1]; th[::2, 6, 0] = 65280
    return pack(xs, nbr, n, o, th, sd)
def setup_inputs_flood(rng):
    xs, nbr, n, o, sd = parts(rng); th = quant(rng, xs, nbr); one = V * np.eye(C, dtype=np.int64)
    n[:, 0] = one[0]; th[:, 0] = 0; n[:, 1] = one[C - 1]; th[:, 1] = 65536; nbr[:, 2, 0] = np.arange(V); n[:, 5] = one[C - 1]; th[:, 5] = 0
    th[:, 4] = 0; th[:, 6] = 65536; th[:, 7] = 65536 * rng.integers(0, 2, (N, C - 1))
    for a in range(N):
        nbr[a, 3, 0][o[a, 3]] = np.roll(o[a, 3], -1); n[a, 4] = force(rng, 0, Q[0]); n[a, 6] = force(rng, C - 1, Q[C - 1])
    for a in range(0, N, 2):
        k = V // C; n[a, 5] = k; n[a, 5, C - 1] = V - (C - 1) * k; th[a, 5] = 32768; q = o[a, 5]
        for c in range(C):
            m = q[c * k:c * k + n[a, 5, c]]; nbr[a, 5, 0][m] = np.roll(m, -1)
        nbr[a, 5, 1:] = rng.choice(q[k:], (15, V)); xs[a, 5] = 0; xs[a, 5][:, q[:k]] = 255
    for a in range(1, N, 2):
        n[a, 1] = max(Q); k = (C - 1) * max(Q); n[a, 1, C - 1] = V - k; q = o[a, 1]
        p = np.searchsorted(lay(n[a, 1]), drawn(n[a, 1], 0, sd[a, 1])); m = np.ones(V, bool); m[p] = False
        early = k + np.flatnonzero(m[k:V - len(p) - Q[C - 1]]); early = rng.permutation(early)[:len(p)]; r = np.ones(V, bool); r[early] = False
        nbr[a, 1, 0][q[p]] = q[early]; nbr[a, 1, 0][q[m]] = rng.permutation(q[r])
    return pack(xs, nbr, n, o, th, sd)
def setup_inputs_alike(rng):
    xs, nbr, n, o, sd = parts(rng); xs[:, ::2] = 255 * rng.integers(0, 2, (N, 4, 16, V))
    nbr[:, 1, 1:] = rng.choice(np.array([0, V - 1, V, W - 1]), (N, 15, V)); nbr[:, 2, 1:] = nbr[:, 2, 1:2]
    nbr[:, 3, 1:] = rng.integers(V, W, (N, 15, V)); nbr[:, 5, 1:] = rng.integers(0, V, (N, 15, V)); nbr[:, 7] = np.arange(V)
    th = quant(rng, xs, nbr)
    watched(rng, 0, 0, xs, nbr, n, o, th, sd); watched(rng, 4, RO - 1, xs, nbr, n, o, th, sd)
    return pack(xs, nbr, n, o, th, sd)
def setup_inputs_spread(rng):
    xs, nbr, n, o, sd = parts(rng)
    xs = np.minimum((np.exp2(8 * rng.random((N, 8, 1, V))) * rng.random((N, 8, 16, V))).astype(np.int64), 255)
    nbr[:, :, 1:] = W - 1 - np.minimum((W * rng.random((N, 8, 15, V)) ** 3).astype(np.int64), W - 1)
    th = quant(rng, xs, nbr); th[:, 1::2] = np.minimum(np.exp2(16 * rng.random((N, 4, C - 1))).astype(np.int64), 65536)
    sd[:, ::3] = rng.choice(np.array([0, 1, 31, 4095]), sd[:, ::3].shape)
    return pack(xs, nbr, n, o, th, sd)
def check_inputs(d):
    bad = []
    v = np.asarray(d["x"]).astype(np.float32)
    if not np.all((v >= 0) & (v <= 255) & (v == np.floor(v))): bad.append("x: whole numbers from 0 to 255")
    for k, hi in (("nb", W - 1), ("plc", C * V - 1), ("th", 65536), ("sd", 4095)):
        if np.min(d[k]) < 0 or np.max(d[k]) > hi: bad.append("range of " + k)
    if np.any(np.sort(np.asarray(d["nb"]).reshape(N, 8, 16, V)[:, :, 0], axis=2) != np.arange(V)): bad.append("first neighbours: every own site once")
    k = np.sort(np.stack([gentries(a) for a in d["plc"]]).astype(np.int64), axis=2); c = k // V; p = np.arange(V)[None, None, :]
    for j in range(C): p = p - np.where(c > j, np.count_nonzero(c == j, axis=2)[:, :, None], 0)
    if np.any(k - V * c != p): bad.append("bags filled from position 0 on, each position once")
    return bad
def reference(x, nb, plc, th, sd):
    w = ghosted(x.astype(np.float32).astype(np.int64).reshape(N, 8, 16, V)); nbr = nb.astype(np.int64).reshape(N, 8, 16, V)
    pl = np.stack([gentries(a) for a in plc]).astype(np.int64)
    bag = np.zeros((N, 8, C * V), np.int64); np.put_along_axis(bag, pl, np.broadcast_to(np.arange(V), pl.shape), 2)
    n = np.stack([np.count_nonzero(pl // V == c, axis=2) for c in range(C)], axis=2).astype(np.int64)
    tv = th.astype(np.int64); sv = sd.astype(np.int64)
    for t in range(RO):
        s = [[bag[a, g][drawn(n[a, g], t, sv[a, g])] for g in range(8)] for a in range(N)]
        for a in range(N):
            for g in range(8): move(w[a, g], nbr[a, g], s[a][g])
        hand(w, s)
        for a in range(N):
            for g in range(8):
                k, h, z = bag[a, g], pl[a, g], n[a, g]
                u = touched(nbr[a, g], s[a][g]); e = energy(w[a, g], nbr[a, g], u)
                new = np.sum(e[None, :] >= tv[a, g][:, None], axis=0); old = h[u] // V
                go = new != old; u, new, old = u[go], new[go], old[go]
                for c in range(C):
                    out = u[old == c]; left = z[c] - len(out); p = h[out]; hole = p[p < V * c + left]
                    tail = k[V * c + left:V * c + z[c]]; stay = tail[~np.isin(tail, out)]
                    k[hole] = stay; h[stay] = hole; z[c] = left
                for c in range(C):
                    come = u[new == c]; p = V * c + z[c] + np.arange(len(come))
                    k[p] = come; h[come] = p; z[c] += len(come)
    return {"yx": np.ascontiguousarray(w[:, :, :, :V]).reshape(N, 128, V).astype(np.float32).astype(BF), "yp": pl.astype(np.float32)}

@@ -1,0 +1,651 @@
+from concourse.bass import DstId, RemoteDMATransfer
+from concourse.mybir import AluOpType as A, ActivationFunctionType as AF, AxisListType as AX
+
+V, GH, CAP, RO, N = 1792, 512, 80, 3, 4
+W = V + (N - 1) * GH
+O = 256
+S1 = O + V
+PL = 3 * V
+DUMP = PL + 256
+MSG = 86
+MAGIC = 12582912.0
+F, B, H, I, U = "float32", "bfloat16", "float16", "int32", "uint16"
+MOVES = ((0, 128), (128, 192), (192, 256))
+CHUNKS = ((0, 64), (64, 192), (192, 320), (320, 448), (448, 512))
+
+
+def _sb(c, d):
+    return ("sbuf", [128, c], d)
+
+
+BUF = {
+    "w": _sb(4688, B), "nbi": _sb(V, I), "nbf": _sb(2048, F), "bag": _sb(6144, F), "plt": _sb(2560, F), "plf": _sb(2560, F), "si": _sb(2048, F),
+    "mk": _sb(3 * 2048, B), "mks": _sb(2048, B), "mk2": _sb(512, B), "w4": _sb(3 * 1536, F), "sl": _sb(3 * 512, F), "sl16": _sb(512, H),
+    "gb": _sb(8192, B), "mx": _sb(8192, B), "selt": _sb(2048, F), "xg": _sb(128, F),
+    "plci": _sb(112, I), "plcf": _sb(112, F), "plcu": _sb(112, U), "junk": _sb(224, F),
+    "prm": _sb(16, I), "prmf": _sb(8, F), "par": _sb(8, F), "col": _sb(24, F), "pint": _sb(8, I), "ea": _sb(16, F),
+    "y0": _sb(144, H), "y1": _sb(144, H), "y123": _sb(144, H), "y45": _sb(144, H), "y01b": _sb(144, B), "y0b": _sb(144, B),
+    "bdf": _sb(128, F), "bdh": _sb(128, H), "bd2": _sb(128, B), "bdm": _sb(128, B), "bd16": _sb(128, B),
+    "i16": _sb(128, B), "ineg": _sb(128, B), "ipos": _sb(128, B), "ibias": _sb(128, B), "ih": _sb(128, H), "um": _sb(128, H), "ub": _sb(128, H),
+    "e8": _sb(128, F), "ones": _sb(128, B), "m4": _sb(512, B), "jt": _sb(256, F), "mv0": _sb(256, B), "mv1": _sb(256, B), "rm": _sb(192, H),
+    "jl": _sb(32, F), "cl": _sb(32, H), "u0": _sb(16, F), "djc": _sb(16, F), "d2k": _sb(32, F), "d15": _sb(32, F), "d1k": _sb(32, F),
+    "d18": _sb(8, F), "d256": _sb(16, F), "ddmp": _sb(32, F), "qc": _sb(4, F),
+    "ns": _sb(4, F), "cnt": _sb(8, F), "sc": _sb(16, F), "bi": _sb(4, I), "bm": _sb(4, I), "bf": _sb(4, F), "iv": _sb(16, I),
+    "pr": _sb(16, I), "ps": _sb(16, I), "pm": _sb(16, F), "posu": _sb(16, U),
+    "dr": _sb(256, H), "drf": _sb(256, F), "n0h": _sb(256, H), "n0f": _sb(256, F), "tu": _sb(32, U), "gu": _sb(16, U), "nbu": _sb(512, U),
+    "t1": _sb(64, F), "oldm": _sb(256, B), "rr": _sb(256, B), "rkd": _sb(256, B), "rk": _sb(512, B), "dru": _sb(16, U), "rku": _sb(32, U),
+    "ds": _sb(512, F), "dsh": _sb(80, H), "ju": _sb(6, U), "osel": _sb(80, B), "msg": _sb(3 * MSG + 6, H), "land": _sb(9 * 88, H), "gou": _sb(24, U),
+    "su": _sb(32, U), "sf": _sb(32, F), "sv": _sb(512, B), "pb": _sb(512, F), "pb16": _sb(512, H), "ge": _sb(512, B),
+    "e1": _sb(160, F), "oh": _sb(96, F), "qj": _sb(96, F), "rq": _sb(96, F), "pp": _sb(96, F), "pos": _sb(32, F), "nq": _sb(12, F), "nqh": _sb(8, H),
+    "fl": _sb(192, H), "s1": _sb(192, H), "s2": _sb(96, H), "zz": _sb(96, F), "ho": _sb(96, H), "hs": _sb(96, H), "xx": _sb(160, F),
+    "o4": _sb(96, F), "o4u": _sb(32, U), "vv": _sb(96, F), "ww": _sb(96, F), "nl": _sb(96, F), "npl": _sb(96, F), "jou": _sb(32, U), "lvu": _sb(32, U),
+    "yy": _sb(224, F), "tpu": _sb(32, U), "tb": _sb(512, H), "ts4": _sb(512, H), "ixu": _sb(32, U), "hg": _sb(512, H), "hf": _sb(512, F),
+    "hou": _sb(32, U), "nrec": _sb(512, F), "st": _sb(96, F), "stu": _sb(32, U), "lg": _sb(16, F),
+    "pS": ("psum", [128, 512], F), "pE": ("psum", [128, 512], F), "pF": ("psum", [128, 512], F), "pM": ("psum", [128, 512], F),
+    "pA": ("psum", [128, 512], F), "pB": ("psum", [128, 512], F), "pC": ("psum", [128, 512], F), "pD": ("psum", [128, 512], F),
+}
+SCRATCH = {}
+PLACE = {}
+for _n, (_w, _s, _d) in BUF.items():
+    if _w == "sbuf" and _s[1] <= 256:
+        _at = SCRATCH.get("tiles_" + _d, (0, [0, 0]))[1][1]
+        PLACE[_n] = ("tiles_" + _d, _at)
+        SCRATCH["tiles_" + _d] = _sb(_at + (_s[1] + 15) // 16 * 16, _d)
+    else:
+        PLACE[_n] = (_n, 0)
+        SCRATCH[_n] = (_w, _s, _d)
+DMAS = 12
+SEMAPHORES = ["cv", "cs", "ct", "cg", "sent0", "sent"] + ["near%d" % k for k in range(4)] + ["far%d" % k for k in range(4)] + ["dma%d" % k for k in range(DMAS)]
+
+
+def r(name, c0=0, c1=None, step=1, p=(0, 128), off=None):
+    if c1 is None:
+        c1 = BUF[name][1][1]
+    buf, at = PLACE[name]
+    return ("ref", buf, at + c0, at + c1, step, p, off)
+
+
+def c(name, k):
+    return r(name, k, k + 1)
+
+
+def is_ref(a):
+    return isinstance(a, tuple) and len(a) == 7 and a[0] == "ref"
+
+
+def emit(g, T, ops):
+    def ap(a):
+        if not is_ref(a):
+            return a
+        _, name, c0, c1, step, p, off = a
+        t = T[name]
+        x = t[p[0]:p[1], c0:c1] if step == 1 else t[p[0]:p[1], c0:c1:step]
+        return x.indirect(ap(off)) if off is not None else x
+
+    def meet(a, b):
+        return SCRATCH[a[1]][0] == "psum" or (a[2] < b[3] and b[2] < a[3] and not (a[4] == b[4] > 1 and (a[2] - b[2]) % a[4]))
+    acc = {}
+    deps = []
+    for k, o in enumerate(ops):
+        d = set()
+        both = [(a, False) for a in o["rd"]] + [(a, True) for a in o["wr"]]
+        for a, wr in both:
+            psum = SCRATCH[a[1]][0] == "psum"
+            for j, b, bw in acc.get(a[1], []):
+                e = ops[j]["q"]
+                if not meet(a, b) or (e == "t" and o["q"] == "t"):
+                    continue
+                if wr or bw or (psum and e != o["q"]):
+                    d.add(j)
+        for a, wr in both:
+            l = acc.setdefault(a[1], [])
+            if wr and a[4] == 1 and a[6] is None and a[5] == (0, 128):
+                l[:] = [x for x in l if x[0] == k or not (a[2] <= x[1][2] and x[1][3] <= a[3])]
+            l.append((k, a, wr))
+        deps.append(d)
+    known = {q: {} for q in "vstgy"}
+    after = [None] * len(ops)
+    waits = []
+    for k, o in enumerate(ops):
+        kn = known[o["q"]]
+        need = {}
+        for j in sorted(deps[k], reverse=True):
+            key = ops[j]["ev"] or ops[j]["q"]
+            if kn.get(key, -1) >= j:
+                continue
+            need[key] = j
+            for x, y in after[j].items():
+                if kn.get(x, -1) < y:
+                    kn[x] = y
+        waits.append(sorted(need.values()))
+        after[k] = dict(kn)
+        after[k][o["ev"] or o["q"]] = k
+    marked = set(j for w in waits for j in w)
+    Q = {"v": g.vector, "s": g.scalar, "t": g.tensor, "g": g, "y": g.sync}
+    count = {q: 0 for q in "vstg"}
+    val = {}
+    top = {}
+    for k, o in enumerate(ops):
+        q = Q[o["q"]]
+        for j in waits[k]:
+            q.wait_ge(*val[j])
+        ins = o["fn"](q, [ap(a) for a in o["args"]], {x: ap(y) for x, y in o["kw"].items()})
+        if o["ev"]:
+            val[k] = (T.sem[o["ev"][0]], o["ev"][1])
+            top[o["ev"][0]] = o["ev"][1]
+            if o["ev"][2]:
+                ins.then_inc(*val[k])
+        elif k in marked:
+            count[o["q"]] += 1
+            val[k] = (T.sem["c" + o["q"]], count[o["q"]])
+            top["c" + o["q"]] = count[o["q"]]
+            ins.then_inc(val[k][0], 1)
+    for s, v in top.items():
+        g.sync.wait_ge(T.sem[s], v)
+
+
+def rank_program(g, core, T, topo):
+    rank = T.rank_of(core)
+    if rank is None:
+        return
+    ops = []
+
+    def op(q, fn, args, kw, rd, wr, ev=None):
+        rd = [a for a in rd if is_ref(a)]
+        rd += [a[6] for a in rd + wr if a[6] is not None]
+        ops.append({"q": q, "fn": fn, "args": args, "kw": kw, "rd": rd, "wr": wr, "ev": ev})
+
+    def ts(o, i, s1, o1, s2=None, o2=None):
+        if o2 is None:
+            op("v", lambda q, a, k: q.tensor_scalar(a[0], a[1], a[2], None, o1), [o, i, s1], {}, [i, s1], [o])
+        else:
+            op("v", lambda q, a, k: q.tensor_scalar(a[0], a[1], a[2], a[3], o1, o2), [o, i, s1, s2], {}, [i, s1, s2], [o])
+
+    def tt(o, x, y, f):
+        op("v", lambda q, a, k: q.tensor_tensor(a[0], a[1], a[2], f), [o, x, y], {}, [x, y], [o])
+
+    def cp(o, i):
+        op("v", lambda q, a, k: q.tensor_copy(a[0], a[1]), [o, i], {}, [i], [o])
+
+    def ms(o, v):
+        op("v", lambda q, a, k: q.memset(a[0], v), [o], {}, [], [o])
+
+    def red(o, i):
+        op("v", lambda q, a, k: q.tensor_reduce(a[0], a[1], AX.X, A.add), [o, i], {}, [i], [o])
+
+    def scan(o, d0, d1, o0, o1):
+        op("v", lambda q, a, k: q.tensor_tensor_scan(a[0], a[1], a[2], 0.0, o0, o1), [o, d0, d1], {}, [d0, d1], [o])
+
+    def cum(o, d):
+        scan(o, d, d, A.add, A.max)
+
+    def act(o, i, f=AF.Identity, **kw):
+        op("s", lambda q, a, k: q.activation(a[0], a[1], f, **k), [o, i], kw, [i, kw.get("bias"), kw.get("scale")], [o])
+
+    def mm(o, l, x, st=True, sp=True):
+        op("t", lambda q, a, k: q.matmul(a[0], a[1], a[2], st, sp), [o, l, x], {}, [l, x], [o])
+
+    def iota(o, pat, base, cm):
+        fl = {"allow_small_or_imprecise_dtypes": True} if SCRATCH[o[1]][2] != I else {}
+        op("g", lambda q, a, k: q.iota(a[0], pat, base, cm, **fl), [o], {}, [], [o])
+    nd = [0]
+
+    def dma(o, i):
+        nd[0] += 1
+        op("y", lambda e, a, k: e.dma_start(a[0], a[1]), [o, i], {}, [i], [o] if is_ref(o) else [], ("dma%d" % (nd[0] - 1), 16, True))
+
+    def tolist(ps, c0, y, src, n, first=True):
+        for a in range(16):
+            mm(r(ps, c0, c0 + n // 16), r(y, 15 - a, 143 - a), r(src, a, n, 16), first and a == 0, a == 15)
+
+    peers = [T.cores[(rank + d) % N] for d in range(1, N)]
+    srcs = [T.cores[(rank - d) % N] for d in range(1, N)]
+    mine = topo.cores_of(core)
+    far = [p for p in peers if p not in mine]
+    far_e = topo.engines(core, far[0])
+    share = len(far_e) // len(far)
+    masks = {p: sum(1 << e for e in far_e[k * share:(k + 1) * share]) for k, p in enumerate(far)}
+    near_n = 0
+    for p in peers:
+        if p in mine:
+            near_e = [e for e in topo.engines(core, p) if e not in far_e]
+            masks[p] = sum(1 << e for e in near_e)
+            near_n = len(near_e)
+    total_e = near_n + share * len(far)
+
+    def exchange(k, src, dst, lsem, lval):
+        def fn(q, a, kw):
+            tr = []
+            for d, p in enumerate(peers):
+                rid, pid = topo.addr(p, core)
+                tr.append(RemoteDMATransfer(dst_ids=[DstId(rid=rid, pnc=pid)], dma_engine_mask=masks[p],
+                                            remote_sem=T.sem[("near%d" if p in mine else "far%d") % k], src=a[0], dst=a[1 + d]))
+            return q.remote_dma_fused(tr, local_sem=T.sem[lsem])
+        op("g", fn, [src] + [dst(d) for d in range(N - 1)], {}, [src], [], (lsem, lval, False))
+        op("y", lambda q, a, kw: None, [], {}, [], [dst(d) for d in range(N - 1) if srcs[d] in mine], ("near%d" % k, near_n, False))
+        op("y", lambda q, a, kw: None, [], {}, [], [dst(d) for d in range(N - 1) if srcs[d] not in mine], ("far%d" % k, share * len(far), False))
+
+    P, AK, G15, K0, K1, K01, K123, K4, K5, K45, G16, RS, RB, RF, HB, TG, THB, P16, JB, MG = range(20)
+    K = lambda k: c("col", k)
+    cls = ((0, 4), (4, 8), (8, 16))
+
+    def clear(k):
+        iota(r("mk", 2048 * k, 2048 * k + 2048), [[0, 2048]], 0, 0)
+        iota(r("sl", 512 * k, 512 * k + 512), [[0, 512]], 0, 0)
+
+    dma(r("plci"), T.plc[:, :])
+    dma(r("w", O, O + GH), T.x[:, 0:GH])
+    dma(r("prm", 0, 2, p=(0, 8)), T.th[:, :])
+    dma(r("prm", 4, 7, p=(0, 8)), T.sd[:, :])
+    dma(r("nbi"), T.nb[:, :])
+    dma(r("w", O + GH, S1), T.x[:, GH:V])
+    iota(r("si", 0, 256), [[1, 256]], 0, 0)
+    iota(c("pint", 0), [[0, 1]], 0, 1)
+    iota(r("xg"), [[16, 8], [0, 16]], 0, 0)
+    iota(r("bag", 4480, PL), [[1, PL - 4480]], 0, 0)
+    exchange(3, r("w", O, O + GH), lambda d: r("w", S1 + d * GH, S1 + (d + 1) * GH), "sent0", total_e)
+    clear(0)
+    ms(r("bag", 0, 3456), 0.0)
+    for k in range(1, 8):
+        act(r("si", 256 * k, 256 * k + 256), r("si", 0, 256), AF.Silu if k == 3 else AF.Identity, bias=256.0 * k) if k != 3 else \
+            act(r("si", 768, 1024), r("si", 512, 768), AF.Silu, bias=256.0)
+    act(r("bag", 3456, 4480), r("si", 0, 1024))
+    cp(r("plcu"), r("plci"))
+    act(r("bag", 0, PL, off=r("plcu")), r("si", O, S1), AF.Silu)
+    act(r("bag", PL, DUMP), r("si", 0, 256))
+    act(r("bag", DUMP, DUMP + 512), r("si", 0, 512))
+    cp(r("plcf"), r("plci"))
+    ts(c("pint", 1), c("pint", 0), 15, A.bitwise_and)
+    cp(K(P), c("pint", 0))
+    ts(r("junk", 0, 112), r("plcf"), float(V), A.is_ge)
+    ts(r("junk", 112, 224), r("plcf"), float(2 * V), A.is_ge)
+    cp(K(AK), c("pint", 1))
+    cp(r("prmf", 0, 2, p=(0, 8)), r("prm", 0, 2, p=(0, 8)))
+    cp(r("prmf", 2, 5, p=(0, 8)), r("prm", 4, 7, p=(0, 8)))
+    red(c("cnt", 0), r("junk", 0, 112))
+    red(c("cnt", 6), r("junk", 112, 224))
+    ts(K(G16), K(P), K(AK), A.subtract)
+    ts(K(G15), K(P), K(AK), A.subtract, 15.0, A.add)
+    ts(K(P16), K(P), 16.0, A.mult)
+    for k, v, f in ((K0, 0, A.is_equal), (K1, 1, A.is_equal), (K01, 1, A.is_le), (RS, 3, A.is_le), (K4, 4, A.is_equal), (K5, 5, A.is_equal)):
+        ts(K(k), K(AK), float(v), f)
+    ts(c("cnt", 4), c("cnt", 0), -1.0, A.mult, 112.0, A.add)
+    ts(c("cnt", 5), c("cnt", 0), c("cnt", 6), A.subtract)
+    ts(r("bdf"), r("xg"), K(G16), A.is_equal)
+    ts(r("e8", p=(0, 8)), r("xg", p=(0, 8)), r("col", P16, P16 + 1, p=(0, 8)), A.is_equal)
+    ts(r("jl"), r("si", 0, 512, 16), K(AK), A.add)
+    mm(r("pC", 0, 3), r("bdf"), r("cnt", 4, 7))
+    mm(r("pC", 4, 9), r("e8", p=(0, 8)), r("prmf", 0, 5, p=(0, 8)))
+    ts(r("ea"), r("si", 0, 16), K(AK), A.is_equal)
+    ts(K(K123), K(RS), K(K0), A.subtract)
+    ts(K(JB), K(K1), -4256.0, A.mult, 4000.0, A.add)
+    for k, (c0, c1) in enumerate(cls):
+        ts(r("u0", c0, c1), r("jl", c0, c1), -16.0 * c0, A.add, 4096.0 / (16 * (c1 - c0)), A.mult)
+        ts(r("djc", c0, c1), r("jl", c0, c1), float(PL - V * k), A.add)
+        ms(c("qc", k), 16.0 * (c1 - c0))
+    cp(r("ns", 0, 3), r("pC", 0, 3))
+    cp(r("par", 0, 5), r("pC", 4, 9))
+
+    def draw_steps(t):
+        def s1():
+            ts(c("sc", 0), c("ns", 0), 13.0, A.mult, 41.0 * t, A.add)
+            tt(r("sc", 4, 7), r("ns", 0, 3), r("qc", 0, 3), A.is_lt)
+
+        def s2():
+            ts(r("bi", 0, 3), r("par", 2, 5), c("sc", 0), A.add)
+            for k, (c0, c1) in enumerate(cls):
+                ts(r("iv", c0, c1), r("djc", c0, c1), c("sc", 4 + k), A.mult)
+
+        def s3():
+            ts(r("bm", 0, 2), r("bi", 0, 2), 63, A.bitwise_and)
+            ts(r("bm", 2, 3), r("bi", 2, 3), 31, A.bitwise_and)
+
+        def s5():
+            for k, (c0, c1) in enumerate(cls):
+                ts(r("pr", c0, c1), r("u0", c0, c1), c("bf", k), A.add, c("ns", k), A.mult)
+
+        def s8():
+            for k, (c0, c1) in enumerate(cls):
+                ts(r("posu", c0, c1), r("pm", c0, c1), float(V * k), A.add)
+        return [s1, s2, s3, lambda: cp(r("bf", 0, 3), r("bm", 0, 3)), s5, lambda: ts(r("ps"), r("pr"), 12, A.arith_shift_right),
+                lambda: tt(r("pm"), r("ps"), r("iv"), A.max), s8]
+
+    def sel(name, k):
+        ts(r(name), r("si", 0, 144), K(G15), A.is_equal, K(k), A.mult)
+
+    def diag(name, v):
+        ts(r(name), r("si", 0, 128), K(P), A.is_equal, v, A.mult)
+
+    def row(name, n, k):
+        ts(r(name), r("si", 0, n), 0.0, A.mult, K(k), A.add)
+    fill = [lambda: sel("y0", K0), lambda: ts(r("jt"), r("si", 0, 256), K(K1), A.mult, K(JB), A.add),
+            lambda: sel("y0b", K0), lambda: sel("y1", K1), lambda: row("mv0", 256, K0), lambda: row("mv1", 256, K1),
+            lambda: diag("i16", 1 / 16), lambda: diag("ineg", -1.0)]
+    for s, f in zip(draw_steps(0), fill):
+        s()
+        f()
+    act(r("ds", 0, CAP), r("jt", 0, CAP))
+    cp(r("nbf", O, S1), r("nbi"))
+    ts(r("nbf", 0, O), r("si", 0, O), -float(O), A.add)
+    ms(r("w", 0, O), 0.0)
+    diag("ibias", -15 / 32)
+    ms(r("ones"), 1.0)
+    ms(r("msg"), 0.0)
+    sel("y01b", K01)
+    ts(r("d18"), r("jl", 0, 8), float(V), A.add)
+    ts(r("d256"), r("jl", 0, 16), 256.0, A.add)
+    ts(K(RB), K(AK), -20480.0, A.mult, 20480.0, A.add)
+    ts(K(RS), K(K123), 10.0, A.mult, K(K0), A.add)
+    ts(K(RF), K(RB), K(K123), A.mult)
+    ts(K(MG), K(K0), -16.0, A.mult, MAGIC, A.add)
+    ts(K(RB), K(K0), 16.0, A.mult, K(RF), A.add)
+    banks = ("pS", "pE", "pF", "pD")
+
+    def consts2(h):
+        for a in range(8 * h, 8 * h + 8):
+            ts(r("selt", 128 * a, 128 * a + 128), r("bdf"), c("ea", a), A.mult)
+
+    def places0():
+        for a in range(16):
+            mm(r(banks[a // 4], 112 * (a % 4), 112 * (a % 4) + 112), r("selt", 128 * a, 128 * a + 128), r("plcf"))
+
+    def consts3():
+        tt(K(K45), K(K4), K(K5), A.add)
+        ts(K(HB), K(RS), float(DUMP), A.mult, K(RB), A.add)
+        ts(K(TG), K(K5), -512.0, A.mult, K(K4), A.add)
+        ts(c("lg", 0), c("par", 0), K(K0), A.mult)
+        diag("ipos", 1.0)
+        diag("ih", 1.0)
+        ts(c("lg", 1), c("par", 1), K(K1), A.mult, c("lg", 0), A.add)
+        for nme, v in (("bd2", 2.0), ("bdm", -1.0), ("bd16", -16.0), ("bdh", 1.0)):
+            ts(r(nme), r("bdf"), v, A.mult)
+        ts(K(THB), c("lg", 1), -1.0, A.mult, 0.5, A.add)
+        sel("y123", K123)
+
+    def consts4():
+        sel("y45", K45)
+        ts(r("xx", 0, 128), r("si", 0, 128), K(P), A.is_le, -1.0, A.mult)
+        diag("e8", 2048.0)
+        tt(r("um"), r("xx", 0, 128), r("bdf"), A.mult)
+        ms(r("rm"), 1.0)
+        row("m4", 512, K4)
+        ts(r("cl"), r("jl"), -1.0, A.mult, 511.0, A.add)
+        for nme, v in (("d1k", 1024), ("d15", 1536), ("d2k", 2048), ("ddmp", DUMP)):
+            ts(r(nme), r("jl"), float(v), A.add)
+        tt(r("ub"), r("um"), r("e8"), A.add)
+        ms(r("rm", 0, 192, 32), 0.0)
+
+    for t in range(RO):
+        final = t == RO - 1
+        mk = lambda a, b, **k: r("mk", 2048 * t + a, 2048 * t + b, **k)
+        w4 = lambda a, b, **k: r("w4", 1536 * t + a, 1536 * t + b, **k)
+        sl = lambda **k: r("sl", 512 * t, 512 * t + 512, **k)
+        tt(r("dr"), r("bag", off=r("posu")), r("jt"), A.min)
+        tolist("pA", 0, "y0", "dr", 256)
+        act(r("drf"), r("bag", off=r("posu")))
+        if t == 0:
+            consts2(0)
+        cp(r("tu", 0, 16), r("pA", 0, 16))
+        cp(r("nbu", 0, 256), r("nbf", off=r("tu", 0, 16)))
+        act(r("oldm"), r("w", 0, S1, off=r("tu", 0, 16)), bias=-192.0)
+        for j0, j1 in MOVES:
+            act(r("gb", 16 * j0, 16 * j1), r("w", O, O + W, off=r("nbu", j0, j1)))
+        ts(r("gu"), r("pA", 0, 16), -float(O), A.add, GH - 1.0, A.min)
+        ts(r("t1", 0, 16), r("pA", 0, 16), float(O + GH), A.is_ge)
+        ts(r("t1", 16, 32), r("pA", 0, 16), float(O), A.is_lt)
+        cp(mk(0, 2048, off=r("tu", 0, 16)), r("mv0"))
+        cum(r("mk2"), mk(O, O + GH))
+        tt(r("t1", 32, 48), r("t1", 0, 16), r("t1", 16, 32), A.add)
+        cp(r("rkd"), r("mk2", off=r("gu")))
+        tolist("pA", 0, "y0b", "rkd", 256)
+        ts(r("n0h"), r("nbf", off=r("tu", 0, 16)), float(O), A.add)
+        tolist("pB", 0, "y0", "n0h", 256)
+        tt(r("t1", 48, 64), r("t1", 32, 48), r("d256"), A.mult)
+        ts(r("t1", 0, 16), r("pA", 0, 16), -1.0, A.add)
+        tt(r("t1", 16, 32), r("t1", 0, 16), r("t1", 48, 64), A.max)
+        cp(r("dru"), r("t1", 16, 32))
+        cp(r("ds", off=r("dru")), r("dr"))
+        cp(r("dsh"), r("ds", 0, CAP))
+
+        def sums(j0, j1):
+            o = r("pM", j0, j1)
+            mm(o, r("ibias"), r("ones", 0, j1 - j0), True, False)
+            mm(o, r("ineg"), r("oldm", j0, j1), False, False)
+            for i in range(16):
+                mm(o, r("i16"), r("gb", 16 * j0 + i, 16 * j1, 16), False, i == 15)
+        sums(*MOVES[0])
+        tolist("pA", 0, "y1", "dsh", CAP)
+        tolist("pA", 8, "y0", "dsh", CAP)
+        cp(r("tu", 16, 32), r("pB", 0, 16))
+        cp(mk(0, 2048, off=r("tu", 16, 32)), r("mv1"))
+        ts(r("ju", 0, 5), r("pA", 0, 5), 256.0, A.add)
+        tt(r("msg", MSG * t + CAP, MSG * t + CAP + 5), r("pA", 8, 13), r("d18", 0, 5), A.min)
+        cp(r("osel"), r("oldm", off=r("ju", 0, 5)))
+        cum(r("mks"), mk(0, 2048))
+        if t == 0:
+            consts2(1)
+        sums(*MOVES[1])
+        sums(*MOVES[2])
+        act(r("rk"), r("mks", off=r("tu")))
+        act(r("n0f"), r("nbf", off=r("tu", 0, 16)), bias=float(O))
+        tolist("pB", 0, "y01b", "rk", 512)
+        if t == 0:
+            places0()
+        ts(r("rr"), r("pM", 0, 256), 188 - 15 / 32, A.max, 196 - 15 / 32, A.min)
+        tt(r("msg", MSG * t, MSG * t + CAP), r("rr", off=r("ju", 0, 5)), r("osel"), A.add)
+        lo = lambda d: 88 * (3 * t + d)
+        exchange(t, r("msg", MSG * t, MSG * t + MSG), lambda d: r("land", lo(d), lo(d) + MSG), "sent", total_e * (t + 1))
+        if not final:
+            clear(t + 1)
+        ts(r("rku"), r("pB", 0, 32), -1.0, A.add)
+        act(sl(off=r("rku", 0, 16)), r("drf"), AF.Silu)
+        act(sl(off=r("rku", 16, 32)), r("n0f"), AF.Silu)
+        tt(r("w", 0, S1, off=r("tu", 0, 16)), r("rr"), r("oldm"), A.add)
+        if final:
+            dma(T.yx[:, :], r("w", O, S1))
+        if t == 0:
+            consts3()
+        else:
+            cp(r("plt", off=r("stu")), r("hf"))
+        cp(r("sl16"), sl())
+        tolist("pA", 0, "y0", "sl16", 512)
+        if t == 0:
+            for a in range(16):
+                act(r("plt", O + a, S1, 16), r(banks[a // 4], 112 * (a % 4), 112 * (a % 4) + 112), AF.Relu, scale=K(RS), bias=K(RB))
+            act(r("plt", 0, O), r("si", 0, O))
+        near_first = sorted(range(N - 1), key=lambda d: srcs[d] not in mine)
+
+        def unpack(d):
+            cp(r("gou", 8 * d, 8 * d + 5), r("land", lo(d) + CAP, lo(d) + CAP + 5))
+            cp(r("w", V + GH * d, V + GH * d + V + CAP, off=r("gou", 8 * d, 8 * d + 5)), r("land", lo(d), lo(d) + CAP))
+        unpack(near_first[0])
+        cp(r("su"), r("pA", 0, 32))
+        cp(r("nbu"), r("nbf", off=r("su")))
+        cp(r("sf"), r("pA", 0, 32))
+        act(r("sv"), r("w", 0, S1, off=r("su")))
+        act(r("pb"), r("plt", 0, S1, off=r("su")))
+        if not final:
+            act(r("ds", 0, CAP), r("jt", 0, CAP))
+        mm(r("pS"), r("ipos"), r("sv"))
+        for d in near_first[1:]:
+            unpack(d)
+        for j0, j1 in CHUNKS[1:]:
+            act(r("gb", 16 * j0, 16 * j1), r("w", O, O + W, off=r("nbu", j0, j1)))
+        j0, j1 = CHUNKS[0]
+        cp(r("gb", 16 * j0, 16 * j1), r("w", O, O + W, off=r("nbu", j0, j1)))
+        ts(r("pb16"), r("pb"), 0.1, A.mult, 2048.0, A.min)
+        tolist("pB", 0, "y123", "pb16", 512)
+        if t == 0:
+            consts4()
+        z = lambda n, k, o=0: r(n, o + 32 * k, o + 32 * k + 32)
+
+        def early1():
+            ts(z("e1", 0), r("pB", 0, 32), float(V), A.is_ge)
+            ts(z("e1", 1), r("pB", 0, 32), float(2 * V), A.is_ge)
+            ts(z("e1", 2), r("sf"), float(O), A.is_lt, 4.0, A.mult)
+            ts(z("nl", 0), r("sf"), float(O), A.is_ge)
+
+        def early2():
+            tt(z("e1", 3), z("e1", 0), z("e1", 1), A.add)
+
+        def early3():
+            tt(z("e1", 4), z("e1", 3), z("e1", 2), A.add)
+            ts(z("e1", 0), z("e1", 3), -float(V), A.mult, -4096.0, A.add)
+
+        def early4():
+            tt(r("pos"), z("e1", 0), r("pB", 0, 32), A.add)
+            for k in range(3):
+                ts(z("oh", k), z("e1", 4), float(k), A.is_equal)
+
+        def early5():
+            for k in range(3):
+                ts(z("rq", k), z("oh", k), 2.0 * k - 11, A.mult, 9.0, A.add)
+                tt(z("qj", k), z("nl", 0), z("oh", k), A.subtract)
+                tt(z("pp", k), z("oh", k), r("pos"), A.mult)
+            cum(r("xx", 0, 96), r("oh"))
+
+        def early6():
+            for k in range(3):
+                ts(z("qj", k), z("qj", k), 2.0 * k - 11, A.mult, 9.0, A.add)
+            ts(r("pp"), r("pp"), 1 / 4096, A.mult, 1.0, A.add)
+            ts(r("nq", 0, 3), r("ns", 0, 3), K(K0), A.mult)
+            ts(r("nq", 8, 11), r("ns", 0, 3), -1024.0, A.add, K(K0), A.mult)
+            cp(c("nq", 4), c("xx", 31))
+            tt(r("nq", 5, 7), r("xx", 63, 96, 32), r("xx", 31, 64, 32), A.subtract)
+
+        def early7():
+            tt(r("nqh", 0, 3), r("nq", 0, 3), r("nq", 4, 7), A.subtract)
+            tt(r("nqh", 4, 7), r("nq", 8, 11), r("xx", 31, 96, 32), A.subtract)
+        early = [early1, early2, early3, early4, early5, early6, early7]
+        for n, (j0, j1) in enumerate(CHUNKS):
+            o = r("pE", j0, j1) if n < len(CHUNKS) - 1 else r("pF", j0, j1)
+            mm(o, r("bd16"), r("sv", j0, j1), True, False)
+            for i in range(16):
+                mm(o, r("bdm"), r("gb", 16 * j0 + i, 16 * j1, 16), False, False)
+            for i in range(16):
+                tt(r("mx", 512 * i + j0, 512 * i + j1), r("gb", 16 * j0 + i, 16 * j1, 16), r("pS", j0, j1), A.max)
+                if i % 4 == 3:
+                    for k in range(i - 3, i + 1):
+                        mm(o, r("bd2"), r("mx", 512 * k + j0, 512 * k + j1), False, k == 15)
+                if early and i % 2 == 1:
+                    early.pop(0)()
+        jl = CHUNKS[-1][0]
+        if t == 0:
+            act(w4(0, 512), r("si", 0, 512), scale=K(K5), bias=K(TG))
+            act(w4(1024, 1536), r("si", 0, 512), AF.Relu, scale=K(RS), bias=K(HB))
+            for k in (1, 2):
+                dma(r("w4", 1536 * k, 1536 * k + 512), w4(0, 512))
+                dma(r("w4", 1536 * k + 1024, 1536 * k + 1536), w4(1024, 1536))
+        act(r("ge", 0, jl), r("pE", 0, jl), AF.Sign, bias=K(THB))
+        act(r("ge", jl, 512), r("pF", jl, 512), AF.Sign, bias=K(THB))
+        tolist("pA", 0, "y01b", "ge", 512)
+        for k in range(3):
+            tt(z("fl", k, 96), r("pA", 0, 32), z("rq", k), A.is_equal)
+        for k in range(3):
+            tt(z("fl", k), r("pA", 0, 32), z("qj", k), A.is_equal)
+        cum(r("s2"), r("fl", 96, 192))
+        scan(r("s1"), r("rm"), r("fl"), A.mult, A.add)
+        Lc, Dn, Nn = (lambda k: c("pC", k)), (lambda k: c("pC", 4 + k)), r("pC", 8, 11)
+        mm(r("pC", 0, 3), r("bdh"), r("nqh", 0, 3), True, False)
+        mm(r("pC", 0, 3), r("bdh"), r("s1", 127, 192, 32), False, True)
+        mm(r("pC", 4, 7), r("bdh"), r("nqh", 4, 7), True, False)
+        mm(r("pC", 4, 7), r("bdh"), r("s2", 31, 96, 32), False, True)
+        mm(Nn, r("bdh"), r("nqh", 0, 3), True, False)
+        mm(Nn, r("bdh"), r("s1", 127, 192, 32), False, False)
+        mm(Nn, r("bdh"), r("s1", 31, 96, 32), False, True)
+        mm(r("pC", 32, 128), r("um"), r("fl", 0, 96), True, False)
+        mm(r("pC", 32, 128), r("bdh"), r("s1", 0, 96), False, True)
+        tt(r("zz"), r("fl", 96, 192), r("pp"), A.max)
+        tt(z("nl", 1), z("fl", 0, 96), z("fl", 1, 96), A.add)
+        tt(z("nl", 2), z("fl", 2, 96), z("nl", 0), A.subtract)
+        for k in range(3):
+            ts(z("ho", k), z("zz", k), 4096.0, A.mult, Lc(k), A.is_lt)
+        for k in range(3):
+            ts(z("xx", k), z("zz", k), 4096.0, A.mult, Dn(k), A.subtract)
+        cum(r("hs"), r("ho"))
+        mm(r("pD", 0, 96), r("ub"), r("ho"), True, False)
+        mm(r("pD", 0, 96), r("bdh"), r("hs"), False, True)
+        mm(c("pD", 100), r("bdh"), c("hs", 95))
+        tt(z("xx", 3), z("xx", 0), z("xx", 1), A.min)
+        tt(z("xx", 4), z("xx", 2), r("d15"), A.min)
+        for k in (1, 2):
+            ts(z("yy", k), r("d1k"), Dn(k), A.add, Lc(k), A.is_ge)
+            ts(z("yy", 2 + k), r("d1k"), Dn(k), A.add, float(V * k), A.add)
+        tt(z("xx", 1), z("xx", 3), z("xx", 4), A.min)
+        ts(z("yy", 0), r("d1k"), Dn(0), A.add)
+        tt(z("o4", 0), z("pD", 0), z("xx", 1), A.max)
+        tt(r("yy", 160, 224), r("yy", 32, 96), r("yy", 96, 160), A.mult)
+        tt(z("o4", 1), z("pD", 1), z("o4", 0), A.max)
+        tt(z("yy", 1), z("yy", 0), z("yy", 5), A.max)
+        tt(z("o4", 2), z("pD", 2), z("o4", 1), A.max)
+        tt(z("yy", 2), z("yy", 1), z("yy", 6), A.max)
+        ts(r("o4u"), z("o4", 2), -1024.0, A.add)
+        act(w4(0, 1536, off=r("o4u")), r("pb"), AF.Silu)
+        cp(r("tpu"), z("yy", 2))
+        for k in range(3):
+            ts(z("vv", k), z("pC", k, 32), Lc(k), A.add, float(V * k), A.add)
+        tt(z("nl", 1), z("nl", 1), z("nl", 2), A.add)
+        cp(r("tb"), r("bag", off=r("tpu")))
+        tt(r("ww"), r("vv"), r("fl", 0, 96), A.mult)
+        ts(z("nl", 2), z("nl", 1), 1.0, A.add)
+        cp(c("lg", 4), c("pD", 100))
+        cp(r("ns", 0, 3), Nn)
+        tt(z("npl", 0), z("ww", 0), z("ww", 1), A.add)
+        tt(z("vv", 0), z("nl", 2), r("ddmp"), A.mult)
+        ts(z("vv", 1), z("nl", 2), 4096.0, A.mult)
+        tt(z("npl", 1), z("ww", 2), z("vv", 0), A.add)
+        tt(z("vv", 2), z("vv", 1), r("sf"), A.add)
+        tt(z("npl", 2), z("npl", 0), z("npl", 1), A.add)
+        tt(z("vv", 1), z("vv", 2), r("d2k"), A.min)
+        tolist("pB", 0, "y0", "tb", 512)
+
+        def rows(a0, a1):
+            for a in range(a0, a1):
+                mm(r("pD", a, 512, 16), r("selt", 128 * a, 128 * a + 128), z("npl", 2))
+            if a1 == 16:
+                act(r("nrec"), r("pD"), AF.Relu, scale=K(RS), bias=K(RF if final else RB))
+        rows(0, 8)
+        if not final:
+            cp(r("jou"), z("npl", 2))
+            act(r("bag", off=r("jou")), sl(), AF.Silu)
+        cp(r("lvu"), z("vv", 1))
+        st = [lambda: None] * 8 if final else draw_steps(t + 1)
+
+        def whole(h):
+            ts(r("plf", O + 896 * h, O + 896 * h + 896), r("plt", O + 896 * h, O + 896 * h + 896), K(MG), A.add, MAGIC, A.subtract)
+        for s in st[:3]:
+            s()
+        if final:
+            whole(0)
+        scan(r("ts4"), r("m4"), w4(0, 512), A.mult, A.add)
+        mm(r("pA", 0, 32), r("ih"), r("cl"), True, False)
+        tolist("pA", 0, "y45", "ts4", 512, first=False)
+        rows(8, 16)
+        for s in st[3:7]:
+            s()
+        if final:
+            whole(1)
+
+        def stayers():
+            ts(z("st", 0), r("pA", 0, 32), c("lg", 4), A.is_ge, 4096.0, A.mult)
+            tt(z("st", 1), z("st", 0), r("pB", 0, 32), A.add)
+            tt(z("st", 2), z("st", 1), r("d2k"), A.min)
+            cp(r("stu"), z("st", 2))
+        if final:
+            cp(r("ixu"), r("pA", 0, 32))
+            ts(r("hf"), w4(1024, 1536, off=r("ixu")), K(MG), A.add, MAGIC, A.subtract)
+            stayers()
+            cp(r("plf", off=r("stu")), r("hf"))
+            cp(r("plf", off=r("lvu")), r("nrec"))
+            op("y", lambda q, a, k: q.dma_start(T.yp[:, :], T.plf[0:128:16, O:S1]), [], {}, [r("plf")], [], ("dma%d" % nd[0], 16, True))
+        else:
+            cp(r("ixu"), r("pA", 0, 32))
+            ts(r("hg"), w4(1024, 1536, off=r("ixu")), 0.1, A.mult, 2048.0, A.min)
+            tolist("pC", 0, "y123", "hg", 512)
+            act(r("plt", off=r("lvu")), r("nrec"), AF.Silu)
+            act(r("hf"), w4(1024, 1536, off=r("ixu")))
+            st[7]()
+            stayers()
+            cp(r("hou"), r("pC", 0, 32))
+            cp(r("bag", off=r("hou")), r("tb"))
+    emit(g, T, ops)

@@ -5,13 +5,18 @@ V, GH, CAP, RO, N = 1792, 512, 80, 3, 4
 W = V + (N - 1) * GH
 O = 256
 S1 = O + V
-PL = 3 * V
-DUMP = PL + 256
-MSG = 86
+B0 = 512
+PL = B0 + 3 * V
+MSG = 96
 MAGIC = 12582912.0
+SC = 16.0
 F, B, H, I, U = "float32", "bfloat16", "float16", "int32", "uint16"
-MOVES = ((0, 128), (128, 192), (192, 256))
-CHUNKS = ((0, 64), (64, 192), (192, 320), (320, 448), (448, 512))
+MOVES = (((0, 96, "s"), (192, 256, "s"), (96, 192, "v")), ((0, 80, "s"), (120, 192, "s"), (192, 256, "s"), (80, 104, 0), (104, 120, 1)))
+SORT = ((1, 1, 1, 1, 1, 1), (1, 1, 1, 1, 1, 1))
+RANK = "s"
+SUMS = (((0, 96), (96, 192), (192, 256)), ((0, 120), (120, 192), (192, 256)))
+CHUNKS = ((0, 96, "v"), (96, 224, "s"), (224, 352, "s"), (352, 448, "s"), (448, 512, "s"))
+FILL = (3328, 4608)
 
 
 def _sb(c, d):
@@ -19,35 +24,39 @@ def _sb(c, d):
 
 
 BUF = {
-    "w": _sb(4688, B), "nbi": _sb(V, I), "nbf": _sb(2048, F), "bag": _sb(6144, F), "plt": _sb(2560, F), "plf": _sb(2560, F), "si": _sb(2048, F),
-    "mk": _sb(3 * 2048, B), "mks": _sb(2048, B), "mk2": _sb(512, B), "w4": _sb(3 * 1536, F), "sl": _sb(3 * 512, F), "sl16": _sb(512, H),
-    "gb": _sb(8192, B), "mx": _sb(8192, B), "selt": _sb(2048, F), "xg": _sb(128, F),
+    "w": _sb(4688, B), "nbi": _sb(2048, I), "bag": _sb(6144, F), "plt": _sb(2560, F), "plf": _sb(2560, F), "si": _sb(2048, F),
+    "mk": _sb(3 * 2560, B), "mks": _sb(2560, B), "mk2": _sb(2048, B), "w4": _sb(1536, F), "sl": _sb(3 * 768, F), "sl16": _sb(512, H),
+    "slb": _sb(512, F), "dj": _sb(256, H), "yrk": _sb(144, B), "mh0": _sb(128, F), "mh1": _sb(128, F), "mh": _sb(128, H), "i0": _sb(128, H),
+    "rm7": _sb(224, F), "pn": _sb(96, F), "zn": _sb(96, F), "xh": _sb(96, H), "d1h": _sb(32, H), "o7": _sb(224, F),
+    "gb": _sb(8192, B), "gm": _sb(4096, B), "mx": _sb(8192, B), "selt": _sb(2048, F), "xg": _sb(128, F),
     "plci": _sb(112, I), "plcf": _sb(112, F), "plcu": _sb(112, U), "junk": _sb(224, F),
-    "prm": _sb(16, I), "prmf": _sb(8, F), "par": _sb(8, F), "col": _sb(24, F), "pint": _sb(8, I), "ea": _sb(16, F),
+    "prm": _sb(16, I), "prmf": _sb(8, F), "par": _sb(8, F), "col": _sb(64, F), "pint": _sb(8, I),
     "y0": _sb(144, H), "y1": _sb(144, H), "y123": _sb(144, H), "y45": _sb(144, H), "y01b": _sb(144, B), "y0b": _sb(144, B),
-    "bdf": _sb(128, F), "bdh": _sb(128, H), "bd2": _sb(128, B), "bdm": _sb(128, B), "bd16": _sb(128, B),
+    "ycl": _sb(144, H), "ypos": _sb(144, H),
+    "bdf": _sb(128, F), "bdh": _sb(128, H), "bdn": _sb(128, H), "bd2": _sb(128, B), "bdm": _sb(128, B), "bd16": _sb(128, B),
     "i16": _sb(128, B), "ineg": _sb(128, B), "ipos": _sb(128, B), "ibias": _sb(128, B), "ih": _sb(128, H), "um": _sb(128, H), "ub": _sb(128, H),
-    "e8": _sb(128, F), "ones": _sb(128, B), "m4": _sb(512, B), "jt": _sb(256, F), "mv0": _sb(256, B), "mv1": _sb(256, B), "rm": _sb(192, H),
+    "e8": _sb(128, F), "d48": _sb(128, F), "tri": _sb(128, F), "ones": _sb(256, B), "m4": _sb(512, B), "jt": _sb(256, F), "mv0": _sb(256, B), "mv1": _sb(256, B),
+    "rm": _sb(192, H), "neg": _sb(96, H),
     "jl": _sb(32, F), "cl": _sb(32, H), "u0": _sb(16, F), "djc": _sb(16, F), "d2k": _sb(32, F), "d15": _sb(32, F), "d1k": _sb(32, F),
-    "d18": _sb(8, F), "d256": _sb(16, F), "ddmp": _sb(32, F), "qc": _sb(4, F),
+    "mo": _sb(8, H), "d257": _sb(16, F), "oc": _sb(4, F), "d81": _sb(128, F), "us": _sb(128, H), "uj": _sb(128, H), "ujn": _sb(128, H),
     "ns": _sb(4, F), "cnt": _sb(8, F), "sc": _sb(16, F), "bi": _sb(4, I), "bm": _sb(4, I), "bf": _sb(4, F), "iv": _sb(16, I),
     "pr": _sb(16, I), "ps": _sb(16, I), "pm": _sb(16, F), "posu": _sb(16, U),
-    "dr": _sb(256, H), "drf": _sb(256, F), "n0h": _sb(256, H), "n0f": _sb(256, F), "tu": _sb(32, U), "gu": _sb(16, U), "nbu": _sb(512, U),
-    "t1": _sb(64, F), "oldm": _sb(256, B), "rr": _sb(256, B), "rkd": _sb(256, B), "rk": _sb(512, B), "dru": _sb(16, U), "rku": _sb(32, U),
-    "ds": _sb(512, F), "dsh": _sb(80, H), "ju": _sb(6, U), "osel": _sb(80, B), "msg": _sb(3 * MSG + 6, H), "land": _sb(9 * 88, H), "gou": _sb(24, U),
+    "dr": _sb(512, H), "rec": _sb(512, F), "tu": _sb(32, U), "nbm": _sb(256, U), "nbu": _sb(512, U),
+    "t1": _sb(16, F), "oldm": _sb(256, B), "rr": _sb(256, B), "rkd": _sb(256, B), "rk": _sb(512, B), "dru": _sb(16, U), "rku": _sb(32, U),
+    "ds": _sb(512, F), "dsh": _sb(80, H), "ju": _sb(6, U), "nbc": _sb(CAP, U), "osel": _sb(80, B), "msg": _sb(3 * MSG, H), "land": _sb(9 * 88, H), "gou": _sb(24, U),
     "su": _sb(32, U), "sf": _sb(32, F), "sv": _sb(512, B), "pb": _sb(512, F), "pb16": _sb(512, H), "ge": _sb(512, B),
-    "e1": _sb(160, F), "oh": _sb(96, F), "qj": _sb(96, F), "rq": _sb(96, F), "pp": _sb(96, F), "pos": _sb(32, F), "nq": _sb(12, F), "nqh": _sb(8, H),
-    "fl": _sb(192, H), "s1": _sb(192, H), "s2": _sb(96, H), "zz": _sb(96, F), "ho": _sb(96, H), "hs": _sb(96, H), "xx": _sb(160, F),
-    "o4": _sb(96, F), "o4u": _sb(32, U), "vv": _sb(96, F), "ww": _sb(96, F), "nl": _sb(96, F), "npl": _sb(96, F), "jou": _sb(32, U), "lvu": _sb(32, U),
-    "yy": _sb(224, F), "tpu": _sb(32, U), "tb": _sb(512, H), "ts4": _sb(512, H), "ixu": _sb(32, U), "hg": _sb(512, H), "hf": _sb(512, F),
+    "ne": _sb(96, H), "rq": _sb(96, F), "pp": _sb(96, F), "v18": _sb(32, H), "sa": _sb(96, F), "sb": _sb(96, F), "nq": _sb(8, F), "nqh": _sb(8, H),
+    "fl": _sb(192, H), "jn": _sb(96, H), "s1": _sb(192, H), "s2": _sb(96, H), "zz": _sb(96, F), "ho": _sb(96, H), "hs": _sb(96, H), "xx": _sb(192, F),
+    "o4": _sb(96, F), "o4u": _sb(32, U), "vv": _sb(96, F), "ww": _sb(96, F), "npl": _sb(96, F), "lv": _sb(96, F), "jou": _sb(32, U), "lvu": _sb(32, U),
+    "yy": _sb(288, F), "tpu": _sb(32, U), "tb": _sb(512, H), "ts4": _sb(512, H), "ixu": _sb(32, U), "hg": _sb(512, H), "hf": _sb(512, F),
     "hou": _sb(32, U), "nrec": _sb(512, F), "st": _sb(96, F), "stu": _sb(32, U), "lg": _sb(16, F),
-    "pS": ("psum", [128, 512], F), "pE": ("psum", [128, 512], F), "pF": ("psum", [128, 512], F), "pM": ("psum", [128, 512], F),
+    "pS": ("psum", [128, 512], F), "pE": ("psum", [128, 512], F), "pF": ("psum", [128, 512], F), "pG": ("psum", [128, 512], F),
     "pA": ("psum", [128, 512], F), "pB": ("psum", [128, 512], F), "pC": ("psum", [128, 512], F), "pD": ("psum", [128, 512], F),
 }
 SCRATCH = {}
 PLACE = {}
 for _n, (_w, _s, _d) in BUF.items():
-    if _w == "sbuf" and _s[1] <= 256:
+    if _w == "sbuf" and _s[1] <= 288:
         _at = SCRATCH.get("tiles_" + _d, (0, [0, 0]))[1][1]
         PLACE[_n] = ("tiles_" + _d, _at)
         SCRATCH["tiles_" + _d] = _sb(_at + (_s[1] + 15) // 16 * 16, _d)
@@ -73,15 +82,11 @@ def is_ref(a):
     return isinstance(a, tuple) and len(a) == 7 and a[0] == "ref"
 
 
-def emit(g, T, ops):
-    def ap(a):
-        if not is_ref(a):
-            return a
-        _, name, c0, c1, step, p, off = a
-        t = T[name]
-        x = t[p[0]:p[1], c0:c1] if step == 1 else t[p[0]:p[1], c0:c1:step]
-        return x.indirect(ap(off)) if off is not None else x
+def width(a):
+    return 16 * width(a[6]) if a[6] is not None else (a[3] - a[2] + a[4] - 1) // a[4]
 
+
+def depend(ops, banks):
     def meet(a, b):
         return SCRATCH[a[1]][0] == "psum" or (a[2] < b[3] and b[2] < a[3] and not (a[4] == b[4] > 1 and (a[2] - b[2]) % a[4]))
     acc = {}
@@ -93,7 +98,7 @@ def emit(g, T, ops):
             psum = SCRATCH[a[1]][0] == "psum"
             for j, b, bw in acc.get(a[1], []):
                 e = ops[j]["q"]
-                if not meet(a, b) or (e == "t" and o["q"] == "t"):
+                if not meet(a, b) or (e == "t" and o["q"] == "t" and not banks):
                     continue
                 if wr or bw or (psum and e != o["q"]):
                     d.add(j)
@@ -103,7 +108,121 @@ def emit(g, T, ops):
                 l[:] = [x for x in l if x[0] == k or not (a[2] <= x[1][2] and x[1][3] <= a[3])]
             l.append((k, a, wr))
         deps.append(d)
-    known = {q: {} for q in "vstgy"}
+    return deps
+
+
+CY, WAKE, GATHER, SCATTER, SEND = 0.83, 200.0, 1.5, 2.5, 2000.0
+
+
+PASSES = 2
+
+
+def cost(q, kind, args, rd, wr):
+    two = lambda a: SCRATCH[a[1]][2] in (B, H, U)
+    if kind == "send":
+        x = SEND if width(rd[0]) == GH else 0.0
+        return 900.0 + x, SEND + x + 640 + 4.3 * width(rd[0])
+    if kind == "land":
+        return 0.0, 0.0
+    if kind == "dma":
+        a = (wr + rd)[0]
+        x = width(a) * (2 if two(a) else 4) * 0.45 * (a[5][1] - a[5][0]) / 128
+        return 50 + x, 2000 + x
+    n = width(args[1] if kind == "red" else wr[0])
+    if q == "t":
+        x = max(64, n) * 0.42 * (1 if two(args[2]) else 4)
+    elif q == "g":
+        x = 150 + 2 * CY * n
+    elif wr[0][6] is not None:
+        x = 60 + (SCATTER + {"tt": 2, "ts": 1}.get(kind, 0)) * CY * n
+    elif any(a[6] is not None for a in rd):
+        x = 60 + (GATHER + {"tt": 2, "ts": 1}.get(kind, 0)) * CY * n
+    elif q == "s":
+        x = 65 + CY * n + (1300 if kind == "table" else 0)
+    elif kind == "tt":
+        x = CY * max(64, n * (2 if all(SCRATCH[a[1]][0] == "sbuf" for a in args[1:3]) else 1))
+    else:
+        x = CY * max(64, n * (0.5 if kind != "red" and all(two(a) for a in rd + wr if width(a) == n) else 1))
+    return x, x
+
+
+def schedule(ops):
+    deps = depend(ops, True)
+    last = {}
+    for k, o in enumerate(ops):
+        if o["kind"] in ("send", "land", "post") and "send" in last:
+            deps[k].add(last["send"])
+        if o["kind"] == "dma" and "dma" in last:
+            deps[k].add(last["dma"])
+        last[o["kind"]] = k
+
+    def lat(j, k):
+        if ops[j]["kind"] == ops[k]["kind"] == "dma" or ops[k]["kind"] == "post" and ops[j]["kind"] == "send":
+            return ops[j]["cost"][0] - ops[j]["cost"][1]
+        return 0.0 if ops[j]["q"] == ops[k]["q"] == "t" else WAKE
+    n = len(ops)
+    succ = [[] for _ in ops]
+    for k in range(n):
+        for j in deps[k]:
+            succ[j].append(k)
+
+    def place(order, before, back):
+        busy = {q: ([], []) for q in "vstgye"}
+        start = [0.0] * n
+        end = [0.0] * n
+        for k in order:
+            hold, total = ops[k]["cost"]
+            pre = total - hold if back else 0.0
+            t = max([end[j] + lat(j, k) for j in before[k]] + [0.0]) + pre
+            a, b = busy[ops[k]["q"]]
+            lo, hi = 0, len(b)
+            while lo < hi:
+                if b[(lo + hi) // 2] <= t:
+                    lo = (lo + hi) // 2 + 1
+                else:
+                    hi = (lo + hi) // 2
+            while lo < len(a) and t + hold > a[lo]:
+                t = max(t, b[lo])
+                lo += 1
+            a.insert(lo, t)
+            b.insert(lo, t + hold)
+            start[k], end[k] = t - pre, t - pre + total
+        return start, end
+    order = []
+    seen = [False] * n
+
+    def visit(k):
+        if not seen[k]:
+            seen[k] = True
+            for j in sorted(deps[k]):
+                visit(j)
+            order.append(k)
+    for late in (False, True):
+        for k in range(n):
+            if late or not ops[k]["lazy"]:
+                visit(k)
+    best = None
+    for _ in range(PASSES):
+        start, end = place(order, deps, False)
+        if best is None or max(end) < best[0]:
+            best = (max(end), start)
+        rank = place(sorted(range(n), key=lambda k: (-end[k], -k)), succ, True)[1]
+        order = sorted(range(n), key=lambda k: (-rank[k], k))
+    return sorted(range(n), key=lambda k: (best[1][k], k))
+
+
+ORDERS = {}
+
+
+def emit(g, T, ops, deps):
+    def ap(a):
+        if not is_ref(a):
+            return a
+        _, name, c0, c1, step, p, off = a
+        t = T[name]
+        x = t[p[0]:p[1], c0:c1] if step == 1 else t[p[0]:p[1], c0:c1:step]
+        return x.indirect(ap(off)) if off is not None else x
+    known = {q: {} for q in "vstgye"}
     after = [None] * len(ops)
     waits = []
     for k, o in enumerate(ops):
@@ -121,7 +240,7 @@ def emit(g, T, ops):
         after[k] = dict(kn)
         after[k][o["ev"] or o["q"]] = k
     marked = set(j for w in waits for j in w)
-    Q = {"v": g.vector, "s": g.scalar, "t": g.tensor, "g": g, "y": g.sync}
+    Q = {"v": g.vector, "s": g.scalar, "t": g.tensor, "g": g, "y": g.sync, "e": None}
     count = {q: 0 for q in "vstg"}
     val = {}
     top = {}
@@ -149,20 +268,22 @@ def rank_program(g, core, T, topo):
     if rank is None:
         return
     ops = []
+    lazy = [False]
 
-    def op(q, fn, args, kw, rd, wr, ev=None):
+    def op(q, fn, args, kw, rd, wr, ev=None, kind=None):
         rd = [a for a in rd if is_ref(a)]
+        x = cost(q, kind, args, rd, wr)
         rd += [a[6] for a in rd + wr if a[6] is not None]
-        ops.append({"q": q, "fn": fn, "args": args, "kw": kw, "rd": rd, "wr": wr, "ev": ev})
+        ops.append({"q": q, "fn": fn, "args": args, "kw": kw, "rd": rd, "wr": wr, "ev": ev, "kind": kind, "cost": x, "lazy": lazy[0]})
 
     def ts(o, i, s1, o1, s2=None, o2=None):
         if o2 is None:
-            op("v", lambda q, a, k: q.tensor_scalar(a[0], a[1], a[2], None, o1), [o, i, s1], {}, [i, s1], [o])
+            op("v", lambda q, a, k: q.tensor_scalar(a[0], a[1], a[2], None, o1), [o, i, s1], {}, [i, s1], [o], kind="ts")
         else:
-            op("v", lambda q, a, k: q.tensor_scalar(a[0], a[1], a[2], a[3], o1, o2), [o, i, s1, s2], {}, [i, s1, s2], [o])
+            op("v", lambda q, a, k: q.tensor_scalar(a[0], a[1], a[2], a[3], o1, o2), [o, i, s1, s2], {}, [i, s1, s2], [o], kind="ts")
 
     def tt(o, x, y, f):
-        op("v", lambda q, a, k: q.tensor_tensor(a[0], a[1], a[2], f), [o, x, y], {}, [x, y], [o])
+        op("v", lambda q, a, k: q.tensor_tensor(a[0], a[1], a[2], f), [o, x, y], {}, [x, y], [o], kind="tt")
 
     def cp(o, i):
         op("v", lambda q, a, k: q.tensor_copy(a[0], a[1]), [o, i], {}, [i], [o])
@@ -171,7 +292,7 @@ def rank_program(g, core, T, topo):
         op("v", lambda q, a, k: q.memset(a[0], v), [o], {}, [], [o])
 
     def red(o, i):
-        op("v", lambda q, a, k: q.tensor_reduce(a[0], a[1], AX.X, A.add), [o, i], {}, [i], [o])
+        op("v", lambda q, a, k: q.tensor_reduce(a[0], a[1], AX.X, A.add), [o, i], {}, [i], [o], kind="red")
 
     def scan(o, d0, d1, o0, o1):
         op("v", lambda q, a, k: q.tensor_tensor_scan(a[0], a[1], a[2], 0.0, o0, o1), [o, d0, d1], {}, [d0, d1], [o])
@@ -180,23 +301,27 @@ def rank_program(g, core, T, topo):
         scan(o, d, d, A.add, A.max)
 
     def act(o, i, f=AF.Identity, **kw):
-        op("s", lambda q, a, k: q.activation(a[0], a[1], f, **k), [o, i], kw, [i, kw.get("bias"), kw.get("scale")], [o])
+        op("s", lambda q, a, k: q.activation(a[0], a[1], f, **k), [o, i], kw, [i, kw.get("bias"), kw.get("scale")], [o],
+           kind="table" if f == AF.Silu and o[6] is None else None)
+
+    def take(e, o, i):
+        (cp if e == "v" else act)(o, i)
 
     def mm(o, l, x, st=True, sp=True):
         op("t", lambda q, a, k: q.matmul(a[0], a[1], a[2], st, sp), [o, l, x], {}, [l, x], [o])
 
-    def iota(o, pat, base, cm):
+    def iota(o, pat, base, cm, kind=None):
         fl = {"allow_small_or_imprecise_dtypes": True} if SCRATCH[o[1]][2] != I else {}
-        op("g", lambda q, a, k: q.iota(a[0], pat, base, cm, **fl), [o], {}, [], [o])
+        op("g", lambda q, a, k: q.iota(a[0], pat, base, cm, **fl), [o], {}, [], [o], kind=kind)
     nd = [0]
 
     def dma(o, i):
         nd[0] += 1
-        op("y", lambda e, a, k: e.dma_start(a[0], a[1]), [o, i], {}, [i], [o] if is_ref(o) else [], ("dma%d" % (nd[0] - 1), 16, True))
+        op("y", lambda e, a, k: e.dma_start(a[0], a[1]), [o, i], {}, [i], [o] if is_ref(o) else [], ("dma%d" % (nd[0] - 1), 16, True), "dma")
 
-    def tolist(ps, c0, y, src, n, first=True):
+    def tolist(ps, c0, y, src, n, first=True, at=0):
         for a in range(16):
-            mm(r(ps, c0, c0 + n // 16), r(y, 15 - a, 143 - a), r(src, a, n, 16), first and a == 0, a == 15)
+            mm(r(ps, c0, c0 + n // 16), r(y, 15 - a, 143 - a), r(src, at + a, at + n, 16), first and a == 0, a == 15)
 
     peers = [T.cores[(rank + d) % N] for d in range(1, N)]
     srcs = [T.cores[(rank - d) % N] for d in range(1, N)]
@@ -213,47 +338,60 @@ def rank_program(g, core, T, topo):
             near_n = len(near_e)
     total_e = near_n + share * len(far)
 
+    def slot(to, d):
+        away = [e for e in range(N - 1) if T.cores[(to - e - 1) % N] not in topo.cores_of(T.cores[to % N])]
+        return away.index(d) if d in away else len(away)
+
     def exchange(k, src, dst, lsem, lval):
+        out = [src(slot(rank + d + 1, d)) for d in range(N - 1)]
+
         def fn(q, a, kw):
             tr = []
             for d, p in enumerate(peers):
                 rid, pid = topo.addr(p, core)
                 tr.append(RemoteDMATransfer(dst_ids=[DstId(rid=rid, pnc=pid)], dma_engine_mask=masks[p],
-                                            remote_sem=T.sem[("near%d" if p in mine else "far%d") % k], src=a[0], dst=a[1 + d]))
+                                            remote_sem=T.sem[("near%d" if p in mine else "far%d") % k], src=a[d], dst=a[N - 1 + d]))
             return q.remote_dma_fused(tr, local_sem=T.sem[lsem])
-        op("g", fn, [src] + [dst(d) for d in range(N - 1)], {}, [src], [], (lsem, lval, False))
-        op("y", lambda q, a, kw: None, [], {}, [], [dst(d) for d in range(N - 1) if srcs[d] in mine], ("near%d" % k, near_n, False))
-        op("y", lambda q, a, kw: None, [], {}, [], [dst(d) for d in range(N - 1) if srcs[d] not in mine], ("far%d" % k, share * len(far), False))
+        op("g", fn, out + [dst(d, slot(rank + d + 1, d)) for d in range(N - 1)], {}, out, [], (lsem, lval, False), "send")
+        here = [dst(d, slot(rank, d)) for d in range(N - 1)]
+        op("e", lambda q, a, kw: None, [], {}, [], [here[d] for d in range(N - 1) if srcs[d] in mine], ("near%d" % k, near_n, False), "land")
+        op("e", lambda q, a, kw: None, [], {}, [], [here[d] for d in range(N - 1) if srcs[d] not in mine], ("far%d" % k, share * len(far), False), "land")
 
-    P, AK, G15, K0, K1, K01, K123, K4, K5, K45, G16, RS, RB, RF, HB, TG, THB, P16, JB, MG = range(20)
+    (P, AK, G15, G16, P16, K0, K1, K01, K02, K12, K4, K5, K45, K6, G7, K78, RS, RB, R0, RF, MN, US, WC, WP, TG, THB, JB, MG,
+     CL, QM, QQ, QR, Q13, BS, BD, X0, X1, X2, X3, X4, X5, X6, X7, X8, X9, K3, K123,
+     K2, K9, G9, WR, WH, MX, X10, X11, X12, X13, X14, X15) = range(59)
     K = lambda k: c("col", k)
-    cls = ((0, 4), (4, 8), (8, 16))
 
-    def clear(k):
-        iota(r("mk", 2048 * k, 2048 * k + 2048), [[0, 2048]], 0, 0)
-        iota(r("sl", 512 * k, 512 * k + 512), [[0, 512]], 0, 0)
-
-    dma(r("plci"), T.plc[:, :])
     dma(r("w", O, O + GH), T.x[:, 0:GH])
+    dma(r("plci"), T.plc[:, :])
     dma(r("prm", 0, 2, p=(0, 8)), T.th[:, :])
     dma(r("prm", 4, 7, p=(0, 8)), T.sd[:, :])
-    dma(r("nbi"), T.nb[:, :])
+    dma(r("nbi", O, S1), T.nb[:, :])
     dma(r("w", O + GH, S1), T.x[:, GH:V])
     iota(r("si", 0, 256), [[1, 256]], 0, 0)
     iota(c("pint", 0), [[0, 1]], 0, 1)
     iota(r("xg"), [[16, 8], [0, 16]], 0, 0)
-    iota(r("bag", 4480, PL), [[1, PL - 4480]], 0, 0)
-    exchange(3, r("w", O, O + GH), lambda d: r("w", S1 + d * GH, S1 + (d + 1) * GH), "sent0", total_e)
-    clear(0)
-    ms(r("bag", 0, 3456), 0.0)
-    for k in range(1, 8):
-        act(r("si", 256 * k, 256 * k + 256), r("si", 0, 256), AF.Silu if k == 3 else AF.Identity, bias=256.0 * k) if k != 3 else \
-            act(r("si", 768, 1024), r("si", 512, 768), AF.Silu, bias=256.0)
-    act(r("bag", 3456, 4480), r("si", 0, 1024))
+    exchange(3, lambda s: r("w", O, O + GH), lambda d, s: r("w", S1 + d * GH, S1 + (d + 1) * GH), "sent0", total_e)
+    ms(r("sl", 0, 512), 0.0)
+    act(r("si", V, 2048), r("si", 0, 256), AF.Silu, bias=float(V))
+    ts(r("si", 256, 512), r("si", 0, 256), 256.0, A.add)
+    ts(r("si", 512, 1024), r("si", 0, 512), 512.0, A.add)
+    ts(r("si", 1024, V), r("si", 0, V - 1024), 1024.0, A.add)
+    ms(c("bag", B0 + 2 * V - 1), 0.0)
+    lazy[0] = True
+    ms(r("mk", 0, 2048), 0.0)
+    ts(r("nbi", 0, O), r("si", 0, O), 2.0, A.mult, float(V), A.add)
+    lazy[0] = False
+
+    def selectors(b):
+        o = r("selt", 512 * b, 512 * b + 512)
+        op("g", lambda q, a, k: q.affine_select(a[0], a[1], [[-1, 4], [-16, 8], [0, 16]], A.not_equal, 1.0, -4 * b, 1),
+           [o, r("sl", 0, 512)], {}, [r("sl", 0, 512)], [o], kind="post")
+    for b in range(4):
+        selectors(b)
     cp(r("plcu"), r("plci"))
-    act(r("bag", 0, PL, off=r("plcu")), r("si", O, S1), AF.Silu)
-    act(r("bag", PL, DUMP), r("si", 0, 256))
-    act(r("bag", DUMP, DUMP + 512), r("si", 0, 512))
+    act(r("bag", B0, PL, off=r("plcu")), r("si", O, S1), AF.Silu)
+    act(r("bag", PL, PL + 256), r("si", 0, 256))
     cp(r("plcf"), r("plci"))
     ts(c("pint", 1), c("pint", 0), 15, A.bitwise_and)
     cp(K(P), c("pint", 0))
@@ -267,7 +405,8 @@ def rank_program(g, core, T, topo):
     ts(K(G16), K(P), K(AK), A.subtract)
     ts(K(G15), K(P), K(AK), A.subtract, 15.0, A.add)
     ts(K(P16), K(P), 16.0, A.mult)
-    for k, v, f in ((K0, 0, A.is_equal), (K1, 1, A.is_equal), (K01, 1, A.is_le), (RS, 3, A.is_le), (K4, 4, A.is_equal), (K5, 5, A.is_equal)):
+    for k, v, f in ((K0, 0, A.is_equal), (K1, 1, A.is_equal), (K01, 1, A.is_le), (K02, 2, A.is_le), (K3, 3, A.is_equal), (K4, 4, A.is_equal), (K5, 5, A.is_equal),
+                    (K6, 6, A.is_equal), (G7, 7, A.is_ge)):
         ts(K(k), K(AK), float(v), f)
     ts(c("cnt", 4), c("cnt", 0), -1.0, A.mult, 112.0, A.add)
     ts(c("cnt", 5), c("cnt", 0), c("cnt", 6), A.subtract)
@@ -276,39 +415,41 @@ def rank_program(g, core, T, topo):
     ts(r("jl"), r("si", 0, 512, 16), K(AK), A.add)
     mm(r("pC", 0, 3), r("bdf"), r("cnt", 4, 7))
     mm(r("pC", 4, 9), r("e8", p=(0, 8)), r("prmf", 0, 5, p=(0, 8)))
-    ts(r("ea"), r("si", 0, 16), K(AK), A.is_equal)
-    ts(K(K123), K(RS), K(K0), A.subtract)
-    ts(K(JB), K(K1), -4256.0, A.mult, 4000.0, A.add)
-    for k, (c0, c1) in enumerate(cls):
-        ts(r("u0", c0, c1), r("jl", c0, c1), -16.0 * c0, A.add, 4096.0 / (16 * (c1 - c0)), A.mult)
-        ts(r("djc", c0, c1), r("jl", c0, c1), float(PL - V * k), A.add)
-        ms(c("qc", k), 16.0 * (c1 - c0))
-    cp(r("ns", 0, 3), r("pC", 0, 3))
+    ts(K(K12), K(K02), K(K0), A.subtract)
+    ts(K(X9), K(K1), -256.0, A.mult)
+    ts(K(JB), K(K0), 4000.0, A.mult, K(X9), A.add)
+    ts(c("oc", 0), K(AK), 3.0, A.is_le)
+    ts(c("oc", 2), K(AK), 8.0, A.is_ge)
+    ts(K(X6), c("oc", 0), c("oc", 2), A.add)
+    ts(c("oc", 1), K(X6), -1.0, A.mult, 1.0, A.add)
+    ts(K(CL), c("oc", 2), 2.0, A.mult, c("oc", 1), A.add)
+    ts(K(QM), c("oc", 2), 1.0, A.add)
+    ts(K(QQ), K(QM), 64.0, A.mult)
+    ts(K(QR), c("oc", 2), -0.5, A.mult, 1.0, A.add)
+    ts(K(Q13), K(QM), 13.0, A.mult)
+    ts(K(BS), K(CL), float(V), A.mult, float(B0), A.add)
+    ts(K(BD), K(CL), 64.0 - V, A.mult, 3.0 * V, A.add)
+    ts(K(X7), K(CL), -4.0, A.mult, K(AK), A.add)
+    ts(K(X8), K(X7), 16.0, A.mult)
+    ts(r("u0"), r("si", 0, 16), K(X8), A.add, 64.0, A.mult)
     cp(r("par", 0, 5), r("pC", 4, 9))
+    tt(r("sc", 4, 7), r("par", 2, 5), r("oc", 0, 3), A.mult)
+    red(c("sc", 8), r("sc", 4, 7))
+    for t in range(RO):
+        ts(c("sc", 9 + t), c("sc", 8), 41.0 * t, A.add, K(QM), A.mult)
 
-    def draw_steps(t):
-        def s1():
-            ts(c("sc", 0), c("ns", 0), 13.0, A.mult, 41.0 * t, A.add)
-            tt(r("sc", 4, 7), r("ns", 0, 3), r("qc", 0, 3), A.is_lt)
-
-        def s2():
-            ts(r("bi", 0, 3), r("par", 2, 5), c("sc", 0), A.add)
-            for k, (c0, c1) in enumerate(cls):
-                ts(r("iv", c0, c1), r("djc", c0, c1), c("sc", 4 + k), A.mult)
-
-        def s3():
-            ts(r("bm", 0, 2), r("bi", 0, 2), 63, A.bitwise_and)
-            ts(r("bm", 2, 3), r("bi", 2, 3), 31, A.bitwise_and)
-
-        def s5():
-            for k, (c0, c1) in enumerate(cls):
-                ts(r("pr", c0, c1), r("u0", c0, c1), c("bf", k), A.add, c("ns", k), A.mult)
-
-        def s8():
-            for k, (c0, c1) in enumerate(cls):
-                ts(r("posu", c0, c1), r("pm", c0, c1), float(V * k), A.add)
-        return [s1, s2, s3, lambda: cp(r("bf", 0, 3), r("bm", 0, 3)), s5, lambda: ts(r("ps"), r("pr"), 12, A.arith_shift_right),
-                lambda: tt(r("pm"), r("ps"), r("iv"), A.max), s8]
+    def draw(t, sizes):
+        ts(c("bi", 0), sizes[:2] + (sizes[2], sizes[2] + 1) + sizes[4:], K(Q13), A.mult, c("sc", 9 + t), A.add)
+        tt(r("sc", 0, 3), sizes, r("oc", 0, 3), A.mult)
+        cp(r("ns", 0, 3), sizes)
+        ts(c("bm", 0), c("bi", 0), 63, A.bitwise_and)
+        red(c("sc", 3), r("sc", 0, 3))
+        cp(c("bf", 0), c("bm", 0))
+        ts(c("bf", 1), c("sc", 3), K(QQ), A.max, K(QR), A.mult)
+        ts(c("bf", 2), c("sc", 3), K(QQ), A.is_lt, K(BD), A.mult)
+        ts(r("pr"), r("u0"), c("bf", 0), A.add, c("bf", 1), A.mult)
+        ts(r("ps"), r("pr"), 12, A.arith_shift_right)
+        ts(r("posu"), r("ps"), c("bf", 2), A.add, K(BS), A.add)
 
     def sel(name, k):
         ts(r(name), r("si", 0, 144), K(G15), A.is_equal, K(k), A.mult)
@@ -318,334 +459,380 @@ def rank_program(g, core, T, topo):
 
     def row(name, n, k):
         ts(r(name), r("si", 0, n), 0.0, A.mult, K(k), A.add)
-    fill = [lambda: sel("y0", K0), lambda: ts(r("jt"), r("si", 0, 256), K(K1), A.mult, K(JB), A.add),
-            lambda: sel("y0b", K0), lambda: sel("y1", K1), lambda: row("mv0", 256, K0), lambda: row("mv1", 256, K1),
-            lambda: diag("i16", 1 / 16), lambda: diag("ineg", -1.0)]
-    for s, f in zip(draw_steps(0), fill):
-        s()
-        f()
+    draw(0, r("pC", 0, 3))
+    lazy[0] = True
+    ts(r("jt"), r("si", 0, 256), K(K1), A.mult, K(JB), A.add)
     act(r("ds", 0, CAP), r("jt", 0, CAP))
-    cp(r("nbf", O, S1), r("nbi"))
-    ts(r("nbf", 0, O), r("si", 0, O), -float(O), A.add)
+    act(r("mv0"), r("si", 0, 256), scale=0.0, bias=K(K0))
+    act(r("mv1"), r("si", 0, 256), scale=0.0, bias=K(K1))
+    act(r("m4"), r("si", 0, 512), scale=0.0, bias=K(K4))
+    ms(r("mk2", 0, O), 1024.0)
+    ms(r("mk2", O + GH, S1), 1024.0)
     ms(r("w", 0, O), 0.0)
-    diag("ibias", -15 / 32)
+    act(r("plt", 0, O), r("si", 0, O), scale=K(K0))
+    act(r("plt", S1, S1 + 512), r("si", 0, 512), scale=0.0)
+    ts(K(K2), K(K12), K(K1), A.subtract)
+    ts(K(X10), K(K0), 0.5, A.mult)
+    ts(K(X11), K(K0), K(K2), A.add)
+    ts(K(WR), K(K2), 512.0, A.mult, K(K01), A.add)
+    act(r("mks", S1, S1 + 512), r("si", 0, 512), scale=K(X10), bias=K(X11))
+    ms(r("rm7"), 1.0)
+    ms(r("rm7", 0, 224, 7), 0.0)
+    ms(r("selt", 0, 2048, 16), 0.0)
     ms(r("ones"), 1.0)
     ms(r("msg"), 0.0)
-    sel("y01b", K01)
-    ts(r("d18"), r("jl", 0, 8), float(V), A.add)
-    ts(r("d256"), r("jl", 0, 16), 256.0, A.add)
-    ts(K(RB), K(AK), -20480.0, A.mult, 20480.0, A.add)
-    ts(K(RS), K(K123), 10.0, A.mult, K(K0), A.add)
-    ts(K(RF), K(RB), K(K123), A.mult)
-    ts(K(MG), K(K0), -16.0, A.mult, MAGIC, A.add)
-    ts(K(RB), K(K0), 16.0, A.mult, K(RF), A.add)
-    banks = ("pS", "pE", "pF", "pD")
-
-    def consts2(h):
-        for a in range(8 * h, 8 * h + 8):
-            ts(r("selt", 128 * a, 128 * a + 128), r("bdf"), c("ea", a), A.mult)
-
-    def places0():
-        for a in range(16):
-            mm(r(banks[a // 4], 112 * (a % 4), 112 * (a % 4) + 112), r("selt", 128 * a, 128 * a + 128), r("plcf"))
-
-    def consts3():
-        tt(K(K45), K(K4), K(K5), A.add)
-        ts(K(HB), K(RS), float(DUMP), A.mult, K(RB), A.add)
-        ts(K(TG), K(K5), -512.0, A.mult, K(K4), A.add)
-        ts(c("lg", 0), c("par", 0), K(K0), A.mult)
-        diag("ipos", 1.0)
-        diag("ih", 1.0)
-        ts(c("lg", 1), c("par", 1), K(K1), A.mult, c("lg", 0), A.add)
-        for nme, v in (("bd2", 2.0), ("bdm", -1.0), ("bd16", -16.0), ("bdh", 1.0)):
-            ts(r(nme), r("bdf"), v, A.mult)
-        ts(K(THB), c("lg", 1), -1.0, A.mult, 0.5, A.add)
-        sel("y123", K123)
-
-    def consts4():
-        sel("y45", K45)
-        ts(r("xx", 0, 128), r("si", 0, 128), K(P), A.is_le, -1.0, A.mult)
-        diag("e8", 2048.0)
-        tt(r("um"), r("xx", 0, 128), r("bdf"), A.mult)
-        ms(r("rm"), 1.0)
-        row("m4", 512, K4)
-        ts(r("cl"), r("jl"), -1.0, A.mult, 511.0, A.add)
-        for nme, v in (("d1k", 1024), ("d15", 1536), ("d2k", 2048), ("ddmp", DUMP)):
-            ts(r(nme), r("jl"), float(v), A.add)
-        tt(r("ub"), r("um"), r("e8"), A.add)
-        ms(r("rm", 0, 192, 32), 0.0)
+    ms(r("neg"), -1.0)
+    ms(r("mo"), -float(O))
+    ms(r("rm"), 1.0)
+    ms(r("rm", 0, 192, 32), 0.0)
+    ts(K(K78), K(AK), 8.0, A.is_le, K(G7), A.mult)
+    ts(K(X0), K(K12), K(K78), A.add)
+    ts(K(K9), K(AK), 9.0, A.is_equal)
+    ts(K(X12), K(K9), K(K3), A.add, K(K0), A.add)
+    ts(K(RS), K(X0), SC, A.mult, K(X12), A.add)
+    ts(K(X13), K(K12), 2048 * SC - 6e4, A.mult, 6e4, A.add)
+    ts(K(X14), K(K3), 2048 - 6e4, A.mult, K(X13), A.add)
+    ts(K(MX), K(K78), SC - 6e4, A.mult, K(X14), A.add)
+    ts(K(WH), K(K12), 1 / SC, A.mult, K(K3), A.add)
+    ts(K(G9), K(G16), 9.0, A.add)
+    ts(K(X1), K(AK), -2048 * SC, A.mult, K(K12), A.mult)
+    ts(K(X2), K(AK), -V * SC, A.mult, (6 * V - B0 + 1) * SC, A.add)
+    ts(K(X3), K(K6), SC, A.mult, K(X1), A.add)
+    ts(K(RB), K(X2), K(K78), A.mult, K(X3), A.add)
+    ts(K(R0), K(RS), float(B0), A.mult, K(RB), A.add)
+    ts(K(RF), K(K9), -float(B0), A.mult, K(RB), A.add)
+    ts(K(MG), K(K9), -float(B0), A.mult, MAGIC, A.add)
+    ts(K(US), K(X0), 1 / SC - 1, A.mult, 1.0, A.add)
+    ts(K(MN), K(K78), -2047.0, A.mult, 2048.0, A.add)
+    ts(K(WC), K(K6), 4 / SC, A.mult, K(K78), A.add)
+    ts(K(K123), K(K12), K(K3), A.add)
+    ts(K(X15), K(X0), K(K3), A.add, K(K6), A.add)
+    diag("mh0", K(X15))
+    ts(r("mh1"), r("si", 0, 128), K(G9), A.is_equal, K(WH), A.mult)
+    tt(r("mh"), r("mh0"), r("mh1"), A.add)
+    diag("i0", K(K0))
+    ts(K(X4), K(K123), 1 / 4096, A.mult)
+    ts(K(X5), K(K6), -B0 / 4096 / SC, A.mult, K(X4), A.add)
+    ts(K(WP), K(K78), -V / 4096, A.mult, K(X5), A.add)
+    ts(K(K45), K(K4), K(K5), A.add)
+    ts(K(TG), K(K5), -512.0, A.mult, K(K4), A.add)
+    ts(c("lg", 0), c("par", 0), K(K0), A.mult)
+    ts(c("lg", 1), c("par", 1), K(K1), A.mult, c("lg", 0), A.add)
+    ts(K(THB), c("lg", 1), -1.0, A.mult, 0.5, A.add)
+    for nme, k in (("y0", K0), ("y0b", K0), ("y1", K1), ("y01b", K01), ("y123", WH), ("yrk", WR), ("y45", K45), ("ycl", WC), ("ypos", WP)):
+        sel(nme, k)
+    for nme, v in (("i16", 1 / 16), ("ineg", -1.0), ("ibias", -15 / 32), ("ipos", 1.0), ("ih", 1.0), ("d48", 2047.0), ("d81", 8192.0)):
+        diag(nme, v)
+    for nme, v in (("bd2", 2.0), ("bdm", -1.0), ("bd16", -16.0)):
+        act(r(nme), r("bdf"), scale=v)
+    for nme, v in (("bdh", 1.0), ("bdn", -1.0)):
+        ts(r(nme), r("bdf"), v, A.mult)
+    ts(r("tri"), r("si", 0, 128), K(P), A.is_lt, -1.0, A.mult)
+    tt(r("us"), r("tri"), r("bdf"), A.mult)
+    tt(r("ub"), r("us"), r("d48"), A.add)
+    tt(r("uj"), r("us"), r("d81"), A.add)
+    ts(r("ujn"), r("uj"), -1.0, A.mult)
+    ts(r("cl"), r("jl"), -1.0, A.mult, 511.0, A.add)
+    for nme, n, v in (("d257", 16, 257), ("d1h", 32, 1024), ("d15", 32, 1536), ("d2k", 32, 2048)):
+        ts(r(nme), r("jl", 0, n), float(v), A.add)
+    for b in range(4):
+        o = lambda a: r(("pS", "pE")[b % 2], 112 * a, 112 * a + 112)
+        for a in range(4):
+            mm(o(a), r("selt", 128 * (4 * b + a), 128 * (4 * b + a) + 128), r("plcf"))
+        for a in range(4):
+            act(r("plt", O + 4 * b + a, S1, 16), o(a), AF.Relu, scale=K(RS), bias=K(R0))
+    nd[0] += 1
+    op("y", lambda q, a, k: q.dma_start(T.plt[0:128:16, O:S1], T.si[0:128:16, O:S1]), [], {}, [r("si", O, S1)], [r("plt", O, S1, p=(0, 8))],
+       ("dma%d" % (nd[0] - 1), 16, True), "dma")
+    lazy[0] = False
 
     for t in range(RO):
         final = t == RO - 1
-        mk = lambda a, b, **k: r("mk", 2048 * t + a, 2048 * t + b, **k)
-        w4 = lambda a, b, **k: r("w4", 1536 * t + a, 1536 * t + b, **k)
-        sl = lambda **k: r("sl", 512 * t, 512 * t + 512, **k)
-        tt(r("dr"), r("bag", off=r("posu")), r("jt"), A.min)
+        mk = lambda a, b, **k: r("mk", 2560 * t + a, 2560 * t + b, **k)
+        w4 = lambda a, b, **k: r("w4", a, b, **k)
+        sl = lambda n=512, **k: r("sl", 768 * t, 768 * t + n, **k)
+        wn = lambda lst: r("w", O, O + W, off=lst)
+        cp(r("dr", 0, 256), r("bag", off=r("posu")))
         tolist("pA", 0, "y0", "dr", 256)
-        act(r("drf"), r("bag", off=r("posu")))
-        if t == 0:
-            consts2(0)
         cp(r("tu", 0, 16), r("pA", 0, 16))
-        cp(r("nbu", 0, 256), r("nbf", off=r("tu", 0, 16)))
-        act(r("oldm"), r("w", 0, S1, off=r("tu", 0, 16)), bias=-192.0)
-        for j0, j1 in MOVES:
-            act(r("gb", 16 * j0, 16 * j1), r("w", O, O + W, off=r("nbu", j0, j1)))
-        ts(r("gu"), r("pA", 0, 16), -float(O), A.add, GH - 1.0, A.min)
-        ts(r("t1", 0, 16), r("pA", 0, 16), float(O + GH), A.is_ge)
-        ts(r("t1", 16, 32), r("pA", 0, 16), float(O), A.is_lt)
-        cp(mk(0, 2048, off=r("tu", 0, 16)), r("mv0"))
-        cum(r("mk2"), mk(O, O + GH))
-        tt(r("t1", 32, 48), r("t1", 0, 16), r("t1", 16, 32), A.add)
-        cp(r("rkd"), r("mk2", off=r("gu")))
-        tolist("pA", 0, "y0b", "rkd", 256)
-        ts(r("n0h"), r("nbf", off=r("tu", 0, 16)), float(O), A.add)
-        tolist("pB", 0, "y0", "n0h", 256)
-        tt(r("t1", 48, 64), r("t1", 32, 48), r("d256"), A.mult)
-        ts(r("t1", 0, 16), r("pA", 0, 16), -1.0, A.add)
-        tt(r("t1", 16, 32), r("t1", 0, 16), r("t1", 48, 64), A.max)
-        cp(r("dru"), r("t1", 16, 32))
-        cp(r("ds", off=r("dru")), r("dr"))
-        cp(r("dsh"), r("ds", 0, CAP))
+        cp(r("nbm"), r("nbi", off=r("tu", 0, 16)))
+        lazy[0] = True
+        tt(r("dj"), r("dr", 0, 256), r("jt"), A.min)
+        lazy[0] = False
+        ids = r("msg", MSG * t, MSG * t + 5)
+        clamp = lambda o, i: ts(o, i, 188 - 15 / 32, A.max, 196 - 15 / 32, A.min)
 
-        def sums(j0, j1):
-            o = r("pM", j0, j1)
+        def sums(o, old, rows, j0, j1):
             mm(o, r("ibias"), r("ones", 0, j1 - j0), True, False)
-            mm(o, r("ineg"), r("oldm", j0, j1), False, False)
+            mm(o, r("ineg"), r(old, j0, j1), False, False)
             for i in range(16):
-                mm(o, r("i16"), r("gb", 16 * j0 + i, 16 * j1, 16), False, i == 15)
-        sums(*MOVES[0])
-        tolist("pA", 0, "y1", "dsh", CAP)
-        tolist("pA", 8, "y0", "dsh", CAP)
-        cp(r("tu", 16, 32), r("pB", 0, 16))
-        cp(mk(0, 2048, off=r("tu", 16, 32)), r("mv1"))
-        ts(r("ju", 0, 5), r("pA", 0, 5), 256.0, A.add)
-        tt(r("msg", MSG * t + CAP, MSG * t + CAP + 5), r("pA", 8, 13), r("d18", 0, 5), A.min)
-        cp(r("osel"), r("oldm", off=r("ju", 0, 5)))
-        cum(r("mks"), mk(0, 2048))
-        if t == 0:
-            consts2(1)
-        sums(*MOVES[1])
-        sums(*MOVES[2])
-        act(r("rk"), r("mks", off=r("tu")))
-        act(r("n0f"), r("nbf", off=r("tu", 0, 16)), bias=float(O))
-        tolist("pB", 0, "y01b", "rk", 512)
-        if t == 0:
-            places0()
-        ts(r("rr"), r("pM", 0, 256), 188 - 15 / 32, A.max, 196 - 15 / 32, A.min)
-        tt(r("msg", MSG * t, MSG * t + CAP), r("rr", off=r("ju", 0, 5)), r("osel"), A.add)
-        lo = lambda d: 88 * (3 * t + d)
-        exchange(t, r("msg", MSG * t, MSG * t + MSG), lambda d: r("land", lo(d), lo(d) + MSG), "sent", total_e * (t + 1))
-        if not final:
-            clear(t + 1)
-        ts(r("rku"), r("pB", 0, 32), -1.0, A.add)
-        act(sl(off=r("rku", 0, 16)), r("drf"), AF.Silu)
-        act(sl(off=r("rku", 16, 32)), r("n0f"), AF.Silu)
-        tt(r("w", 0, S1, off=r("tu", 0, 16)), r("rr"), r("oldm"), A.add)
-        if final:
-            dma(T.yx[:, :], r("w", O, S1))
-        if t == 0:
-            consts3()
-        else:
-            cp(r("plt", off=r("stu")), r("hf"))
-        cp(r("sl16"), sl())
-        tolist("pA", 0, "y0", "sl16", 512)
-        if t == 0:
-            for a in range(16):
-                act(r("plt", O + a, S1, 16), r(banks[a // 4], 112 * (a % 4), 112 * (a % 4) + 112), AF.Relu, scale=K(RS), bias=K(RB))
-            act(r("plt", 0, O), r("si", 0, O))
-        near_first = sorted(range(N - 1), key=lambda d: srcs[d] not in mine)
+                mm(o, r("i16"), r(rows, 16 * j0 + i, 16 * j1, 16), False, i == 15)
 
-        def unpack(d):
-            cp(r("gou", 8 * d, 8 * d + 5), r("land", lo(d) + CAP, lo(d) + CAP + 5))
-            cp(r("w", V + GH * d, V + GH * d + V + CAP, off=r("gou", 8 * d, 8 * d + 5)), r("land", lo(d), lo(d) + CAP))
-        unpack(near_first[0])
-        cp(r("su"), r("pA", 0, 32))
-        cp(r("nbu"), r("nbf", off=r("su")))
-        cp(r("sf"), r("pA", 0, 32))
-        act(r("sv"), r("w", 0, S1, off=r("su")))
-        act(r("pb"), r("plt", 0, S1, off=r("su")))
+        def moves(on, late=False):
+            for j0, j1, e in MOVES[t > 0]:
+                if e == on and late == (t == 0 and j1 == 256):
+                    take(e, r("gm", 16 * j0, 16 * j1), wn(r("nbm", j0, j1)))
+
+        def steps():
+            for j0, j1 in SUMS[t > 0]:
+                sums(r("pF", j0, j1), "oldm", "gm", j0, j1)
+            clamp(r("rr"), r("pF", 0, 256))
+
+        def ascending():
+            ts(r("dr", 256, 512), r("nbm"), float(O), A.add)
+            tolist("pC", 0, "y0", "dr", 256, at=256)
+            yield
+            cp(r("tu", 16, 32), r("pC", 0, 16))
+            cp(mk(0, 2560, off=r("tu", 16, 32)), r("mv1"))
+            yield
+            cum(r("mks", 0, S1), mk(0, S1))
+            yield
+            take(RANK, r("rk"), r("mks", off=r("tu")))
+            tolist("pG", 0, "yrk", "rk", 512)
+            act(r("rec"), r("plt", off=r("tu")))
+            ts(r("rku"), r("pG", 0, 32), -1.0, A.add)
+            yield
+            act(sl(768, off=r("rku", 0, 16)), r("rec", 0, 256), AF.Silu)
+            act(sl(768, off=r("rku", 16, 32)), r("rec", 256, 512), AF.Silu)
+            yield
+            ts(r("sl16"), sl(), K(US), A.mult, K(MN), A.min)
+            tolist("pA", 0, "y0", "sl16", 512)
+            cp(r("su"), r("pA", 0, 32))
+            cp(r("nbu"), r("nbi", off=r("su")))
+            yield
+        asc = ascending()
+
+        def sort(k):
+            for _ in range(SORT[t > 0][k]):
+                next(asc)
+            for j0, j1, e in MOVES[t > 0]:
+                if e == k:
+                    cp(r("gm", 16 * j0, 16 * j1), wn(r("nbm", j0, j1)))
+        act(r("oldm"), r("w", 0, S1, off=r("tu", 0, 16)), bias=-192.0)
+        if t > 0:
+            moves("s")
+        sort(0)
+        cp(mk(0, 2048, off=r("tu", 0, 16)), r("mv0"))
+        cum(r("mk2", O, O + GH), mk(O, O + GH))
+        cp(r("rkd"), r("mk2", off=r("tu", 0, 16)))
+        tolist("pB", 0, "y0b", "rkd", 256)
+        sort(1)
+        tt(r("t1"), r("pB", 0, 16), r("d257"), A.min)
+        ts(r("dru"), r("t1"), -1.0, A.add)
+        cp(r("ds", off=r("dru")), r("dj"))
+        cp(r("dsh"), r("ds", 0, CAP))
+        sort(2)
+        lazy[0] = True
         if not final:
             act(r("ds", 0, CAP), r("jt", 0, CAP))
-        mm(r("pS"), r("ipos"), r("sv"))
-        for d in near_first[1:]:
-            unpack(d)
-        for j0, j1 in CHUNKS[1:]:
-            act(r("gb", 16 * j0, 16 * j1), r("w", O, O + W, off=r("nbu", j0, j1)))
-        j0, j1 = CHUNKS[0]
-        cp(r("gb", 16 * j0, 16 * j1), r("w", O, O + W, off=r("nbu", j0, j1)))
-        ts(r("pb16"), r("pb"), 0.1, A.mult, 2048.0, A.min)
-        tolist("pB", 0, "y123", "pb16", 512)
+        lazy[0] = False
+        if t > 0:
+            tolist("pD", 0, "y1", "dsh", CAP)
+            ts(r("ju", 0, 5), r("pD", 0, 5), 256.0, A.add)
+            cp(r("osel"), r("oldm", off=r("ju", 0, 5)))
+        vals = r("msg", MSG * t + 8, MSG * t + 8 + CAP)
+        if t > 0:
+            moves("v")
+            steps()
+            tt(vals, r("rr", off=r("ju", 0, 5)), r("osel"), A.add)
+        mm(r("pB", 32, 37), r("ih"), r("mo", 0, 5), True, False)
+        tolist("pB", 32, "y0", "dsh", CAP, first=False)
+        tt(ids, r("pB", 32, 37), r("d15", 0, 5), A.min)
+        tt(r("msg", MSG * t + 8 + CAP, MSG * t + 13 + CAP), r("pB", 32, 37), r("d15", 0, 5), A.min)
+        if t > 0:
+            pass
+        else:
+            ts(r("ju", 0, 5), ids, float(O), A.add)
+            cp(r("nbc"), r("nbi", off=r("ju", 0, 5)))
+            act(r("osel"), r("w", 0, S1, off=r("ju", 0, 5)), bias=-192.0)
+            take("v", r("gb", 0, 8 * CAP), wn(r("nbc", 0, CAP // 2)))
+            take("s", r("gb", 8 * CAP, 16 * CAP), wn(r("nbc", CAP // 2, CAP)))
+            sums(r("pD", 0, CAP), "osel", "gb", 0, CAP)
+            clamp(r("rr", 0, CAP), r("pD", 0, CAP))
+            tt(vals, r("rr", 0, CAP), r("osel"), A.add)
+        at = lambda s: (MSG - 8) * (3 * t + s)
+        exchange(t, lambda s: r("msg", MSG * t + 8 * (s == 1), MSG * t + MSG - 8 * (s != 1)), lambda d, s: r("land", at(s), at(s + 1)), "sent", total_e * (t + 1))
+        if not final:
+            iota(mk(2560, 2560 + S1), [[0, S1]], 0, 0, "post")
+            iota(r("sl", 768 * t + 768, 768 * t + 1280), [[0, 512]], 0, 0, "post")
+        sort(3)
         if t == 0:
-            consts4()
+            moves("s")
+            moves("v")
+            sort(4)
+            moves("s", True)
+            steps()
+        tt(r("w", 0, S1, off=r("tu", 0, 16)), r("rr"), r("oldm"), A.add)
+        if t > 0:
+            sort(4)
+        sort(5)
+        if final:
+            dma(T.yx[:, :], r("w", O, S1))
+        came = {slot(rank, d): float(GH * d) for d in range(N - 1)}
+        ts(r("gou", 16, 21), r("land", at(2), at(2) + 5), came[2], A.add)
+        cp(r("w", S1, off=r("gou", 16, 21)), r("land", at(2) + 8, at(3)))
+        ts(r("gou", 0, 5), r("land", at(0), at(0) + 5), came[0], A.add)
+        ts(r("gou", 5, 10), r("land", at(2) - 8, at(2) - 3), came[1], A.add)
+        cp(r("w", S1, off=r("gou", 0, 10)), r("land", at(0) + 8, at(2) - 8))
+        act(r("sv"), r("w", 0, S1, off=r("su")))
+        mm(r("pS"), r("ipos"), r("sv"))
+        for j0, j1, e in CHUNKS:
+            take(e, r("gb", 16 * j0, 16 * j1), wn(r("nbu", j0, j1)))
+        cp(r("sf"), r("pA", 0, 32))
+        lazy[0] = True
+        if not final:
+            ts(r("slb"), sl(), K(MX), A.min)
+        lazy[0] = False
         z = lambda n, k, o=0: r(n, o + 32 * k, o + 32 * k + 32)
-
-        def early1():
-            ts(z("e1", 0), r("pB", 0, 32), float(V), A.is_ge)
-            ts(z("e1", 1), r("pB", 0, 32), float(2 * V), A.is_ge)
-            ts(z("e1", 2), r("sf"), float(O), A.is_lt, 4.0, A.mult)
-            ts(z("nl", 0), r("sf"), float(O), A.is_ge)
-
-        def early2():
-            tt(z("e1", 3), z("e1", 0), z("e1", 1), A.add)
-
-        def early3():
-            tt(z("e1", 4), z("e1", 3), z("e1", 2), A.add)
-            ts(z("e1", 0), z("e1", 3), -float(V), A.mult, -4096.0, A.add)
-
-        def early4():
-            tt(r("pos"), z("e1", 0), r("pB", 0, 32), A.add)
-            for k in range(3):
-                ts(z("oh", k), z("e1", 4), float(k), A.is_equal)
-
-        def early5():
-            for k in range(3):
-                ts(z("rq", k), z("oh", k), 2.0 * k - 11, A.mult, 9.0, A.add)
-                tt(z("qj", k), z("nl", 0), z("oh", k), A.subtract)
-                tt(z("pp", k), z("oh", k), r("pos"), A.mult)
-            cum(r("xx", 0, 96), r("oh"))
-
-        def early6():
-            for k in range(3):
-                ts(z("qj", k), z("qj", k), 2.0 * k - 11, A.mult, 9.0, A.add)
-            ts(r("pp"), r("pp"), 1 / 4096, A.mult, 1.0, A.add)
-            ts(r("nq", 0, 3), r("ns", 0, 3), K(K0), A.mult)
-            ts(r("nq", 8, 11), r("ns", 0, 3), -1024.0, A.add, K(K0), A.mult)
-            cp(c("nq", 4), c("xx", 31))
-            tt(r("nq", 5, 7), r("xx", 63, 96, 32), r("xx", 31, 64, 32), A.subtract)
-
-        def early7():
-            tt(r("nqh", 0, 3), r("nq", 0, 3), r("nq", 4, 7), A.subtract)
-            tt(r("nqh", 4, 7), r("nq", 8, 11), r("xx", 31, 96, 32), A.subtract)
-        early = [early1, early2, early3, early4, early5, early6, early7]
-        for n, (j0, j1) in enumerate(CHUNKS):
+        tolist("pB", 0, "ycl", "sl16", 512)
+        tolist("pC", 0, "ypos", "sl16", 512)
+        ts(r("v18"), r("pB", 0, 32), 4.0, A.is_ge, 18.0, A.mult)
+        for k in range(3):
+            ts(z("ne", k), r("pB", 0, 32), 4.0 + k, A.not_equal)
+        for k in range(3):
+            ts(z("rq", k), z("ne", k), 83.0 - 2 * k, A.mult, 16.0 + 2 * k, A.add)
+            tt(z("pp", k), r("pC", 0, 32), z("ne", k), A.max)
+            tt(z("pn", k), r("pC", 0, 32), z("ne", k), A.subtract)
+        scan(r("sa"), r("rm", 0, 96), r("ne"), A.mult, A.add)
+        scan(r("sb"), r("ne"), r("neg"), A.add, A.add)
+        ts(r("nq", 0, 3), r("ns", 0, 3), K(K0), A.mult, -32.0, A.add)
+        ts(r("nq", 4, 7), r("ns", 0, 3), -1536.0, A.add, K(K0), A.mult)
+        ts(c("lg", 5), c("ns", 2), B0 + 2 * V - 1.0, A.add)
+        tt(r("nqh", 0, 3), r("nq", 0, 3), r("sa", 31, 96, 32), A.add)
+        tt(r("nqh", 4, 7), r("nq", 4, 7), r("sb", 31, 96, 32), A.add)
+        for n, (j0, j1, e) in enumerate(CHUNKS):
             o = r("pE", j0, j1) if n < len(CHUNKS) - 1 else r("pF", j0, j1)
             mm(o, r("bd16"), r("sv", j0, j1), True, False)
             for i in range(16):
                 mm(o, r("bdm"), r("gb", 16 * j0 + i, 16 * j1, 16), False, False)
             for i in range(16):
                 tt(r("mx", 512 * i + j0, 512 * i + j1), r("gb", 16 * j0 + i, 16 * j1, 16), r("pS", j0, j1), A.max)
-                if i % 4 == 3:
-                    for k in range(i - 3, i + 1):
-                        mm(o, r("bd2"), r("mx", 512 * k + j0, 512 * k + j1), False, k == 15)
-                if early and i % 2 == 1:
-                    early.pop(0)()
+                mm(o, r("bd2"), r("mx", 512 * i + j0, 512 * i + j1), False, i == 15)
         jl = CHUNKS[-1][0]
-        if t == 0:
-            act(w4(0, 512), r("si", 0, 512), scale=K(K5), bias=K(TG))
-            act(w4(1024, 1536), r("si", 0, 512), AF.Relu, scale=K(RS), bias=K(HB))
-            for k in (1, 2):
-                dma(r("w4", 1536 * k, 1536 * k + 512), w4(0, 512))
-                dma(r("w4", 1536 * k + 1024, 1536 * k + 1536), w4(1024, 1536))
         act(r("ge", 0, jl), r("pE", 0, jl), AF.Sign, bias=K(THB))
         act(r("ge", jl, 512), r("pF", jl, 512), AF.Sign, bias=K(THB))
-        tolist("pA", 0, "y01b", "ge", 512)
+        mm(r("pA", 0, 32), r("ih"), r("v18"), True, False)
+        tolist("pA", 0, "y01b", "ge", 512, first=False)
         for k in range(3):
             tt(z("fl", k, 96), r("pA", 0, 32), z("rq", k), A.is_equal)
-        for k in range(3):
-            tt(z("fl", k), r("pA", 0, 32), z("qj", k), A.is_equal)
+        scan(r("s1", 96, 192), r("rm", 0, 96), r("fl", 96, 192), A.mult, A.add)
         cum(r("s2"), r("fl", 96, 192))
-        scan(r("s1"), r("rm"), r("fl"), A.mult, A.add)
-        Lc, Dn, Nn = (lambda k: c("pC", k)), (lambda k: c("pC", 4 + k)), r("pC", 8, 11)
+        Lc, Dn, Nn = (lambda k: c("pC", k)), (lambda k: c("pC", 4 + k)), r("pG", 100, 103)
         mm(r("pC", 0, 3), r("bdh"), r("nqh", 0, 3), True, False)
         mm(r("pC", 0, 3), r("bdh"), r("s1", 127, 192, 32), False, True)
         mm(r("pC", 4, 7), r("bdh"), r("nqh", 4, 7), True, False)
         mm(r("pC", 4, 7), r("bdh"), r("s2", 31, 96, 32), False, True)
-        mm(Nn, r("bdh"), r("nqh", 0, 3), True, False)
-        mm(Nn, r("bdh"), r("s1", 127, 192, 32), False, False)
-        mm(Nn, r("bdh"), r("s1", 31, 96, 32), False, True)
-        mm(r("pC", 32, 128), r("um"), r("fl", 0, 96), True, False)
-        mm(r("pC", 32, 128), r("bdh"), r("s1", 0, 96), False, True)
         tt(r("zz"), r("fl", 96, 192), r("pp"), A.max)
-        tt(z("nl", 1), z("fl", 0, 96), z("fl", 1, 96), A.add)
-        tt(z("nl", 2), z("fl", 2, 96), z("nl", 0), A.subtract)
         for k in range(3):
             ts(z("ho", k), z("zz", k), 4096.0, A.mult, Lc(k), A.is_lt)
-        for k in range(3):
-            ts(z("xx", k), z("zz", k), 4096.0, A.mult, Dn(k), A.subtract)
         cum(r("hs"), r("ho"))
-        mm(r("pD", 0, 96), r("ub"), r("ho"), True, False)
-        mm(r("pD", 0, 96), r("bdh"), r("hs"), False, True)
-        mm(c("pD", 100), r("bdh"), c("hs", 95))
-        tt(z("xx", 3), z("xx", 0), z("xx", 1), A.min)
-        tt(z("xx", 4), z("xx", 2), r("d15"), A.min)
-        for k in (1, 2):
-            ts(z("yy", k), r("d1k"), Dn(k), A.add, Lc(k), A.is_ge)
-            ts(z("yy", 2 + k), r("d1k"), Dn(k), A.add, float(V * k), A.add)
-        tt(z("xx", 1), z("xx", 3), z("xx", 4), A.min)
-        ts(z("yy", 0), r("d1k"), Dn(0), A.add)
-        tt(z("o4", 0), z("pD", 0), z("xx", 1), A.max)
-        tt(r("yy", 160, 224), r("yy", 32, 96), r("yy", 96, 160), A.mult)
-        tt(z("o4", 1), z("pD", 1), z("o4", 0), A.max)
-        tt(z("yy", 1), z("yy", 0), z("yy", 5), A.max)
-        tt(z("o4", 2), z("pD", 2), z("o4", 1), A.max)
-        tt(z("yy", 2), z("yy", 1), z("yy", 6), A.max)
-        ts(r("o4u"), z("o4", 2), -1024.0, A.add)
-        act(w4(0, 1536, off=r("o4u")), r("pb"), AF.Silu)
-        cp(r("tpu"), z("yy", 2))
+        tt(r("zn"), r("pn"), r("fl", 96, 192), A.subtract)
         for k in range(3):
-            ts(z("vv", k), z("pC", k, 32), Lc(k), A.add, float(V * k), A.add)
-        tt(z("nl", 1), z("nl", 1), z("nl", 2), A.add)
-        cp(r("tb"), r("bag", off=r("tpu")))
-        tt(r("ww"), r("vv"), r("fl", 0, 96), A.mult)
-        ts(z("nl", 2), z("nl", 1), 1.0, A.add)
-        cp(c("lg", 4), c("pD", 100))
-        cp(r("ns", 0, 3), Nn)
-        tt(z("npl", 0), z("ww", 0), z("ww", 1), A.add)
-        tt(z("vv", 0), z("nl", 2), r("ddmp"), A.mult)
-        ts(z("vv", 1), z("nl", 2), 4096.0, A.mult)
-        tt(z("npl", 1), z("ww", 2), z("vv", 0), A.add)
-        tt(z("vv", 2), z("vv", 1), r("sf"), A.add)
-        tt(z("npl", 2), z("npl", 0), z("npl", 1), A.add)
-        tt(z("vv", 1), z("vv", 2), r("d2k"), A.min)
-        tolist("pB", 0, "y0", "tb", 512)
-
-        def rows(a0, a1):
-            for a in range(a0, a1):
-                mm(r("pD", a, 512, 16), r("selt", 128 * a, 128 * a + 128), z("npl", 2))
-            if a1 == 16:
-                act(r("nrec"), r("pD"), AF.Relu, scale=K(RS), bias=K(RF if final else RB))
-        rows(0, 8)
+            ts(z("xh", k), z("zn", k), 4096.0, A.mult, Dn(k), A.subtract)
+        mm(r("pD", 0, 224, 7), r("ih"), r("d1h"))
+        for k in range(3):
+            mm(r("pD", 1 + k, 224, 7), r("ih"), z("xh", k))
+        for k in range(3):
+            mm(r("pD", 4 + k, 224, 7), r("ub"), z("ho", k), True, False)
+            mm(r("pD", 4 + k, 224, 7), r("bdh"), z("hs", k), False, True)
+        mm(c("pD", 300), r("bdh"), c("hs", 95))
+        scan(r("o7"), r("rm7"), r("pD", 0, 224), A.mult, A.max)
+        ts(r("o4u"), r("o7", 6, 224, 7), -1024.0, A.add)
+        act(w4(512, 1024), r("si", 0, 512), scale=K(K5), bias=K(TG))
+        act(w4(1024, 1536), r("si", 0, 512), AF.Relu, scale=K(RS), bias=K(RB))
+        act(w4(0, 1536, off=r("o4u")), sl() if final else r("slb"), AF.Silu)
+        lazy[0] = True
+        cp(c("lg", 4), c("pD", 300))
+        for k in range(3):
+            ts(z("fl", k), r("pA", 0, 32), 16.0 + 2 * k, A.is_equal)
+        scan(r("s1", 0, 96), r("rm", 0, 96), r("fl", 0, 96), A.mult, A.add)
+        mm(r("pG", 0, 96), r("bdn"), r("s1", 96, 192), True, False)
+        mm(r("pG", 0, 96), r("ujn"), r("fl", 96, 192), False, False)
+        mm(r("pG", 0, 96), r("uj"), r("fl", 0, 96), False, False)
+        mm(r("pG", 0, 96), r("bdh"), r("s1", 0, 96), False, True)
         if not final:
-            cp(r("jou"), z("npl", 2))
-            act(r("bag", off=r("jou")), sl(), AF.Silu)
-        cp(r("lvu"), z("vv", 1))
-        st = [lambda: None] * 8 if final else draw_steps(t + 1)
+            mm(Nn, r("bdh"), r("nqh", 0, 3), True, False)
+            mm(Nn, r("bdh"), r("s1", 31, 96, 32), False, True)
+        for k in range(3):
+            ts(z("vv", k), z("pG", k), Lc(k), A.add, B0 + V * k - 8193.0, A.add)
+        tt(z("npl", 0), z("vv", 0), z("vv", 1), A.max)
+        tt(z("npl", 1), z("vv", 2), r("jl"), A.max)
+        tt(z("npl", 2), z("npl", 0), z("npl", 1), A.max)
 
-        def whole(h):
-            ts(r("plf", O + 896 * h, O + 896 * h + 896), r("plt", O + 896 * h, O + 896 * h + 896), K(MG), A.add, MAGIC, A.subtract)
-        for s in st[:3]:
-            s()
-        if final:
-            whole(0)
-        scan(r("ts4"), r("m4"), w4(0, 512), A.mult, A.add)
-        mm(r("pA", 0, 32), r("ih"), r("cl"), True, False)
-        tolist("pA", 0, "y45", "ts4", 512, first=False)
-        rows(8, 16)
-        for s in st[3:7]:
-            s()
-        if final:
-            whole(1)
+        def tails():
+            for k in (1, 2):
+                ts(z("yy", k), r("d15"), Dn(k), A.add, Lc(k), A.is_ge)
+                ts(z("yy", 2 + k), r("d15"), Dn(k), A.add, float(B0 + V * k), A.add)
+            ts(z("yy", 0), r("d15"), Dn(0), A.add, float(B0), A.add)
+            tt(r("yy", 160, 224), r("yy", 32, 96), r("yy", 96, 160), A.mult)
+            tt(z("yy", 7), z("yy", 0), z("yy", 5), A.max)
+            tt(z("yy", 8), z("yy", 7), z("yy", 6), A.max)
+            ts(r("tpu"), z("yy", 8), c("lg", 5), A.min)
+            cp(r("tb"), r("bag", off=r("tpu")))
+            tolist("pB", 0, "y0", "tb", 512)
+
+        def leavers():
+            ts(z("lv", 0), z("npl", 2), float(B0), A.is_lt, 4096.0, A.mult)
+            tt(z("lv", 1), z("lv", 0), r("sf"), A.add)
+            tt(z("lv", 2), z("lv", 1), r("d2k"), A.min)
+            cp(r("lvu"), z("lv", 2))
+
+        def records():
+            if not final:
+                mm(r("pS"), r("i0"), r("sl16"), True, False)
+            for a in range(16):
+                mm(r("pS", a, 512, 16), r("selt", 128 * a, 128 * a + 128), z("npl", 2), final, final or a == 15)
+            act(r("nrec"), r("pS"), AF.Relu, scale=K(RS), bias=K(RF if final else RB))
+
+        def holes():
+            scan(r("ts4"), r("m4"), w4(512, 1024), A.mult, A.add)
+            mm(r("pF", 0, 32), r("ih"), r("cl"), True, False)
+            tolist("pF", 0, "y45", "ts4", 512, first=False)
+            cp(r("ixu"), r("pF", 0, 32))
 
         def stayers():
-            ts(z("st", 0), r("pA", 0, 32), c("lg", 4), A.is_ge, 4096.0, A.mult)
+            ts(z("st", 0), r("pF", 0, 32), c("lg", 4), A.is_ge, 4096.0, A.mult)
             tt(z("st", 1), z("st", 0), r("pB", 0, 32), A.add)
             tt(z("st", 2), z("st", 1), r("d2k"), A.min)
             cp(r("stu"), z("st", 2))
         if final:
-            cp(r("ixu"), r("pA", 0, 32))
-            ts(r("hf"), w4(1024, 1536, off=r("ixu")), K(MG), A.add, MAGIC, A.subtract)
+            for h in range(4):
+                ts(r("plf", O + 448 * h, O + 448 * h + 448), r("plt", O + 448 * h, O + 448 * h + 448), K(MG), A.add, MAGIC, A.subtract)
+            lazy[0] = False
+            records()
+            holes()
+            act(r("hf"), w4(1024, 1536, off=r("ixu")), bias=K(MG))
+            tails()
+            leavers()
             stayers()
-            cp(r("plf", off=r("stu")), r("hf"))
             cp(r("plf", off=r("lvu")), r("nrec"))
-            op("y", lambda q, a, k: q.dma_start(T.yp[:, :], T.plf[0:128:16, O:S1]), [], {}, [r("plf")], [], ("dma%d" % nd[0], 16, True))
+            ts(r("plf", off=r("stu")), r("hf"), 1.0, A.mult, -MAGIC, A.add)
+            op("y", lambda q, a, k: q.dma_start(T.yp[:, :], T.plf[9:128:16, O:S1]), [], {}, [r("plf", p=(0, 8))], [], ("dma%d" % nd[0], 16, True), "dma")
         else:
-            cp(r("ixu"), r("pA", 0, 32))
-            ts(r("hg"), w4(1024, 1536, off=r("ixu")), 0.1, A.mult, 2048.0, A.min)
-            tolist("pC", 0, "y123", "hg", 512)
-            act(r("plt", off=r("lvu")), r("nrec"), AF.Silu)
-            act(r("hf"), w4(1024, 1536, off=r("ixu")))
-            st[7]()
+            cp(r("jou"), z("npl", 2))
+            tails()
+            leavers()
+            act(r("bag", off=r("jou")), sl(), AF.Silu)
+            draw(t + 1, Nn)
+            records()
+            lazy[0] = False
+            holes()
+            lazy[0] = True
             stayers()
-            cp(r("hou"), r("pC", 0, 32))
+            lazy[0] = False
+            cp(r("hg"), w4(1024, 1536, off=r("ixu")))
+            tolist("pE", 0, "y123", "hg", 512)
+            cp(r("hou"), r("pE", 0, 32))
             cp(r("bag", off=r("hou")), r("tb"))
-    emit(g, T, ops)
+            act(r("plt", off=r("lvu")), r("nrec"), AF.Silu)
+            lazy[0] = True
+            mm(r("pD"), r("i0"), r("tb"), True, False)
+            mm(r("pD"), r("mh"), r("hg"), False, True)
+            act(r("hf"), r("pD"))
+            act(r("plt", off=r("stu")), r("hf"), AF.Silu)
+            lazy[0] = False
+    key = slot(rank, 0)
+    if key not in ORDERS:
+        order = schedule(ops)
+        ORDERS[key] = (order, depend([ops[k] for k in order], False))
+    emit(g, T, [ops[k] for k in ORDERS[key][0]], ORDERS[key][1])

@@ -11,11 +11,12 @@ MSG = 96
 MAGIC = 12582912.0
 SC = 16.0
 F, B, H, I, U = "float32", "bfloat16", "float16", "int32", "uint16"
-MOVES = (((0, 96, "s"), (192, 256, "s"), (96, 192, "v")), ((0, 80, "s"), (120, 192, "s"), (192, 256, "s"), (80, 104, 0), (104, 120, 1)))
+MOVES = (((0, 80, "s"), (80, 144, "s"), (144, 208, "s"), (208, 256, "v")), ((0, 80, "s"), (120, 192, "s"), (192, 256, "s"), (80, 104, 0), (104, 120, 1)))
 SORT = ((1, 1, 1, 1, 1, 1), (1, 1, 1, 1, 1, 1))
-RANK = "s"
-SUMS = (((0, 96), (96, 192), (192, 256)), ((0, 120), (120, 192), (192, 256)))
-CHUNKS = ((0, 96, "v"), (96, 224, "s"), (224, 352, "s"), (352, 448, "s"), (448, 512, "s"))
+RANK, EARLY, VIAW, NEW = "vs", 4, False, False
+CUTM, CUTU, SV, PRE = 1, 4, 1, 1
+SUMS = (((0, 80), (80, 144), (144, 256)), ((0, 120), (120, 192), (192, 256)))
+CHUNKS = ((0, 64, "s"), (64, 160, "v"), (160, 288, "s"), (288, 384, "s"), (384, 448, "s"), (448, 512, "s"))
 FILL = (3328, 4608)
 
 
@@ -26,7 +27,7 @@ def _sb(c, d):
 BUF = {
     "w": _sb(4688, B), "nbi": _sb(2048, I), "bag": _sb(6144, F), "plt": _sb(2560, F), "plf": _sb(2560, F), "si": _sb(2048, F),
     "mk": _sb(3 * 2560, B), "mks": _sb(2560, B), "mk2": _sb(2048, B), "w4": _sb(1536, F), "sl": _sb(3 * 768, F), "sl16": _sb(512, H),
-    "slb": _sb(512, F), "dj": _sb(256, H), "yrk": _sb(144, B), "mh0": _sb(128, F), "mh1": _sb(128, F), "mh": _sb(128, H), "i0": _sb(128, H),
+    "slb": _sb(512, F), "dj": _sb(256, H), "dz": _sb(256, H), "nw": _sb(256, B), "yrk": _sb(144, B), "mh0": _sb(128, F), "mh1": _sb(128, F), "mh": _sb(128, H), "id16": _sb(112, H), "r0": _sb(16, F), "mb": _sb(128, H), "i0": _sb(128, H),
     "rm7": _sb(224, F), "pn": _sb(96, F), "zn": _sb(96, F), "xh": _sb(96, H), "d1h": _sb(32, H), "o7": _sb(224, F),
     "gb": _sb(8192, B), "gm": _sb(4096, B), "mx": _sb(8192, B), "selt": _sb(2048, F), "xg": _sb(128, F),
     "plci": _sb(112, I), "plcf": _sb(112, F), "plcu": _sb(112, U), "junk": _sb(224, F),
@@ -38,13 +39,13 @@ BUF = {
     "e8": _sb(128, F), "d48": _sb(128, F), "tri": _sb(128, F), "ones": _sb(256, B), "m4": _sb(512, B), "jt": _sb(256, F), "mv0": _sb(256, B), "mv1": _sb(256, B),
     "rm": _sb(192, H), "neg": _sb(96, H),
     "jl": _sb(32, F), "cl": _sb(32, H), "u0": _sb(16, F), "djc": _sb(16, F), "d2k": _sb(32, F), "d15": _sb(32, F), "d1k": _sb(32, F),
-    "mo": _sb(8, H), "d257": _sb(16, F), "oc": _sb(4, F), "d81": _sb(128, F), "us": _sb(128, H), "uj": _sb(128, H), "ujn": _sb(128, H),
+    "mo": _sb(8, H), "d257": _sb(16, F), "oc": _sb(4, F), "eq": _sb(16, F), "le": _sb(16, F), "ge": _sb(16, F), "xu": _sb(16, F), "d81": _sb(128, F), "us": _sb(128, H), "uj": _sb(128, H), "ujn": _sb(128, H),
     "ns": _sb(4, F), "cnt": _sb(8, F), "sc": _sb(16, F), "bi": _sb(4, I), "bm": _sb(4, I), "bf": _sb(4, F), "iv": _sb(16, I),
     "pr": _sb(16, I), "ps": _sb(16, I), "pm": _sb(16, F), "posu": _sb(16, U),
     "dr": _sb(512, H), "rec": _sb(512, F), "tu": _sb(32, U), "nbm": _sb(256, U), "nbu": _sb(512, U),
     "t1": _sb(16, F), "oldm": _sb(256, B), "rr": _sb(256, B), "rkd": _sb(256, B), "rk": _sb(512, B), "dru": _sb(16, U), "rku": _sb(32, U),
     "ds": _sb(512, F), "dsh": _sb(80, H), "ju": _sb(6, U), "nbc": _sb(CAP, U), "osel": _sb(80, B), "msg": _sb(3 * MSG, H), "land": _sb(9 * 88, H), "gou": _sb(24, U),
-    "su": _sb(32, U), "sf": _sb(32, F), "sv": _sb(512, B), "pb": _sb(512, F), "pb16": _sb(512, H), "ge": _sb(512, B),
+    "su": _sb(32, U), "sf": _sb(32, F), "sv": _sb(512, B), "sg": _sb(512, B),
     "ne": _sb(96, H), "rq": _sb(96, F), "pp": _sb(96, F), "v18": _sb(32, H), "sa": _sb(96, F), "sb": _sb(96, F), "nq": _sb(8, F), "nqh": _sb(8, H),
     "fl": _sb(192, H), "jn": _sb(96, H), "s1": _sb(192, H), "s2": _sb(96, H), "zz": _sb(96, F), "ho": _sb(96, H), "hs": _sb(96, H), "xx": _sb(192, F),
     "o4": _sb(96, F), "o4u": _sb(32, U), "vv": _sb(96, F), "ww": _sb(96, F), "npl": _sb(96, F), "lv": _sb(96, F), "jou": _sb(32, U), "lvu": _sb(32, U),
@@ -114,7 +115,7 @@ def depend(ops, banks):
 CY, WAKE, GATHER, SCATTER, SEND = 0.83, 200.0, 1.5, 2.5, 2000.0
 
 
-PASSES = 2
+PASSES, SAME, TRIES = 2, 200.0, 200
 
 
 def cost(q, kind, args, rd, wr):
@@ -127,7 +128,7 @@ def cost(q, kind, args, rd, wr):
     if kind == "dma":
         a = (wr + rd)[0]
         x = width(a) * (2 if two(a) else 4) * 0.45 * (a[5][1] - a[5][0]) / 128
-        return 50 + x, 2000 + x
+        return 100 + x, 1500 + x
     n = width(args[1] if kind == "red" else wr[0])
     if q == "t":
         x = max(64, n) * 0.42 * (1 if two(args[2]) else 4)
@@ -159,7 +160,9 @@ def schedule(ops):
     def lat(j, k):
         if ops[j]["kind"] == ops[k]["kind"] == "dma" or ops[k]["kind"] == "post" and ops[j]["kind"] == "send":
             return ops[j]["cost"][0] - ops[j]["cost"][1]
-        return 0.0 if ops[j]["q"] == ops[k]["q"] == "t" else WAKE
+        if ops[k]["kind"] == "land":
+            return -500.0 if ops[k]["ev"][0][0] == "n" else 0.0
+        return WAKE if ops[j]["q"] != ops[k]["q"] else 0.0 if ops[k]["q"] == "t" else SAME
     n = len(ops)
     succ = [[] for _ in ops]
     for k in range(n):
@@ -207,8 +210,47 @@ def schedule(ops):
         if best is None or max(end) < best[0]:
             best = (max(end), start)
         rank = place(sorted(range(n), key=lambda k: (-end[k], -k)), succ, True)[1]
-        order = sorted(range(n), key=lambda k: (-rank[k], k))
-    return sorted(range(n), key=lambda k: (best[1][k], k))
+        order.clear()
+        seen[:] = [False] * n
+        for k in sorted(range(n), key=lambda k: (-rank[k], k)):
+            visit(k)
+    order = sorted(range(n), key=lambda k: (best[1][k], k))
+    start, end = place(order, deps, False)
+    tried = set()
+    for _ in range(TRIES):
+        ahead = {}
+        for q in "vstg":
+            l = sorted((k for k in range(n) if ops[k]["q"] == q), key=lambda k: start[k])
+            ahead.update(zip(l[1:], l))
+        k = max(range(n), key=lambda k: end[k])
+        pairs = []
+        while start[k] > 0:
+            j = max(deps[k], key=lambda j: end[j] + lat(j, k), default=None)
+            if j is None or end[j] + lat(j, k) < start[k] - 1:
+                j = ahead.get(k)
+                if j is None:
+                    break
+                if j not in deps[k] and (j, k) not in tried and ops[k]["q"] != "t":
+                    pairs.append((j, k))
+            k = j
+        if not pairs:
+            break
+        j, k = max(pairs, key=lambda x: ops[x[0]]["cost"][0])
+        tried.add((j, k))
+        later = {j}
+        a, b = order.index(j), order.index(k)
+        if a > b:
+            continue
+        for x in order[a:b]:
+            if deps[x] & later:
+                later.add(x)
+        if deps[k] & later:
+            continue
+        new = order[:a] + [x for x in order[a:b + 1] if x not in later] + [x for x in order[a:b] if x in later] + order[b + 1:]
+        s2, e2 = place(new, deps, False)
+        if max(e2) <= max(end):
+            order, start, end = new, s2, e2
+    return sorted(range(n), key=lambda k: (start[k], k))
 
 
 ORDERS = {}
@@ -360,81 +402,88 @@ def rank_program(g, core, T, topo):
     (P, AK, G15, G16, P16, K0, K1, K01, K02, K12, K4, K5, K45, K6, G7, K78, RS, RB, R0, RF, MN, US, WC, WP, TG, THB, JB, MG,
      CL, QM, QQ, QR, Q13, BS, BD, X0, X1, X2, X3, X4, X5, X6, X7, X8, X9, K3, K123,
      K2, K9, G9, WR, WH, MX, X10, X11, X12, X13, X14, X15) = range(59)
-    K = lambda k: c("col", k)
+    FLAG = {K0: ("eq", 0), K1: ("eq", 1), K2: ("eq", 2), K3: ("eq", 3), K4: ("eq", 4), K5: ("eq", 5), K6: ("eq", 6), K9: ("eq", 9),
+            K01: ("le", 1), K02: ("le", 2), G7: ("ge", 7)}
+    K = lambda k: c(*FLAG.get(k, ("col", k)))
 
     dma(r("w", O, O + GH), T.x[:, 0:GH])
     dma(r("plci"), T.plc[:, :])
-    dma(r("prm", 0, 2, p=(0, 8)), T.th[:, :])
     dma(r("prm", 4, 7, p=(0, 8)), T.sd[:, :])
+    dma(r("prm", 0, 2, p=(0, 8)), T.th[:, :])
     dma(r("nbi", O, S1), T.nb[:, :])
     dma(r("w", O + GH, S1), T.x[:, GH:V])
     iota(r("si", 0, 256), [[1, 256]], 0, 0)
     iota(c("pint", 0), [[0, 1]], 0, 1)
     iota(r("xg"), [[16, 8], [0, 16]], 0, 0)
     exchange(3, lambda s: r("w", O, O + GH), lambda d, s: r("w", S1 + d * GH, S1 + (d + 1) * GH), "sent0", total_e)
-    ms(r("sl", 0, 512), 0.0)
-    act(r("si", V, 2048), r("si", 0, 256), AF.Silu, bias=float(V))
-    ts(r("si", 256, 512), r("si", 0, 256), 256.0, A.add)
-    ts(r("si", 512, 1024), r("si", 0, 512), 512.0, A.add)
-    ts(r("si", 1024, V), r("si", 0, V - 1024), 1024.0, A.add)
     ms(c("bag", B0 + 2 * V - 1), 0.0)
-    lazy[0] = True
-    ms(r("mk", 0, 2048), 0.0)
-    ts(r("nbi", 0, O), r("si", 0, O), 2.0, A.mult, float(V), A.add)
-    lazy[0] = False
+    ms(r("sl", 0, 512), 0.0)
 
     def selectors(b):
         o = r("selt", 512 * b, 512 * b + 512)
         op("g", lambda q, a, k: q.affine_select(a[0], a[1], [[-1, 4], [-16, 8], [0, 16]], A.not_equal, 1.0, -4 * b, 1),
-           [o, r("sl", 0, 512)], {}, [r("sl", 0, 512)], [o], kind="post")
+           [o, r("sl", 0, 512)], {}, [r("sl", 0, 512)], [o], kind="post" if b >= PRE else None)
     for b in range(4):
         selectors(b)
+    iota(r("plt", S1, S1 + 512), [[0, 512]], 0, 0, "post")
+    iota(r("rm7"), [[0, 32], [1, 7]], 0, 0, "post")
+    op("g", lambda q, a, k: q.affine_select(a[0], a[0], [[0, 32], [1, 7]], A.is_equal, 1.0, 0, 0), [r("rm7")], {}, [r("rm7")], [r("rm7")], kind="post")
+    act(r("si", V, 2048), r("si", 0, 256), AF.Silu, bias=float(V))
+    ts(r("si", 256, 512), r("si", 0, 256), 256.0, A.add)
+    ts(c("pint", 1), c("pint", 0), 15, A.bitwise_and)
+    cp(K(P), c("pint", 0))
+    ts(r("si", 512, 768), r("si", 0, 256), 512.0, A.add)
+    cp(K(AK), c("pint", 1))
+    ts(r("si", 768, 1280), r("si", 0, 512), 768.0, A.add)
+    ts(r("eq"), r("si", 0, 16), K(AK), A.is_equal)
+    ts(r("le"), r("si", 0, 16), K(AK), A.is_ge)
+    ts(r("ge"), r("si", 0, 16), K(AK), A.is_le)
+    ts(K(G16), K(P), K(AK), A.subtract)
+    ts(K(P16), K(P), 16.0, A.mult)
+    ts(r("si", 1280, V), r("si", 0, 512), 1280.0, A.add)
+    ts(r("e8", p=(0, 8)), r("xg", p=(0, 8)), r("col", P16, P16 + 1, p=(0, 8)), A.is_equal)
+    ts(r("bdf"), r("xg"), K(G16), A.is_equal)
+    lazy[0] = True
+    ts(r("xu"), r("si", 0, 16), 1 / 16, A.mult)
+    for k in range(4):
+        ms(r("mk", 512 * k, 512 * k + 512), 0.0)
+    ts(r("nbi", 0, O), r("si", 0, O), 2.0, A.mult, float(V), A.add)
+    lazy[0] = False
     cp(r("plcu"), r("plci"))
     act(r("bag", B0, PL, off=r("plcu")), r("si", O, S1), AF.Silu)
     act(r("bag", PL, PL + 256), r("si", 0, 256))
-    cp(r("plcf"), r("plci"))
-    ts(c("pint", 1), c("pint", 0), 15, A.bitwise_and)
-    cp(K(P), c("pint", 0))
-    ts(r("junk", 0, 112), r("plcf"), float(V), A.is_ge)
-    ts(r("junk", 112, 224), r("plcf"), float(2 * V), A.is_ge)
-    cp(K(AK), c("pint", 1))
-    cp(r("prmf", 0, 2, p=(0, 8)), r("prm", 0, 2, p=(0, 8)))
     cp(r("prmf", 2, 5, p=(0, 8)), r("prm", 4, 7, p=(0, 8)))
+    cp(r("prmf", 0, 2, p=(0, 8)), r("prm", 0, 2, p=(0, 8)))
+    ts(r("junk", 0, 112), r("plci"), float(V), A.is_ge)
+    ts(r("junk", 112, 224), r("plci"), float(2 * V), A.is_ge)
     red(c("cnt", 0), r("junk", 0, 112))
     red(c("cnt", 6), r("junk", 112, 224))
-    ts(K(G16), K(P), K(AK), A.subtract)
-    ts(K(G15), K(P), K(AK), A.subtract, 15.0, A.add)
-    ts(K(P16), K(P), 16.0, A.mult)
-    for k, v, f in ((K0, 0, A.is_equal), (K1, 1, A.is_equal), (K01, 1, A.is_le), (K02, 2, A.is_le), (K3, 3, A.is_equal), (K4, 4, A.is_equal), (K5, 5, A.is_equal),
-                    (K6, 6, A.is_equal), (G7, 7, A.is_ge)):
-        ts(K(k), K(AK), float(v), f)
     ts(c("cnt", 4), c("cnt", 0), -1.0, A.mult, 112.0, A.add)
     ts(c("cnt", 5), c("cnt", 0), c("cnt", 6), A.subtract)
-    ts(r("bdf"), r("xg"), K(G16), A.is_equal)
-    ts(r("e8", p=(0, 8)), r("xg", p=(0, 8)), r("col", P16, P16 + 1, p=(0, 8)), A.is_equal)
-    ts(r("jl"), r("si", 0, 512, 16), K(AK), A.add)
-    mm(r("pC", 0, 3), r("bdf"), r("cnt", 4, 7))
-    mm(r("pC", 4, 9), r("e8", p=(0, 8)), r("prmf", 0, 5, p=(0, 8)))
+    lazy[0] = True
+    cp(r("plcf"), r("plci"))
     ts(K(K12), K(K02), K(K0), A.subtract)
-    ts(K(X9), K(K1), -256.0, A.mult)
-    ts(K(JB), K(K0), 4000.0, A.mult, K(X9), A.add)
-    ts(c("oc", 0), K(AK), 3.0, A.is_le)
-    ts(c("oc", 2), K(AK), 8.0, A.is_ge)
-    ts(K(X6), c("oc", 0), c("oc", 2), A.add)
-    ts(c("oc", 1), K(X6), -1.0, A.mult, 1.0, A.add)
-    ts(K(CL), c("oc", 2), 2.0, A.mult, c("oc", 1), A.add)
-    ts(K(QM), c("oc", 2), 1.0, A.add)
-    ts(K(QQ), K(QM), 64.0, A.mult)
-    ts(K(QR), c("oc", 2), -0.5, A.mult, 1.0, A.add)
-    ts(K(Q13), K(QM), 13.0, A.mult)
+    ts(K(JB), K(K0), 4000.0, A.mult, K(K1), A.add)
+    ts(r("jl"), r("si", 0, 512, 16), K(AK), A.add)
+    ts(K(G15), K(P), K(AK), A.subtract, 15.0, A.add)
+    ts(c("oc", 0), c("ge", 4), -1.0, A.mult, 1.0, A.add)
+    ts(c("oc", 1), c("ge", 4), c("ge", 8), A.subtract)
+    cp(c("oc", 2), c("ge", 8))
+    ts(K(CL), c("ge", 4), c("ge", 8), A.add)
+    ts(K(QM), c("ge", 8), 1.0, A.add)
+    ts(K(QQ), c("ge", 8), 64.0, A.mult, 64.0, A.add)
+    ts(K(QR), c("ge", 8), -0.5, A.mult, 1.0, A.add)
+    ts(K(Q13), c("ge", 8), 13.0, A.mult, 13.0, A.add)
     ts(K(BS), K(CL), float(V), A.mult, float(B0), A.add)
     ts(K(BD), K(CL), 64.0 - V, A.mult, 3.0 * V, A.add)
     ts(K(X7), K(CL), -4.0, A.mult, K(AK), A.add)
-    ts(K(X8), K(X7), 16.0, A.mult)
-    ts(r("u0"), r("si", 0, 16), K(X8), A.add, 64.0, A.mult)
-    cp(r("par", 0, 5), r("pC", 4, 9))
-    tt(r("sc", 4, 7), r("par", 2, 5), r("oc", 0, 3), A.mult)
+    ts(r("u0"), r("xu"), K(X7), A.add, 1024.0, A.mult)
+    lazy[0] = False
+    mm(r("pC", 4, 9), r("e8", p=(0, 8)), r("prmf", 0, 5, p=(0, 8)))
+    tt(r("sc", 4, 7), r("pC", 6, 9), r("oc", 0, 3), A.mult)
+    cp(r("par", 0, 2), r("pC", 4, 6))
     red(c("sc", 8), r("sc", 4, 7))
+    mm(r("pB", 0, 3), r("bdf"), r("cnt", 4, 7))
     for t in range(RO):
         ts(c("sc", 9 + t), c("sc", 8), 41.0 * t, A.add, K(QM), A.mult)
 
@@ -459,10 +508,9 @@ def rank_program(g, core, T, topo):
 
     def row(name, n, k):
         ts(r(name), r("si", 0, n), 0.0, A.mult, K(k), A.add)
-    draw(0, r("pC", 0, 3))
+    draw(0, r("pB", 0, 3))
     lazy[0] = True
-    ts(r("jt"), r("si", 0, 256), K(K1), A.mult, K(JB), A.add)
-    act(r("ds", 0, CAP), r("jt", 0, CAP))
+    act(r("ds", 0, CAP), r("si", 0, CAP), scale=0.0, bias=K(JB))
     act(r("mv0"), r("si", 0, 256), scale=0.0, bias=K(K0))
     act(r("mv1"), r("si", 0, 256), scale=0.0, bias=K(K1))
     act(r("m4"), r("si", 0, 512), scale=0.0, bias=K(K4))
@@ -470,15 +518,12 @@ def rank_program(g, core, T, topo):
     ms(r("mk2", O + GH, S1), 1024.0)
     ms(r("w", 0, O), 0.0)
     act(r("plt", 0, O), r("si", 0, O), scale=K(K0))
-    act(r("plt", S1, S1 + 512), r("si", 0, 512), scale=0.0)
-    ts(K(K2), K(K12), K(K1), A.subtract)
     ts(K(X10), K(K0), 0.5, A.mult)
     ts(K(X11), K(K0), K(K2), A.add)
     ts(K(WR), K(K2), 512.0, A.mult, K(K01), A.add)
     act(r("mks", S1, S1 + 512), r("si", 0, 512), scale=K(X10), bias=K(X11))
-    ms(r("rm7"), 1.0)
-    ms(r("rm7", 0, 224, 7), 0.0)
-    ms(r("selt", 0, 2048, 16), 0.0)
+    for b in range(4):
+        ms(r("selt", 512 * b, 512 * b + 512, 16), 0.0)
     ms(r("ones"), 1.0)
     ms(r("msg"), 0.0)
     ms(r("neg"), -1.0)
@@ -487,12 +532,9 @@ def rank_program(g, core, T, topo):
     ms(r("rm", 0, 192, 32), 0.0)
     ts(K(K78), K(AK), 8.0, A.is_le, K(G7), A.mult)
     ts(K(X0), K(K12), K(K78), A.add)
-    ts(K(K9), K(AK), 9.0, A.is_equal)
     ts(K(X12), K(K9), K(K3), A.add, K(K0), A.add)
     ts(K(RS), K(X0), SC, A.mult, K(X12), A.add)
-    ts(K(X13), K(K12), 2048 * SC - 6e4, A.mult, 6e4, A.add)
-    ts(K(X14), K(K3), 2048 - 6e4, A.mult, K(X13), A.add)
-    ts(K(MX), K(K78), SC - 6e4, A.mult, K(X14), A.add)
+    ts(K(X13), K(RS), K(K6), A.add, K(K9), A.subtract)
     ts(K(WH), K(K12), 1 / SC, A.mult, K(K3), A.add)
     ts(K(G9), K(G16), 9.0, A.add)
     ts(K(X1), K(AK), -2048 * SC, A.mult, K(K12), A.mult)
@@ -510,6 +552,7 @@ def rank_program(g, core, T, topo):
     diag("mh0", K(X15))
     ts(r("mh1"), r("si", 0, 128), K(G9), A.is_equal, K(WH), A.mult)
     tt(r("mh"), r("mh0"), r("mh1"), A.add)
+    diag("mb", K(X13))
     diag("i0", K(K0))
     ts(K(X4), K(K123), 1 / 4096, A.mult)
     ts(K(X5), K(K6), -B0 / 4096 / SC, A.mult, K(X4), A.add)
@@ -535,16 +578,17 @@ def rank_program(g, core, T, topo):
     ts(r("cl"), r("jl"), -1.0, A.mult, 511.0, A.add)
     for nme, n, v in (("d257", 16, 257), ("d1h", 32, 1024), ("d15", 32, 1536), ("d2k", 32, 2048)):
         ts(r(nme), r("jl", 0, n), float(v), A.add)
-    for b in range(4):
+    ts(r("id16"), r("si", 0, 112), 16.0, A.mult, float(O - B0), A.add)
+    ts(r("r0"), r("si", 0, 16), K(K0), A.mult, K(R0), A.add)
+    lazy[0] = False
+
+    def places(b):
         o = lambda a: r(("pS", "pE")[b % 2], 112 * a, 112 * a + 112)
         for a in range(4):
-            mm(o(a), r("selt", 128 * (4 * b + a), 128 * (4 * b + a) + 128), r("plcf"))
+            mm(o(a), r("i0"), r("id16"), True, False)
+            mm(o(a), r("selt", 128 * (4 * b + a), 128 * (4 * b + a) + 128), r("plcf"), False, True)
         for a in range(4):
-            act(r("plt", O + 4 * b + a, S1, 16), o(a), AF.Relu, scale=K(RS), bias=K(R0))
-    nd[0] += 1
-    op("y", lambda q, a, k: q.dma_start(T.plt[0:128:16, O:S1], T.si[0:128:16, O:S1]), [], {}, [r("si", O, S1)], [r("plt", O, S1, p=(0, 8))],
-       ("dma%d" % (nd[0] - 1), 16, True), "dma")
-    lazy[0] = False
+            act(r("plt", O + 4 * b + a, S1, 16), o(a), AF.Relu, scale=K(RS), bias=c("r0", 4 * b + a))
 
     for t in range(RO):
         final = t == RO - 1
@@ -555,9 +599,12 @@ def rank_program(g, core, T, topo):
         cp(r("dr", 0, 256), r("bag", off=r("posu")))
         tolist("pA", 0, "y0", "dr", 256)
         cp(r("tu", 0, 16), r("pA", 0, 16))
-        cp(r("nbm"), r("nbi", off=r("tu", 0, 16)))
+        for a, b in ((0, 6), (6, 16)) if CUTM else ((0, 16),):
+            cp(r("nbm", 16 * a, 16 * b), r("nbi", off=r("tu", a, b)))
         lazy[0] = True
-        tt(r("dj"), r("dr", 0, 256), r("jt"), A.min)
+        if not VIAW:
+            ts(r("dz"), r("dr", 0, 256), K(K0), A.mult, K(K1), A.add)
+            scan(r("dj"), r("mv1"), r("dz"), A.mult, A.add)
         lazy[0] = False
         ids = r("msg", MSG * t, MSG * t + 5)
         clamp = lambda o, i: ts(o, i, 188 - 15 / 32, A.max, 196 - 15 / 32, A.min)
@@ -568,9 +615,9 @@ def rank_program(g, core, T, topo):
             for i in range(16):
                 mm(o, r("i16"), r(rows, 16 * j0 + i, 16 * j1, 16), False, i == 15)
 
-        def moves(on, late=False):
+        def moves(on):
             for j0, j1, e in MOVES[t > 0]:
-                if e == on and late == (t == 0 and j1 == 256):
+                if e == on:
                     take(e, r("gm", 16 * j0, 16 * j1), wn(r("nbm", j0, j1)))
 
         def steps():
@@ -587,7 +634,8 @@ def rank_program(g, core, T, topo):
             yield
             cum(r("mks", 0, S1), mk(0, S1))
             yield
-            take(RANK, r("rk"), r("mks", off=r("tu")))
+            for h, e in enumerate(RANK):
+                take(e, r("rk", 256 * h, 256 * h + 256), r("mks", off=r("tu", 16 * h, 16 * h + 16)))
             tolist("pG", 0, "yrk", "rk", 512)
             act(r("rec"), r("plt", off=r("tu")))
             ts(r("rku"), r("pG", 0, 32), -1.0, A.add)
@@ -598,7 +646,8 @@ def rank_program(g, core, T, topo):
             ts(r("sl16"), sl(), K(US), A.mult, K(MN), A.min)
             tolist("pA", 0, "y0", "sl16", 512)
             cp(r("su"), r("pA", 0, 32))
-            cp(r("nbu"), r("nbi", off=r("su")))
+            for a, b in ((0, CUTU), (CUTU, 32)) if CUTU else ((0, 32),):
+                cp(r("nbu", 16 * a, 16 * b), r("nbi", off=r("su", a, b)))
             yield
         asc = ascending()
 
@@ -609,8 +658,11 @@ def rank_program(g, core, T, topo):
                 if e == k:
                     cp(r("gm", 16 * j0, 16 * j1), wn(r("nbm", j0, j1)))
         act(r("oldm"), r("w", 0, S1, off=r("tu", 0, 16)), bias=-192.0)
-        if t > 0:
-            moves("s")
+        for b in range(EARLY if t == 0 else 0):
+            places(b)
+        moves("s")
+        for b in range(EARLY, 4 if t == 0 else 0):
+            places(b)
         sort(0)
         cp(mk(0, 2048, off=r("tu", 0, 16)), r("mv0"))
         cum(r("mk2", O, O + GH), mk(O, O + GH))
@@ -619,52 +671,48 @@ def rank_program(g, core, T, topo):
         sort(1)
         tt(r("t1"), r("pB", 0, 16), r("d257"), A.min)
         ts(r("dru"), r("t1"), -1.0, A.add)
-        cp(r("ds", off=r("dru")), r("dj"))
+        cp(r("ds", off=r("dru")), r("dr", 0, 256) if VIAW else r("dj"))
         cp(r("dsh"), r("ds", 0, CAP))
         sort(2)
         lazy[0] = True
         if not final:
-            act(r("ds", 0, CAP), r("jt", 0, CAP))
+            act(r("ds", 0, CAP), r("si", 0, CAP), scale=0.0, bias=K(JB))
         lazy[0] = False
-        if t > 0:
-            tolist("pD", 0, "y1", "dsh", CAP)
-            ts(r("ju", 0, 5), r("pD", 0, 5), 256.0, A.add)
-            cp(r("osel"), r("oldm", off=r("ju", 0, 5)))
         vals = r("msg", MSG * t + 8, MSG * t + 8 + CAP)
-        if t > 0:
-            moves("v")
-            steps()
-            tt(vals, r("rr", off=r("ju", 0, 5)), r("osel"), A.add)
+        if not VIAW:
+            tolist("pD", 0, "y1", "dsh", CAP)
+            ts(r("ju", 0, 5), r("pD", 0, 5), -1.0, A.add)
+            if NEW:
+                moves("v")
+                steps()
+                tt(r("nw"), r("rr"), r("oldm"), A.add)
+                cp(vals, r("nw", off=r("ju", 0, 5)))
+            else:
+                cp(r("osel"), r("oldm", off=r("ju", 0, 5)))
+                moves("v")
+                steps()
+                tt(vals, r("rr", off=r("ju", 0, 5)), r("osel"), A.add)
         mm(r("pB", 32, 37), r("ih"), r("mo", 0, 5), True, False)
         tolist("pB", 32, "y0", "dsh", CAP, first=False)
         tt(ids, r("pB", 32, 37), r("d15", 0, 5), A.min)
         tt(r("msg", MSG * t + 8 + CAP, MSG * t + 13 + CAP), r("pB", 32, 37), r("d15", 0, 5), A.min)
-        if t > 0:
-            pass
-        else:
-            ts(r("ju", 0, 5), ids, float(O), A.add)
-            cp(r("nbc"), r("nbi", off=r("ju", 0, 5)))
-            act(r("osel"), r("w", 0, S1, off=r("ju", 0, 5)), bias=-192.0)
-            take("v", r("gb", 0, 8 * CAP), wn(r("nbc", 0, CAP // 2)))
-            take("s", r("gb", 8 * CAP, 16 * CAP), wn(r("nbc", CAP // 2, CAP)))
-            sums(r("pD", 0, CAP), "osel", "gb", 0, CAP)
-            clamp(r("rr", 0, CAP), r("pD", 0, CAP))
-            tt(vals, r("rr", 0, CAP), r("osel"), A.add)
+        if VIAW:
+            cp(r("ju", 0, 5), ids)
+            moves("v")
+            steps()
+            tt(r("w", 0, S1, off=r("tu", 0, 16)), r("rr"), r("oldm"), A.add)
+            cp(vals, r("w", O, S1, off=r("ju", 0, 5)))
         at = lambda s: (MSG - 8) * (3 * t + s)
         exchange(t, lambda s: r("msg", MSG * t + 8 * (s == 1), MSG * t + MSG - 8 * (s != 1)), lambda d, s: r("land", at(s), at(s + 1)), "sent", total_e * (t + 1))
         if not final:
             iota(mk(2560, 2560 + S1), [[0, S1]], 0, 0, "post")
             iota(r("sl", 768 * t + 768, 768 * t + 1280), [[0, 512]], 0, 0, "post")
         sort(3)
-        if t == 0:
-            moves("s")
-            moves("v")
-            sort(4)
-            moves("s", True)
-            steps()
-        tt(r("w", 0, S1, off=r("tu", 0, 16)), r("rr"), r("oldm"), A.add)
-        if t > 0:
-            sort(4)
+        if NEW:
+            cp(r("w", 0, S1, off=r("tu", 0, 16)), r("nw"))
+        elif not VIAW:
+            tt(r("w", 0, S1, off=r("tu", 0, 16)), r("rr"), r("oldm"), A.add)
+        sort(4)
         sort(5)
         if final:
             dma(T.yx[:, :], r("w", O, S1))
@@ -674,14 +722,16 @@ def rank_program(g, core, T, topo):
         ts(r("gou", 0, 5), r("land", at(0), at(0) + 5), came[0], A.add)
         ts(r("gou", 5, 10), r("land", at(2) - 8, at(2) - 3), came[1], A.add)
         cp(r("w", S1, off=r("gou", 0, 10)), r("land", at(0) + 8, at(2) - 8))
-        act(r("sv"), r("w", 0, S1, off=r("su")))
-        mm(r("pS"), r("ipos"), r("sv"))
-        for j0, j1, e in CHUNKS:
+        for n, (j0, j1, e) in enumerate(CHUNKS):
+            if n == SV:
+                act(r("sv"), r("w", 0, S1, off=r("su")))
+                mm(r("pS"), r("ipos"), r("sv"))
             take(e, r("gb", 16 * j0, 16 * j1), wn(r("nbu", j0, j1)))
         cp(r("sf"), r("pA", 0, 32))
         lazy[0] = True
         if not final:
-            ts(r("slb"), sl(), K(MX), A.min)
+            mm(r("pG"), r("mb"), r("sl16"))
+            act(r("slb"), r("pG"))
         lazy[0] = False
         z = lambda n, k, o=0: r(n, o + 32 * k, o + 32 * k + 32)
         tolist("pB", 0, "ycl", "sl16", 512)
@@ -709,10 +759,10 @@ def rank_program(g, core, T, topo):
                 tt(r("mx", 512 * i + j0, 512 * i + j1), r("gb", 16 * j0 + i, 16 * j1, 16), r("pS", j0, j1), A.max)
                 mm(o, r("bd2"), r("mx", 512 * i + j0, 512 * i + j1), False, i == 15)
         jl = CHUNKS[-1][0]
-        act(r("ge", 0, jl), r("pE", 0, jl), AF.Sign, bias=K(THB))
-        act(r("ge", jl, 512), r("pF", jl, 512), AF.Sign, bias=K(THB))
+        act(r("sg", 0, jl), r("pE", 0, jl), AF.Sign, bias=K(THB))
+        act(r("sg", jl, 512), r("pF", jl, 512), AF.Sign, bias=K(THB))
         mm(r("pA", 0, 32), r("ih"), r("v18"), True, False)
-        tolist("pA", 0, "y01b", "ge", 512, first=False)
+        tolist("pA", 0, "y01b", "sg", 512, first=False)
         for k in range(3):
             tt(z("fl", k, 96), r("pA", 0, 32), z("rq", k), A.is_equal)
         scan(r("s1", 96, 192), r("rm", 0, 96), r("fl", 96, 192), A.mult, A.add)
@@ -799,14 +849,15 @@ def rank_program(g, core, T, topo):
             for h in range(4):
                 ts(r("plf", O + 448 * h, O + 448 * h + 448), r("plt", O + 448 * h, O + 448 * h + 448), K(MG), A.add, MAGIC, A.subtract)
             lazy[0] = False
+            tails()
             records()
             holes()
-            act(r("hf"), w4(1024, 1536, off=r("ixu")), bias=K(MG))
-            tails()
+            act(r("slb"), w4(1024, 1536, off=r("ixu")), bias=K(MG))
+            act(r("hf"), r("slb"), bias=-MAGIC)
             leavers()
             stayers()
             cp(r("plf", off=r("lvu")), r("nrec"))
-            ts(r("plf", off=r("stu")), r("hf"), 1.0, A.mult, -MAGIC, A.add)
+            cp(r("plf", off=r("stu")), r("hf"))
             op("y", lambda q, a, k: q.dma_start(T.yp[:, :], T.plf[9:128:16, O:S1]), [], {}, [r("plf", p=(0, 8))], [], ("dma%d" % nd[0], 16, True), "dma")
         else:
             cp(r("jou"), z("npl", 2))

@@ -5,19 +5,33 @@ V, GH, CAP, RO, N = 1792, 512, 80, 3, 4
 W = V + (N - 1) * GH
 O = 256
 S1 = O + V
-B0 = 512
+WS = O + W
+B0 = 544
 PL = B0 + 3 * V
-MSG = 96
+PT = 544
+NB = 576
+BIG = 65536.0
 MAGIC = 12582912.0
 SC = 16.0
 F, B, H, I, U = "float32", "bfloat16", "float16", "int32", "uint16"
-MOVES = (((0, 80, "s"), (80, 144, "s"), (144, 208, "s"), (208, 256, "v")), ((0, 80, "s"), (120, 192, "s"), (192, 256, "s"), (80, 104, 0), (104, 120, 1)))
-SORT = ((1, 1, 1, 1, 1, 1), (1, 1, 1, 1, 1, 1))
-RANK, EARLY, VIAW, NEW = "vs", 4, False, False
-CUTM, CUTU, SV, PRE = 1, 4, 1, 1
-SUMS = (((0, 80), (80, 144), (144, 256)), ((0, 120), (120, 192), (192, 256)))
-CHUNKS = ((0, 64, "s"), (64, 160, "v"), (160, 288, "s"), (288, 384, "s"), (384, 448, "s"), (448, 512, "s"))
-FILL = (3328, 4608)
+MOVES = (((0, 64, "s"), (64, 128, "v"), (128, 192, "s"), (192, 256, "v")),
+         ((0, 64, "s"), (64, 96, "v"), (96, 160, "s"), (160, 208, "v"), (208, 256, "s")))
+SUMS = tuple(tuple((a, b) for a, b, e in m) for m in MOVES)
+CHUNKS = ((0, 80, "s"), (80, 192, "v"), (192, 320, "s"), (320, 384, "s"), (384, 448, "s"), (448, 512, "s"))
+RANK, CUTM, CUTU, SELV = "vs", 6, 6, 2
+ENG = {"ri": "s", "jou": "s", "sv": "s", "rkd": "v"}
+QUEUES = {
+    "s": ["-si -bag -bag@ plt gm#1 gm#0 oldm -mks rec#0 junk rk rec#1 sl@ sv tb gb ri sg tg nl@ bag@ nrec plt@#0 hf",
+          "oldm gm -plt@#1 rk rec junk sl@ sv tb gb ri sg tg nl@ bag@ nrec plt@#0 hf",
+          "oldm gm -plt@#1 rk rec#0 junk rec#1 sl@ tb sv gb#0 gb#3 gb ri sg tg nl@ nrec"],
+    "v": ["dr#0 -mk mk@#0 nbm mk2 rkd gm#0 tu#1 gm#1 mk@#1 t1 mks pu rr rk pub@ rku sl16 -mkp w@ tpu su tbh nbu#1 nbu#0 gb"
+          " mx#0:64 tbu mx riu tg itu ihu occ bag@",
+          "dr#0 nbm mk@#0 mk2 gm#0 tu#1 rkd gm#1 mk@#1 t1 mks pu rr rk pub@ rku sl16 w@ tpu su tbh nbu gb"
+          " mx#0:80 tbu mx riu tg itu ihu occ bag@",
+          "dr#0 nbm mk@#0 mk2 gm#1 tu#1 rkd mk@#1 gm#0 mks t1 rr pu rk pub@ plf#0 rku plf#3 w@ plf#2 sl16 su tpu plf#1 nbu#0 tbh"
+          " nbu#1 slr gb tbu mx#0:16 mx#64:80 mx riu tg itu ihu occ plf@"],
+    "g": ["-si#0 -xg -pint -si#1 -selt -nbi -sl -plt", "", ""],
+}
 
 
 def _sb(c, d):
@@ -25,32 +39,34 @@ def _sb(c, d):
 
 
 BUF = {
-    "w": _sb(4688, B), "nbi": _sb(2048, I), "bag": _sb(6144, F), "plt": _sb(2560, F), "plf": _sb(2560, F), "si": _sb(2048, F),
-    "mk": _sb(3 * 2560, B), "mks": _sb(2560, B), "mk2": _sb(2048, B), "w4": _sb(1536, F), "sl": _sb(3 * 768, F), "sl16": _sb(512, H),
-    "slb": _sb(512, F), "dj": _sb(256, H), "dz": _sb(256, H), "nw": _sb(256, B), "yrk": _sb(144, B), "mh0": _sb(128, F), "mh1": _sb(128, F), "mh": _sb(128, H), "id16": _sb(112, H), "r0": _sb(16, F), "mb": _sb(128, H), "i0": _sb(128, H),
-    "rm7": _sb(224, F), "pn": _sb(96, F), "zn": _sb(96, F), "xh": _sb(96, H), "d1h": _sb(32, H), "o7": _sb(224, F),
-    "gb": _sb(8192, B), "gm": _sb(4096, B), "mx": _sb(8192, B), "selt": _sb(2048, F), "xg": _sb(128, F),
-    "plci": _sb(112, I), "plcf": _sb(112, F), "plcu": _sb(112, U), "junk": _sb(224, F),
-    "prm": _sb(16, I), "prmf": _sb(8, F), "par": _sb(8, F), "col": _sb(64, F), "pint": _sb(8, I),
-    "y0": _sb(144, H), "y1": _sb(144, H), "y123": _sb(144, H), "y45": _sb(144, H), "y01b": _sb(144, B), "y0b": _sb(144, B),
-    "ycl": _sb(144, H), "ypos": _sb(144, H),
-    "bdf": _sb(128, F), "bdh": _sb(128, H), "bdn": _sb(128, H), "bd2": _sb(128, B), "bdm": _sb(128, B), "bd16": _sb(128, B),
-    "i16": _sb(128, B), "ineg": _sb(128, B), "ipos": _sb(128, B), "ibias": _sb(128, B), "ih": _sb(128, H), "um": _sb(128, H), "ub": _sb(128, H),
-    "e8": _sb(128, F), "d48": _sb(128, F), "tri": _sb(128, F), "ones": _sb(256, B), "m4": _sb(512, B), "jt": _sb(256, F), "mv0": _sb(256, B), "mv1": _sb(256, B),
-    "rm": _sb(192, H), "neg": _sb(96, H),
-    "jl": _sb(32, F), "cl": _sb(32, H), "u0": _sb(16, F), "djc": _sb(16, F), "d2k": _sb(32, F), "d15": _sb(32, F), "d1k": _sb(32, F),
-    "mo": _sb(8, H), "d257": _sb(16, F), "oc": _sb(4, F), "eq": _sb(16, F), "le": _sb(16, F), "ge": _sb(16, F), "xu": _sb(16, F), "d81": _sb(128, F), "us": _sb(128, H), "uj": _sb(128, H), "ujn": _sb(128, H),
-    "ns": _sb(4, F), "cnt": _sb(8, F), "sc": _sb(16, F), "bi": _sb(4, I), "bm": _sb(4, I), "bf": _sb(4, F), "iv": _sb(16, I),
-    "pr": _sb(16, I), "ps": _sb(16, I), "pm": _sb(16, F), "posu": _sb(16, U),
+    "w": _sb(4 * WS, B), "pub": _sb(4096, B), "nbi": _sb(2048, I), "bag": _sb(PL + 256, F), "plt": _sb(3072, F), "plf": _sb(3072, F),
+    "si": _sb(2048, F), "mk": _sb(2 * 2560, B), "mkp": _sb(512, B), "mks": _sb(2560, B), "mk2": _sb(GH, B), "tuc": _sb(16, U), "bd0": _sb(128, B), "nl": _sb(512 + 4544, F),
+    "sl": _sb(2 * 768, F), "sl16": _sb(512, H), "slr": _sb(512, F),
+    "gb": _sb(8192, B), "gm": _sb(4096, B), "mx": _sb(8192, B), "selt": _sb(2048, B), "nz": _sb(512, B), "xg": _sb(128, F),
+    "plci": _sb(112, I), "plcj": _sb(224, I), "plch": _sb(224, H), "plcu": _sb(112, U), "junk": _sb(256, F),
+    "acc": _sb(4, F), "cf": _sb(4, F), "uq": _sb(4, H), "pq": _sb(32, F), "posl": _sb(32, H), "id16": _sb(112, H), "r0": _sb(16, F),
+    "prm": _sb(16, I), "prmf": _sb(8, F), "par": _sb(8, F), "col": _sb(80, F), "pint": _sb(8, I),
+    "yb": _sb(144, B), "y0": _sb(144, B), "y123": _sb(144, B), "y01": _sb(144, B), "yrk": _sb(144, B),
+    "ycl": _sb(144, B), "ypos": _sb(144, B), "ynl": _sb(144, B),
+    "bd": _sb(128, B), "bdn": _sb(128, B), "bd2": _sb(128, B), "bd16": _sb(128, B), "msk": _sb(128, B), "mcl": _sb(128, B),
+    "i16": _sb(128, B), "ineg": _sb(128, B), "ibias": _sb(128, B), "ih": _sb(128, B),
+    "i0": _sb(128, B), "i8k": _sb(128, B), "ic": _sb(384, B), "mh0": _sb(128, B),
+    "e8": _sb(128, F), "us": _sb(128, B), "usn": _sb(128, B), "ones": _sb(256, B), "mv0": _sb(256, B), "mv1": _sb(256, B),
+    "rm": _sb(96, B), "rm4": _sb(128, B),
+    "jl": _sb(48, F), "c16": _sb(48, F), "dl": _sb(48, H), "u0": _sb(16, F), "d2k": _sb(32, F),
+    "oc": _sb(4, F), "eq": _sb(16, F), "le": _sb(16, F), "ge": _sb(16, F), "xu": _sb(16, F),
+    "ns": _sb(4, F), "cnt": _sb(8, H), "cnf": _sb(8, F), "sc": _sb(16, F), "bi": _sb(4, I), "bm": _sb(4, I), "bf": _sb(4, F),
+    "pr": _sb(16, I), "ps": _sb(16, I), "posu": _sb(16, U),
     "dr": _sb(512, H), "rec": _sb(512, F), "tu": _sb(32, U), "nbm": _sb(256, U), "nbu": _sb(512, U),
-    "t1": _sb(16, F), "oldm": _sb(256, B), "rr": _sb(256, B), "rkd": _sb(256, B), "rk": _sb(512, B), "dru": _sb(16, U), "rku": _sb(32, U),
-    "ds": _sb(512, F), "dsh": _sb(80, H), "ju": _sb(6, U), "nbc": _sb(CAP, U), "osel": _sb(80, B), "msg": _sb(3 * MSG, H), "land": _sb(9 * 88, H), "gou": _sb(24, U),
-    "su": _sb(32, U), "sf": _sb(32, F), "sv": _sb(512, B), "sg": _sb(512, B),
-    "ne": _sb(96, H), "rq": _sb(96, F), "pp": _sb(96, F), "v18": _sb(32, H), "sa": _sb(96, F), "sb": _sb(96, F), "nq": _sb(8, F), "nqh": _sb(8, H),
-    "fl": _sb(192, H), "jn": _sb(96, H), "s1": _sb(192, H), "s2": _sb(96, H), "zz": _sb(96, F), "ho": _sb(96, H), "hs": _sb(96, H), "xx": _sb(192, F),
-    "o4": _sb(96, F), "o4u": _sb(32, U), "vv": _sb(96, F), "ww": _sb(96, F), "npl": _sb(96, F), "lv": _sb(96, F), "jou": _sb(32, U), "lvu": _sb(32, U),
-    "yy": _sb(288, F), "tpu": _sb(32, U), "tb": _sb(512, H), "ts4": _sb(512, H), "ixu": _sb(32, U), "hg": _sb(512, H), "hf": _sb(512, F),
-    "hou": _sb(32, U), "nrec": _sb(512, F), "st": _sb(96, F), "stu": _sb(32, U), "lg": _sb(16, F),
+    "t1": _sb(32, F), "oldm": _sb(256, B), "rr": _sb(256, B), "rkd": _sb(256, B), "rk": _sb(512, B), "pu": _sb(16, U), "rku": _sb(32, U),
+    "su": _sb(32, U), "sf": _sb(64, F), "sv": _sb(512, B), "sg": _sb(528, B),
+    "ne": _sb(96, H), "rq": _sb(192, F), "pp": _sb(96, F), "v18": _sb(32, H), "sa": _sb(96, H), "nq": _sb(8, F), "nqh": _sb(8, H),
+    "ai": _sb(4, I), "af": _sb(16, F), "tq": _sb(240, F), "bb": _sb(96, H), "rx": _sb(144, F), "tpu": _sb(48, U),
+    "tb": _sb(PT, F), "tbh": _sb(PT, H), "d1h": _sb(32, H),
+    "tbu": _sb(48, U), "ri": _sb(PT, B), "riu": _sb(48, U), "tg": _sb(PT, B), "tx": _sb(144, H), "itu": _sb(48, U),
+    "fl": _sb(192, H), "s1": _sb(192, H), "zz": _sb(96, F), "ho": _sb(96, H), "hs": _sb(96, H), "o3": _sb(128, F), "ihu": _sb(32, U),
+    "vv": _sb(128, F), "o4": _sb(128, F), "lv": _sb(96, F), "jou": _sb(32, U), "lvu": _sb(32, U), "hv": _sb(96, F), "hou": _sb(32, U),
+    "occ": _sb(512, H), "hf": _sb(512, F), "nrec": _sb(512, F), "stu": _sb(32, U), "lg": _sb(16, F),
     "pS": ("psum", [128, 512], F), "pE": ("psum", [128, 512], F), "pF": ("psum", [128, 512], F), "pG": ("psum", [128, 512], F),
     "pA": ("psum", [128, 512], F), "pB": ("psum", [128, 512], F), "pC": ("psum", [128, 512], F), "pD": ("psum", [128, 512], F),
 }
@@ -64,8 +80,8 @@ for _n, (_w, _s, _d) in BUF.items():
     else:
         PLACE[_n] = (_n, 0)
         SCRATCH[_n] = (_w, _s, _d)
-DMAS = 12
-SEMAPHORES = ["cv", "cs", "ct", "cg", "sent0", "sent"] + ["near%d" % k for k in range(4)] + ["far%d" % k for k in range(4)] + ["dma%d" % k for k in range(DMAS)]
+DMAS = 16
+SEMAPHORES = ["cv", "cs", "ct", "cg", "sent0", "sent"] + ["came%d" % k for k in range(4)] + ["dma%d" % k for k in range(DMAS)]
 
 
 def r(name, c0=0, c1=None, step=1, p=(0, 128), off=None):
@@ -99,45 +115,45 @@ def depend(ops, banks):
             psum = SCRATCH[a[1]][0] == "psum"
             for j, b, bw in acc.get(a[1], []):
                 e = ops[j]["q"]
-                if not meet(a, b) or (e == "t" and o["q"] == "t" and not banks):
+                if not meet(a, b) or (e == "t" and o["q"] == "t" and (not banks or o["kind"] == ops[j]["kind"] == "free")):
                     continue
                 if wr or bw or (psum and e != o["q"]):
                     d.add(j)
         for a, wr in both:
             l = acc.setdefault(a[1], [])
-            if wr and a[4] == 1 and a[6] is None and a[5] == (0, 128):
+            if wr and SCRATCH[a[1]][0] == "psum":
+                if o["kind"] != "free" or not banks:
+                    l[:] = [x for x in l if x[0] == k]
+            elif wr and a[4] == 1 and a[6] is None and a[5] == (0, 128):
                 l[:] = [x for x in l if x[0] == k or not (a[2] <= x[1][2] and x[1][3] <= a[3])]
             l.append((k, a, wr))
         deps.append(d)
     return deps
 
 
-CY, WAKE, GATHER, SCATTER, SEND = 0.83, 200.0, 1.5, 2.5, 2000.0
-
-
-PASSES, SAME, TRIES = 2, 200.0, 200
+CY, WAKE, GATHER, SCATTER, SEND = 0.9, 200.0, 1.4, 2.8, 2000.0
 
 
 def cost(q, kind, args, rd, wr):
     two = lambda a: SCRATCH[a[1]][2] in (B, H, U)
     if kind == "send":
-        x = SEND if width(rd[0]) == GH else 0.0
+        x = SEND if rd[0][1] == "w" else 0.0
         return 900.0 + x, SEND + x + 640 + 4.3 * width(rd[0])
     if kind == "land":
         return 0.0, 0.0
     if kind == "dma":
         a = (wr + rd)[0]
         x = width(a) * (2 if two(a) else 4) * 0.45 * (a[5][1] - a[5][0]) / 128
-        return 100 + x, 1500 + x
+        return 100 + (x if q == "y" else 0), 1500 + x
     n = width(args[1] if kind == "red" else wr[0])
     if q == "t":
-        x = max(64, n) * 0.42 * (1 if two(args[2]) else 4)
+        x = max(64, n) * CY / 2 * (1 if two(args[2]) else 4)
     elif q == "g":
         x = 150 + 2 * CY * n
     elif wr[0][6] is not None:
-        x = 60 + (SCATTER + {"tt": 2, "ts": 1}.get(kind, 0)) * CY * n
+        x = 60 + SCATTER * CY * n
     elif any(a[6] is not None for a in rd):
-        x = 60 + (GATHER + {"tt": 2, "ts": 1}.get(kind, 0)) * CY * n
+        x = 60 + GATHER * CY * n
     elif q == "s":
         x = 65 + CY * n + (1300 if kind == "table" else 0)
     elif kind == "tt":
@@ -148,109 +164,74 @@ def cost(q, kind, args, rd, wr):
 
 
 def schedule(ops):
-    deps = depend(ops, True)
-    last = {}
-    for k, o in enumerate(ops):
-        if o["kind"] in ("send", "land", "post") and "send" in last:
-            deps[k].add(last["send"])
-        if o["kind"] == "dma" and "dma" in last:
-            deps[k].add(last["dma"])
-        last[o["kind"]] = k
-
-    def lat(j, k):
-        if ops[j]["kind"] == ops[k]["kind"] == "dma" or ops[k]["kind"] == "post" and ops[j]["kind"] == "send":
-            return ops[j]["cost"][0] - ops[j]["cost"][1]
-        if ops[k]["kind"] == "land":
-            return -500.0 if ops[k]["ev"][0][0] == "n" else 0.0
-        return WAKE if ops[j]["q"] != ops[k]["q"] else 0.0 if ops[k]["q"] == "t" else SAME
     n = len(ops)
-    succ = [[] for _ in ops]
-    for k in range(n):
-        for j in deps[k]:
-            succ[j].append(k)
-
-    def place(order, before, back):
-        busy = {q: ([], []) for q in "vstgye"}
-        start = [0.0] * n
-        end = [0.0] * n
-        for k in order:
-            hold, total = ops[k]["cost"]
-            pre = total - hold if back else 0.0
-            t = max([end[j] + lat(j, k) for j in before[k]] + [0.0]) + pre
-            a, b = busy[ops[k]["q"]]
-            lo, hi = 0, len(b)
-            while lo < hi:
-                if b[(lo + hi) // 2] <= t:
-                    lo = (lo + hi) // 2 + 1
-                else:
-                    hi = (lo + hi) // 2
-            while lo < len(a) and t + hold > a[lo]:
-                t = max(t, b[lo])
-                lo += 1
-            a.insert(lo, t)
-            b.insert(lo, t + hold)
-            start[k], end[k] = t - pre, t - pre + total
-        return start, end
+    before = [{} for _ in ops]
+    last = {}
+    rounds = [{}]
+    for k, (o, d) in enumerate(zip(ops, depend(ops, True))):
+        for j in d:
+            before[k][j] = ops[j]["cost"][1] + (0.0 if o["q"] == ops[j]["q"] == "t" else WAKE)
+        if o["kind"] in ("send", "land", "post") and "send" in last:
+            j = last["send"]
+            before[k][j] = max(before[k].get(j, 0.0), ops[j]["cost"][o["kind"] == "land"])
+        if o["kind"] == "dma" and o["q"] in last:
+            j = last[o["q"]]
+            before[k][j] = max(before[k].get(j, 0.0), ops[j]["cost"][0])
+        last[o["q"] if o["kind"] == "dma" else o["kind"]] = k
+        if o["wr"] and o["kind"] != "dma":
+            a = o["wr"][0]
+            name = max((at, x) for x, (b, at) in PLACE.items() if b == a[1] and at <= a[2])[1] + ("@" if a[6] else "")
+            if name == "dr" and o["rd"][0][6] is not None:
+                rounds.append({})
+            rounds[-1].setdefault(o["q"] + name, []).append(k)
+    for q, lists in QUEUES.items():
+        chain = []
+        for t, names in enumerate(lists):
+            for x in names.split():
+                name, _, part = x.lstrip("-").partition("#")
+                calls = rounds[t + (x[0] != "-")].get(q + name, [])
+                if part:
+                    a, _, b = part.partition(":")
+                    calls = calls[int(a):int(b) if b else int(a) + 1]
+                chain += [k for k in calls if k not in chain]
+        for j, k in zip(chain, chain[1:]):
+            before[k][j] = max(before[k].get(j, 0.0), ops[j]["cost"][0])
     order = []
-    seen = [False] * n
-
-    def visit(k):
-        if not seen[k]:
-            seen[k] = True
-            for j in sorted(deps[k]):
-                visit(j)
-            order.append(k)
-    for late in (False, True):
-        for k in range(n):
-            if late or not ops[k]["lazy"]:
-                visit(k)
-    best = None
-    for _ in range(PASSES):
-        start, end = place(order, deps, False)
-        if best is None or max(end) < best[0]:
-            best = (max(end), start)
-        rank = place(sorted(range(n), key=lambda k: (-end[k], -k)), succ, True)[1]
-        order.clear()
-        seen[:] = [False] * n
-        for k in sorted(range(n), key=lambda k: (-rank[k], k)):
-            visit(k)
-    order = sorted(range(n), key=lambda k: (best[1][k], k))
-    start, end = place(order, deps, False)
-    tried = set()
-    for _ in range(TRIES):
-        ahead = {}
-        for q in "vstg":
-            l = sorted((k for k in range(n) if ops[k]["q"] == q), key=lambda k: start[k])
-            ahead.update(zip(l[1:], l))
-        k = max(range(n), key=lambda k: end[k])
-        pairs = []
-        while start[k] > 0:
-            j = max(deps[k], key=lambda j: end[j] + lat(j, k), default=None)
-            if j is None or end[j] + lat(j, k) < start[k] - 1:
-                j = ahead.get(k)
-                if j is None:
-                    break
-                if j not in deps[k] and (j, k) not in tried and ops[k]["q"] != "t":
-                    pairs.append((j, k))
-            k = j
-        if not pairs:
-            break
-        j, k = max(pairs, key=lambda x: ops[x[0]]["cost"][0])
-        tried.add((j, k))
-        later = {j}
-        a, b = order.index(j), order.index(k)
-        if a > b:
-            continue
-        for x in order[a:b]:
-            if deps[x] & later:
-                later.add(x)
-        if deps[k] & later:
-            continue
-        new = order[:a] + [x for x in order[a:b + 1] if x not in later] + [x for x in order[a:b] if x in later] + order[b + 1:]
-        s2, e2 = place(new, deps, False)
-        if max(e2) <= max(end):
-            order, start, end = new, s2, e2
-    return sorted(range(n), key=lambda k: (start[k], k))
+    waiting = [len(b) for b in before]
+    after = [[] for _ in ops]
+    for k in range(n):
+        for j in before[k]:
+            after[j].append(k)
+    order = [k for k in range(n) if not waiting[k]]
+    for j in order:
+        for k in after[j]:
+            waiting[k] -= 1
+            if not waiting[k]:
+                order.append(k)
+    left = [o["cost"][1] for o in ops]
+    for k in reversed(order):
+        for j, x in before[k].items():
+            left[j] = max(left[j], x + left[k])
+    pos = {k: i for i, k in enumerate(order)}
+    busy = {q: ([], []) for q in "vstgye"}
+    start = [0.0] * n
+    for k in sorted(range(n), key=lambda k: (-left[k], pos[k])):
+        hold = ops[k]["cost"][0]
+        t = max([start[j] + x for j, x in before[k].items()] + [0.0])
+        a, b = busy[ops[k]["q"]]
+        lo, hi = 0, len(b)
+        while lo < hi:
+            if b[(lo + hi) // 2] <= t:
+                lo = (lo + hi) // 2 + 1
+            else:
+                hi = (lo + hi) // 2
+        while lo < len(a) and t + hold > a[lo]:
+            t = max(t, b[lo])
+            lo += 1
+        a.insert(lo, t)
+        b.insert(lo, t + hold)
+        start[k] = t
+    return sorted(range(n), key=lambda k: (start[k], pos[k]))
 
 
 ORDERS = {}
@@ -310,13 +291,12 @@ def rank_program(g, core, T, topo):
     if rank is None:
         return
     ops = []
-    lazy = [False]
 
     def op(q, fn, args, kw, rd, wr, ev=None, kind=None):
         rd = [a for a in rd if is_ref(a)]
         x = cost(q, kind, args, rd, wr)
         rd += [a[6] for a in rd + wr if a[6] is not None]
-        ops.append({"q": q, "fn": fn, "args": args, "kw": kw, "rd": rd, "wr": wr, "ev": ev, "kind": kind, "cost": x, "lazy": lazy[0]})
+        ops.append({"q": q, "fn": fn, "args": args, "kw": kw, "rd": rd, "wr": wr, "ev": ev, "kind": kind, "cost": x})
 
     def ts(o, i, s1, o1, s2=None, o2=None):
         if o2 is None:
@@ -343,30 +323,35 @@ def rank_program(g, core, T, topo):
         scan(o, d, d, A.add, A.max)
 
     def act(o, i, f=AF.Identity, **kw):
-        op("s", lambda q, a, k: q.activation(a[0], a[1], f, **k), [o, i], kw, [i, kw.get("bias"), kw.get("scale")], [o],
-           kind="table" if f == AF.Silu and o[6] is None else None)
+        op("s", lambda q, a, k: q.activation(a[0], a[1], f, **k), [o, i], kw, [i, kw.get("bias"), kw.get("scale")],
+           [o] + ([kw["accum_out"]] if "accum_out" in kw else []), kind="table" if f == AF.Silu and o[6] is None else None)
+
+    def lin(o, i, scale=1.0, bias=0.0):
+        act(o, i, scale=scale, bias=bias)
 
     def take(e, o, i):
         (cp if e == "v" else act)(o, i)
 
     def mm(o, l, x, st=True, sp=True):
-        op("t", lambda q, a, k: q.matmul(a[0], a[1], a[2], st, sp), [o, l, x], {}, [l, x], [o])
+        op("t", lambda q, a, k: q.matmul(a[0], a[1], a[2], st, sp), [o, l, x], {}, [l, x], [o], kind=None if st or sp else "free")
 
-    def iota(o, pat, base, cm, kind=None):
+    def iota(o, pat, base, cm, kind="post"):
         fl = {"allow_small_or_imprecise_dtypes": True} if SCRATCH[o[1]][2] != I else {}
         op("g", lambda q, a, k: q.iota(a[0], pat, base, cm, **fl), [o], {}, [], [o], kind=kind)
+
+    def keep(o, i, pat, how, fill, base, cm):
+        op("g", lambda q, a, k: q.affine_select(a[0], a[1], pat, how, fill, base, cm), [o, i], {}, [i], [o], kind="post")
     nd = [0]
 
-    def dma(o, i):
+    def dma(o, i, q="y", after=None):
         nd[0] += 1
-        op("y", lambda e, a, k: e.dma_start(a[0], a[1]), [o, i], {}, [i], [o] if is_ref(o) else [], ("dma%d" % (nd[0] - 1), 16, True), "dma")
+        op(q, lambda e, a, k: e.dma_start(a[0], a[1]), [o, i], {}, [i, after], [o] if is_ref(o) else [], ("dma%d" % (nd[0] - 1), 16, True), "dma")
 
     def tolist(ps, c0, y, src, n, first=True, at=0):
         for a in range(16):
             mm(r(ps, c0, c0 + n // 16), r(y, 15 - a, 143 - a), r(src, at + a, at + n, 16), first and a == 0, a == 15)
 
     peers = [T.cores[(rank + d) % N] for d in range(1, N)]
-    srcs = [T.cores[(rank - d) % N] for d in range(1, N)]
     mine = topo.cores_of(core)
     far = [p for p in peers if p not in mine]
     far_e = topo.engines(core, far[0])
@@ -380,54 +365,53 @@ def rank_program(g, core, T, topo):
             near_n = len(near_e)
     total_e = near_n + share * len(far)
 
-    def slot(to, d):
-        away = [e for e in range(N - 1) if T.cores[(to - e - 1) % N] not in topo.cores_of(T.cores[to % N])]
-        return away.index(d) if d in away else len(away)
+    def w(t, a, b, **k):
+        return r("w", WS * t + a, WS * t + b, **k)
 
-    def exchange(k, src, dst, lsem, lval):
-        out = [src(slot(rank + d + 1, d)) for d in range(N - 1)]
-
+    def exchange(k, src, lsem, lval):
         def fn(q, a, kw):
             tr = []
             for d, p in enumerate(peers):
                 rid, pid = topo.addr(p, core)
                 tr.append(RemoteDMATransfer(dst_ids=[DstId(rid=rid, pnc=pid)], dma_engine_mask=masks[p],
-                                            remote_sem=T.sem[("near%d" if p in mine else "far%d") % k], src=a[d], dst=a[N - 1 + d]))
+                                            remote_sem=T.sem["came%d" % k], src=a[0], dst=a[1 + d]))
             return q.remote_dma_fused(tr, local_sem=T.sem[lsem])
-        op("g", fn, out + [dst(d, slot(rank + d + 1, d)) for d in range(N - 1)], {}, out, [], (lsem, lval, False), "send")
-        here = [dst(d, slot(rank, d)) for d in range(N - 1)]
-        op("e", lambda q, a, kw: None, [], {}, [], [here[d] for d in range(N - 1) if srcs[d] in mine], ("near%d" % k, near_n, False), "land")
-        op("e", lambda q, a, kw: None, [], {}, [], [here[d] for d in range(N - 1) if srcs[d] not in mine], ("far%d" % k, share * len(far), False), "land")
+        op("g", fn, [src] + [w(k, S1 + d * GH, S1 + (d + 1) * GH) for d in range(N - 1)], {}, [src], [], (lsem, lval, False), "send")
+        op("e", lambda q, a, kw: None, [], {}, [], [w(k, S1, WS)], ("came%d" % k, total_e, False), "land")
 
-    (P, AK, G15, G16, P16, K0, K1, K01, K02, K12, K4, K5, K45, K6, G7, K78, RS, RB, R0, RF, MN, US, WC, WP, TG, THB, JB, MG,
-     CL, QM, QQ, QR, Q13, BS, BD, X0, X1, X2, X3, X4, X5, X6, X7, X8, X9, K3, K123,
-     K2, K9, G9, WR, WH, MX, X10, X11, X12, X13, X14, X15) = range(59)
-    FLAG = {K0: ("eq", 0), K1: ("eq", 1), K2: ("eq", 2), K3: ("eq", 3), K4: ("eq", 4), K5: ("eq", 5), K6: ("eq", 6), K9: ("eq", 9),
-            K01: ("le", 1), K02: ("le", 2), G7: ("ge", 7)}
+    (P, AK, G15, G16, P16, K0, K1, K2, K3, K4, K5, K6, K7, K8, K9, K01, K02, K12, K23, K45, K26, K78, K123, RS, RB, R0, RF, RN, MN, US,
+     WC, WP, THB, MG, CL, QM, QQ, QR, Q13, BS, BD, KB, WN, MA, MB, MC,
+     X0, X1, X2, X3, X4, X5, X6, X7, X8, X9, X10, X11, X12, X13, X14, X15, X16, X17, X18, X19, X20, X21, X22) = range(69)
+    FLAG = {K0: ("eq", 0), K1: ("eq", 1), K2: ("eq", 2), K3: ("eq", 3), K4: ("eq", 4), K5: ("eq", 5), K6: ("eq", 6), K7: ("eq", 7),
+            K8: ("eq", 8), K9: ("eq", 9), K01: ("le", 1), K02: ("le", 2)}
     K = lambda k: c(*FLAG.get(k, ("col", k)))
 
-    dma(r("w", O, O + GH), T.x[:, 0:GH])
-    dma(r("plci"), T.plc[:, :])
-    dma(r("prm", 4, 7, p=(0, 8)), T.sd[:, :])
-    dma(r("prm", 0, 2, p=(0, 8)), T.th[:, :])
+    dma(w(0, O, O + GH), T.x[:, 0:GH])
+    ms(w(0, 0, O), 0.0)
+    dma(r("plci"), T.plc[:, :], "s")
+    dma(r("prm", 4, 7, p=(0, 8)), T.sd[:, :], "s")
+    dma(r("prm", 0, 2, p=(0, 8)), T.th[:, :], "s")
     dma(r("nbi", O, S1), T.nb[:, :])
-    dma(r("w", O + GH, S1), T.x[:, GH:V])
-    iota(r("si", 0, 256), [[1, 256]], 0, 0)
-    iota(c("pint", 0), [[0, 1]], 0, 1)
-    iota(r("xg"), [[16, 8], [0, 16]], 0, 0)
-    exchange(3, lambda s: r("w", O, O + GH), lambda d, s: r("w", S1 + d * GH, S1 + (d + 1) * GH), "sent0", total_e)
-    ms(c("bag", B0 + 2 * V - 1), 0.0)
-    ms(r("sl", 0, 512), 0.0)
-
-    def selectors(b):
-        o = r("selt", 512 * b, 512 * b + 512)
-        op("g", lambda q, a, k: q.affine_select(a[0], a[1], [[-1, 4], [-16, 8], [0, 16]], A.not_equal, 1.0, -4 * b, 1),
-           [o, r("sl", 0, 512)], {}, [r("sl", 0, 512)], [o], kind="post" if b >= PRE else None)
-    for b in range(4):
-        selectors(b)
-    iota(r("plt", S1, S1 + 512), [[0, 512]], 0, 0, "post")
-    iota(r("rm7"), [[0, 32], [1, 7]], 0, 0, "post")
-    op("g", lambda q, a, k: q.affine_select(a[0], a[0], [[0, 32], [1, 7]], A.is_equal, 1.0, 0, 0), [r("rm7")], {}, [r("rm7")], [r("rm7")], kind="post")
+    dma(w(0, O + GH, S1), T.x[:, GH:V])
+    iota(r("si", 0, 256), [[1, 256]], 0, 0, None)
+    iota(c("pint", 0), [[0, 1]], 0, 1, None)
+    iota(r("xg"), [[16, 8], [0, 16]], 0, 0, None)
+    iota(r("si", 1280, V), [[1, 512]], 1280, 0, None)
+    exchange(0, w(0, O, O + GH), "sent0", total_e)
+    dma(r("pub", O, O + GH), T.x[:, 0:GH], after=w(0, S1, WS))
+    dma(w(1, 0, S1), w(0, 0, S1))
+    ms(r("bag", B0 + 2 * V - PT, B0 + 2 * V), 0.0)
+    ms(r("bag", B0 - 16, B0), 0.0)
+    ms(r("bag", B0 + V - 16, B0 + V), 0.0)
+    ms(r("ones"), 1.0)
+    iota(r("nbi", 0, O), [[2, O]], V, 0)
+    if SELV < 4:
+        ms(r("nz"), 1.0)
+        ms(r("nz", 0, 512, 16), 0.0)
+    for b in range(SELV, 4):
+        keep(r("selt", 512 * b, 512 * b + 512), r("nz"), [[-1, 4], [-16, 8], [0, 16]], A.is_equal, 0.0, -4 * b, 1)
+    iota(r("plt", S1, S1 + 512), [[0, 512]], 0, 0)
+    iota(r("sl", 0, 512), [[0, 512]], 0, 0)
     act(r("si", V, 2048), r("si", 0, 256), AF.Silu, bias=float(V))
     ts(r("si", 256, 512), r("si", 0, 256), 256.0, A.add)
     ts(c("pint", 1), c("pint", 0), 15, A.bitwise_and)
@@ -440,15 +424,17 @@ def rank_program(g, core, T, topo):
     ts(r("ge"), r("si", 0, 16), K(AK), A.is_le)
     ts(K(G16), K(P), K(AK), A.subtract)
     ts(K(P16), K(P), 16.0, A.mult)
-    ts(r("si", 1280, V), r("si", 0, 512), 1280.0, A.add)
     ts(r("e8", p=(0, 8)), r("xg", p=(0, 8)), r("col", P16, P16 + 1, p=(0, 8)), A.is_equal)
-    ts(r("bdf"), r("xg"), K(G16), A.is_equal)
-    lazy[0] = True
+    ts(r("bd"), r("xg"), K(G16), A.is_equal)
+    if SELV:
+        cp(r("bd0"), r("bd"))
+        ms(r("bd0", 0, 128, 16), 0.0)
+    for a in range(4 * SELV):
+        ts(r("selt", 128 * a, 128 * a + 128), r("bd0"), c("eq", a), A.mult)
     ts(r("xu"), r("si", 0, 16), 1 / 16, A.mult)
-    for k in range(4):
-        ms(r("mk", 512 * k, 512 * k + 512), 0.0)
-    ts(r("nbi", 0, O), r("si", 0, O), 2.0, A.mult, float(V), A.add)
-    lazy[0] = False
+    ts(K(KB), K(K2), -1024.0, A.mult)
+    for o in [r("mk", 512 * k, 512 * k + 512) for k in range(4)] + [r("mkp")]:
+        ts(o, w(0, O, O + GH), 0.0, A.mult, K(KB), A.add)
     cp(r("plcu"), r("plci"))
     act(r("bag", B0, PL, off=r("plcu")), r("si", O, S1), AF.Silu)
     act(r("bag", PL, PL + 256), r("si", 0, 256))
@@ -456,15 +442,14 @@ def rank_program(g, core, T, topo):
     cp(r("prmf", 0, 2, p=(0, 8)), r("prm", 0, 2, p=(0, 8)))
     ts(r("junk", 0, 112), r("plci"), float(V), A.is_ge)
     ts(r("junk", 112, 224), r("plci"), float(2 * V), A.is_ge)
-    red(c("cnt", 0), r("junk", 0, 112))
-    red(c("cnt", 6), r("junk", 112, 224))
-    ts(c("cnt", 4), c("cnt", 0), -1.0, A.mult, 112.0, A.add)
-    ts(c("cnt", 5), c("cnt", 0), c("cnt", 6), A.subtract)
-    lazy[0] = True
-    cp(r("plcf"), r("plci"))
-    ts(K(K12), K(K02), K(K0), A.subtract)
-    ts(K(JB), K(K0), 4000.0, A.mult, K(K1), A.add)
-    ts(r("jl"), r("si", 0, 512, 16), K(AK), A.add)
+    red(c("cnf", 0), r("junk", 0, 112))
+    red(c("cnf", 1), r("junk", 112, 224))
+    ts(c("cnt", 0), c("cnf", 0), -1.0, A.mult, 112.0, A.add)
+    ts(c("cnt", 1), c("cnf", 0), c("cnf", 1), A.subtract)
+    cp(c("cnt", 2), c("cnf", 1))
+    for h, m in enumerate((8128, 63)):
+        ts(r("plcj", 112 * h, 112 * h + 112), r("plci"), m, A.bitwise_and)
+    cp(r("plch"), r("plcj"))
     ts(K(G15), K(P), K(AK), A.subtract, 15.0, A.add)
     ts(c("oc", 0), c("ge", 4), -1.0, A.mult, 1.0, A.add)
     ts(c("oc", 1), c("ge", 4), c("ge", 8), A.subtract)
@@ -478,12 +463,11 @@ def rank_program(g, core, T, topo):
     ts(K(BD), K(CL), 64.0 - V, A.mult, 3.0 * V, A.add)
     ts(K(X7), K(CL), -4.0, A.mult, K(AK), A.add)
     ts(r("u0"), r("xu"), K(X7), A.add, 1024.0, A.mult)
-    lazy[0] = False
     mm(r("pC", 4, 9), r("e8", p=(0, 8)), r("prmf", 0, 5, p=(0, 8)))
     tt(r("sc", 4, 7), r("pC", 6, 9), r("oc", 0, 3), A.mult)
     cp(r("par", 0, 2), r("pC", 4, 6))
     red(c("sc", 8), r("sc", 4, 7))
-    mm(r("pB", 0, 3), r("bdf"), r("cnt", 4, 7))
+    mm(r("pB", 0, 3), r("bd"), r("cnt", 0, 3))
     for t in range(RO):
         ts(c("sc", 9 + t), c("sc", 8), 41.0 * t, A.add, K(QM), A.mult)
 
@@ -499,391 +483,312 @@ def rank_program(g, core, T, topo):
         ts(r("pr"), r("u0"), c("bf", 0), A.add, c("bf", 1), A.mult)
         ts(r("ps"), r("pr"), 12, A.arith_shift_right)
         ts(r("posu"), r("ps"), c("bf", 2), A.add, K(BS), A.add)
-
-    def sel(name, k):
-        ts(r(name), r("si", 0, 144), K(G15), A.is_equal, K(k), A.mult)
-
-    def diag(name, v):
-        ts(r(name), r("si", 0, 128), K(P), A.is_equal, v, A.mult)
-
-    def row(name, n, k):
-        ts(r(name), r("si", 0, n), 0.0, A.mult, K(k), A.add)
     draw(0, r("pB", 0, 3))
-    lazy[0] = True
-    act(r("ds", 0, CAP), r("si", 0, CAP), scale=0.0, bias=K(JB))
-    act(r("mv0"), r("si", 0, 256), scale=0.0, bias=K(K0))
-    act(r("mv1"), r("si", 0, 256), scale=0.0, bias=K(K1))
-    act(r("m4"), r("si", 0, 512), scale=0.0, bias=K(K4))
-    ms(r("mk2", 0, O), 1024.0)
-    ms(r("mk2", O + GH, S1), 1024.0)
-    ms(r("w", 0, O), 0.0)
-    act(r("plt", 0, O), r("si", 0, O), scale=K(K0))
-    ts(K(X10), K(K0), 0.5, A.mult)
-    ts(K(X11), K(K0), K(K2), A.add)
-    ts(K(WR), K(K2), 512.0, A.mult, K(K01), A.add)
-    act(r("mks", S1, S1 + 512), r("si", 0, 512), scale=K(X10), bias=K(X11))
-    for b in range(4):
-        ms(r("selt", 512 * b, 512 * b + 512, 16), 0.0)
-    ms(r("ones"), 1.0)
-    ms(r("msg"), 0.0)
-    ms(r("neg"), -1.0)
-    ms(r("mo"), -float(O))
-    ms(r("rm"), 1.0)
-    ms(r("rm", 0, 192, 32), 0.0)
-    ts(K(K78), K(AK), 8.0, A.is_le, K(G7), A.mult)
-    ts(K(X0), K(K12), K(K78), A.add)
-    ts(K(X12), K(K9), K(K3), A.add, K(K0), A.add)
-    ts(K(RS), K(X0), SC, A.mult, K(X12), A.add)
-    ts(K(X13), K(RS), K(K6), A.add, K(K9), A.subtract)
-    ts(K(WH), K(K12), 1 / SC, A.mult, K(K3), A.add)
-    ts(K(G9), K(G16), 9.0, A.add)
-    ts(K(X1), K(AK), -2048 * SC, A.mult, K(K12), A.mult)
-    ts(K(X2), K(AK), -V * SC, A.mult, (6 * V - B0 + 1) * SC, A.add)
-    ts(K(X3), K(K6), SC, A.mult, K(X1), A.add)
-    ts(K(RB), K(X2), K(K78), A.mult, K(X3), A.add)
-    ts(K(R0), K(RS), float(B0), A.mult, K(RB), A.add)
-    ts(K(RF), K(K9), -float(B0), A.mult, K(RB), A.add)
-    ts(K(MG), K(K9), -float(B0), A.mult, MAGIC, A.add)
-    ts(K(US), K(X0), 1 / SC - 1, A.mult, 1.0, A.add)
-    ts(K(MN), K(K78), -2047.0, A.mult, 2048.0, A.add)
-    ts(K(WC), K(K6), 4 / SC, A.mult, K(K78), A.add)
-    ts(K(K123), K(K12), K(K3), A.add)
-    ts(K(X15), K(X0), K(K3), A.add, K(K6), A.add)
-    diag("mh0", K(X15))
-    ts(r("mh1"), r("si", 0, 128), K(G9), A.is_equal, K(WH), A.mult)
-    tt(r("mh"), r("mh0"), r("mh1"), A.add)
-    diag("mb", K(X13))
-    diag("i0", K(K0))
-    ts(K(X4), K(K123), 1 / 4096, A.mult)
-    ts(K(X5), K(K6), -B0 / 4096 / SC, A.mult, K(X4), A.add)
-    ts(K(WP), K(K78), -V / 4096, A.mult, K(X5), A.add)
-    ts(K(K45), K(K4), K(K5), A.add)
-    ts(K(TG), K(K5), -512.0, A.mult, K(K4), A.add)
-    ts(c("lg", 0), c("par", 0), K(K0), A.mult)
-    ts(c("lg", 1), c("par", 1), K(K1), A.mult, c("lg", 0), A.add)
-    ts(K(THB), c("lg", 1), -1.0, A.mult, 0.5, A.add)
-    for nme, k in (("y0", K0), ("y0b", K0), ("y1", K1), ("y01b", K01), ("y123", WH), ("yrk", WR), ("y45", K45), ("ycl", WC), ("ypos", WP)):
-        sel(nme, k)
-    for nme, v in (("i16", 1 / 16), ("ineg", -1.0), ("ibias", -15 / 32), ("ipos", 1.0), ("ih", 1.0), ("d48", 2047.0), ("d81", 8192.0)):
-        diag(nme, v)
-    for nme, v in (("bd2", 2.0), ("bdm", -1.0), ("bd16", -16.0)):
-        act(r(nme), r("bdf"), scale=v)
-    for nme, v in (("bdh", 1.0), ("bdn", -1.0)):
-        ts(r(nme), r("bdf"), v, A.mult)
-    ts(r("tri"), r("si", 0, 128), K(P), A.is_lt, -1.0, A.mult)
-    tt(r("us"), r("tri"), r("bdf"), A.mult)
-    tt(r("ub"), r("us"), r("d48"), A.add)
-    tt(r("uj"), r("us"), r("d81"), A.add)
-    ts(r("ujn"), r("uj"), -1.0, A.mult)
-    ts(r("cl"), r("jl"), -1.0, A.mult, 511.0, A.add)
-    for nme, n, v in (("d257", 16, 257), ("d1h", 32, 1024), ("d15", 32, 1536), ("d2k", 32, 2048)):
-        ts(r(nme), r("jl", 0, n), float(v), A.add)
+    ts(r("mv0"), r("ones"), K(K0), A.mult)
+    ts(r("mv1"), r("ones"), K(K1), A.mult)
+    lin(r("nl", 0, 512), r("si", 0, 512), 2.0, 2048.0)
+    lin(r("plt", 0, O), r("si", 0, O), K(K0))
+    lin(K(X10), K(K0), -0.5)
+    lin(r("mks", S1, S1 + 512), r("si", 0, 512), K(X10))
+    keep(r("rm"), r("ones", 0, 96), [[0, 3], [1, 32]], A.not_equal, 0.0, 0, 0)
+    keep(r("rm4"), r("ones", 0, 128), [[0, 32], [1, 4]], A.not_equal, 0.0, 0, 0)
+    lin(K(K12), K(K1), 1.0, K(K2))
+    lin(K(K78), K(K7), 1.0, K(K8))
+    lin(K(X0), K(K12), 1.0, K(K78))
+    lin(K(X17), K(K9), 1.0, K(K3))
+    lin(K(X12), K(X0), SC, K(X17))
+    lin(K(RS), K(X12), 1.0, K(K0))
+    lin(K(X1), K(K2), -4096 * SC)
+    lin(K(X18), K(K1), -2048 * SC, K(X1))
+    lin(K(X3), K(K6), SC, K(X18))
+    lin(K(X2), K(K7), -(B0 + V - 1) * SC, K(X3))
+    lin(K(RB), K(K8), -(B0 + 2 * V - 1) * SC, K(X2))
+    lin(K(R0), K(RS), float(B0), K(RB))
+    lin(K(RN), K(X12), float(V + B0), K(RB))
+    lin(K(RF), K(K9), -float(B0), K(RN))
+    lin(K(X8), K(K7), -1.0, K(K6))
+    lin(K(X9), K(K8), -1.0, K(K7))
+    lin(c("cf", 0), K(X8), 1 / 16)
+    lin(c("cf", 1), K(X9), 1 / 16)
+    lin(K(MG), K(K9), -float(B0), MAGIC)
+    lin(K(US), K(X0), 1 / SC - 1, 1.0)
+    lin(K(MN), K(K78), -2047.0, 2048.0)
+    lin(K(WC), K(K6), 4 / SC, K(K78))
+    lin(K(K123), K(K12), 1.0, K(K3))
+    lin(K(X14), K(K3), 1.0, K(K6))
+    lin(K(X13), K(X0), SC, K(X14))
+    lin(K(X4), K(K123), 1 / 4096)
+    lin(K(X5), K(K6), -B0 / 4096 / SC, K(X4))
+    lin(K(WP), K(K78), -V / 4096, K(X5))
+    lin(K(K23), K(K2), 1.0, K(K3))
+    lin(K(K45), K(K4), 1.0, K(K5))
+    lin(K(K26), c("le", 6), -BIG, 0.5)
+    lin(K(X6), K(K01), BIG, K(K26))
+    ts(c("lg", 0), c("par", 0), c("par", 1), A.min, K(K23), A.mult)
+    ts(c("lg", 1), c("par", 0), c("par", 1), A.max, K(K45), A.mult)
+    lin(c("lg", 2), c("par", 0), K(K0), c("lg", 0))
+    lin(c("lg", 3), c("par", 1), K(K1), c("lg", 1))
+    lin(c("lg", 4), c("lg", 2), -1.0, K(X6))
+    lin(K(THB), c("lg", 3), -1.0, c("lg", 4))
+    lin(K(X19), K(K7), -BIG)
+    lin(K(MA), K(K6), BIG / SC, K(X19))
+    lin(K(MB), K(X9), BIG)
+    lin(K(MC), K(K8), BIG)
+    lin(r("msk"), r("bd"), 0.0)
+    for k, m in ((2, MA), (6, MA), (3, MB), (4, MB), (5, MC)):
+        lin(r("msk", k, 128, 16), r("bd", k, 128, 16), K(m))
+    lin(K(X20), K(K5), 1.0, K(X14))
+    lin(K(X11), K(K2), -1.0, K(X20))
+    lin(K(X21), K(K4), -1.0, K(X11))
+    lin(K(X16), K(K7), 1.0, K(X21))
+    lin(K(WN), K(X16), 0.5)
+    lin(K(X15), K(K7), 2.0)
+    lin(r("sg", 512, 528), r("ones", 0, 16), K(X15))
+    ts(r("yb"), r("si", 0, 144), K(G15), A.is_equal)
+    ts(r("y0"), r("yb"), K(K0), A.mult)
+    ts(r("yrk"), r("yb"), K(K02), A.mult, -1.0, A.mult)
+    for nme, k in (("y01", K01), ("y123", K123), ("ycl", WC), ("ypos", WP), ("ynl", WN)):
+        lin(r(nme), r("yb"), K(k))
+    ts(r("ih"), r("si", 0, 128), K(P), A.is_equal)
+    for nme, v in (("i16", 1 / 16), ("ineg", -1.0), ("ibias", -15 / 32), ("i0", K(K0))):
+        ts(r(nme), r("ih"), v, A.mult)
+    lin(r("mh0"), r("ih"), K(X13))
+    for o, v in [(r("i8k"), 8192.0)] + [(r("ic", 128 * k, 128 * k + 128), 1536.0 + NB * k) for k in range(3)]:
+        keep(o, w(0, 0, 128), [[-1, 128]], A.not_equal, v, 0, 1)
+    for nme, v in (("bd2", 2.0), ("bd16", -16.0), ("bdn", -1.0)):
+        lin(r(nme), r("bd"), v)
+    keep(r("usn"), r("bd"), [[-1, 128]], A.is_gt, 0.0, 0, 1)
+    keep(r("us"), r("bdn"), [[-1, 128]], A.is_gt, 0.0, 0, 1)
+    lin(K(X22), K(K01), V / 2)
+    lin(r("mcl"), r("bd"), K(X22))
+    lin(r("mcl", 0, 128, 16), r("bd", 0, 128, 16), 0.0)
+    lin(r("jl", 0, 34), r("si", 0, PT, 16), 1.0, K(AK))
+    lin(r("d2k"), r("jl", 0, 32), 1.0, 2048.0)
+    ts(r("d1h"), r("jl", 0, 32), 1024.0, A.add)
+    ts(r("dl", 0, 34), r("jl", 0, 34), 2.0, A.mult, 3.0 * NB, A.add)
+    iota(r("c16", 0, 34), [[16, 34]], 0, 0)
+    lin(r("vv", 0, 128, 4), r("jl", 0, 32))
     ts(r("id16"), r("si", 0, 112), 16.0, A.mult, float(O - B0), A.add)
-    ts(r("r0"), r("si", 0, 16), K(K0), A.mult, K(R0), A.add)
-    lazy[0] = False
+    lin(r("r0"), r("si", 0, 16), K(K0), K(R0))
 
     def places(b):
         o = lambda a: r(("pS", "pE")[b % 2], 112 * a, 112 * a + 112)
         for a in range(4):
             mm(o(a), r("i0"), r("id16"), True, False)
-            mm(o(a), r("selt", 128 * (4 * b + a), 128 * (4 * b + a) + 128), r("plcf"), False, True)
+            for h in range(2):
+                mm(o(a), r("selt", 128 * (4 * b + a), 128 * (4 * b + a) + 128), r("plch", 112 * h, 112 * h + 112), False, h == 1)
         for a in range(4):
             act(r("plt", O + 4 * b + a, S1, 16), o(a), AF.Relu, scale=K(RS), bias=c("r0", 4 * b + a))
 
     for t in range(RO):
         final = t == RO - 1
-        mk = lambda a, b, **k: r("mk", 2560 * t + a, 2560 * t + b, **k)
-        w4 = lambda a, b, **k: r("w4", a, b, **k)
-        sl = lambda n=512, **k: r("sl", 768 * t, 768 * t + n, **k)
-        wn = lambda lst: r("w", O, O + W, off=lst)
+        mk = lambda a, b, u=t, **k: r("mk", 2560 * (u % 2) + a, 2560 * (u % 2) + b, **k)
+        sl = lambda n=512, a=0, u=t, **k: r("sl", 768 * (u % 2) + a, 768 * (u % 2) + n, **k)
+        z = lambda n, k, o=0: r(n, o + 32 * k, o + 32 * k + 32)
+        y = lambda n, k: r(n, 48 * k, 48 * k + 34)
         cp(r("dr", 0, 256), r("bag", off=r("posu")))
         tolist("pA", 0, "y0", "dr", 256)
         cp(r("tu", 0, 16), r("pA", 0, 16))
-        for a, b in ((0, 6), (6, 16)) if CUTM else ((0, 16),):
+        for a, b in ((0, CUTM), (CUTM, 16)):
             cp(r("nbm", 16 * a, 16 * b), r("nbi", off=r("tu", a, b)))
-        lazy[0] = True
-        if not VIAW:
-            ts(r("dz"), r("dr", 0, 256), K(K0), A.mult, K(K1), A.add)
-            scan(r("dj"), r("mv1"), r("dz"), A.mult, A.add)
-        lazy[0] = False
-        ids = r("msg", MSG * t, MSG * t + 5)
-        clamp = lambda o, i: ts(o, i, 188 - 15 / 32, A.max, 196 - 15 / 32, A.min)
-
-        def sums(o, old, rows, j0, j1):
-            mm(o, r("ibias"), r("ones", 0, j1 - j0), True, False)
-            mm(o, r("ineg"), r(old, j0, j1), False, False)
+        act(r("oldm"), w(t, 0, S1, off=r("tu", 0, 16)), bias=-192.0)
+        for j0, j1, e in MOVES[t > 0]:
+            take(e, r("gm", 16 * j0, 16 * j1), w(t, O, WS, off=r("nbm", j0, j1)))
+        mm(r("pF", 0, 256), r("ibias"), r("ones"), True, False)
+        mm(r("pF", 0, 256), r("ineg"), r("oldm"), False, False)
+        for j0, j1 in SUMS[t > 0]:
             for i in range(16):
-                mm(o, r("i16"), r(rows, 16 * j0 + i, 16 * j1, 16), False, i == 15)
-
-        def moves(on):
-            for j0, j1, e in MOVES[t > 0]:
-                if e == on:
-                    take(e, r("gm", 16 * j0, 16 * j1), wn(r("nbm", j0, j1)))
-
-        def steps():
-            for j0, j1 in SUMS[t > 0]:
-                sums(r("pF", j0, j1), "oldm", "gm", j0, j1)
-            clamp(r("rr"), r("pF", 0, 256))
-
-        def ascending():
-            ts(r("dr", 256, 512), r("nbm"), float(O), A.add)
-            tolist("pC", 0, "y0", "dr", 256, at=256)
-            yield
-            cp(r("tu", 16, 32), r("pC", 0, 16))
-            cp(mk(0, 2560, off=r("tu", 16, 32)), r("mv1"))
-            yield
-            cum(r("mks", 0, S1), mk(0, S1))
-            yield
-            for h, e in enumerate(RANK):
-                take(e, r("rk", 256 * h, 256 * h + 256), r("mks", off=r("tu", 16 * h, 16 * h + 16)))
-            tolist("pG", 0, "yrk", "rk", 512)
-            act(r("rec"), r("plt", off=r("tu")))
-            ts(r("rku"), r("pG", 0, 32), -1.0, A.add)
-            yield
-            act(sl(768, off=r("rku", 0, 16)), r("rec", 0, 256), AF.Silu)
-            act(sl(768, off=r("rku", 16, 32)), r("rec", 256, 512), AF.Silu)
-            yield
-            ts(r("sl16"), sl(), K(US), A.mult, K(MN), A.min)
-            tolist("pA", 0, "y0", "sl16", 512)
-            cp(r("su"), r("pA", 0, 32))
-            for a, b in ((0, CUTU), (CUTU, 32)) if CUTU else ((0, 32),):
-                cp(r("nbu", 16 * a, 16 * b), r("nbi", off=r("su", a, b)))
-            yield
-        asc = ascending()
-
-        def sort(k):
-            for _ in range(SORT[t > 0][k]):
-                next(asc)
-            for j0, j1, e in MOVES[t > 0]:
-                if e == k:
-                    cp(r("gm", 16 * j0, 16 * j1), wn(r("nbm", j0, j1)))
-        act(r("oldm"), r("w", 0, S1, off=r("tu", 0, 16)), bias=-192.0)
-        for b in range(EARLY if t == 0 else 0):
-            places(b)
-        moves("s")
-        for b in range(EARLY, 4 if t == 0 else 0):
-            places(b)
-        sort(0)
+                mm(r("pF", j0, j1), r("i16"), r("gm", 16 * j0 + i, 16 * j1, 16), False, i == 15 and (j0, j1) == SUMS[t > 0][-1])
+        ts(r("rr"), r("pF", 0, 256), 188 - 15 / 32, A.max, 196 - 15 / 32, A.min)
         cp(mk(0, 2048, off=r("tu", 0, 16)), r("mv0"))
-        cum(r("mk2", O, O + GH), mk(O, O + GH))
-        cp(r("rkd"), r("mk2", off=r("tu", 0, 16)))
-        tolist("pB", 0, "y0b", "rkd", 256)
-        sort(1)
-        tt(r("t1"), r("pB", 0, 16), r("d257"), A.min)
-        ts(r("dru"), r("t1"), -1.0, A.add)
-        cp(r("ds", off=r("dru")), r("dr", 0, 256) if VIAW else r("dj"))
-        cp(r("dsh"), r("ds", 0, CAP))
-        sort(2)
-        lazy[0] = True
+        cum(r("mk2"), mk(O, O + GH))
+        ts(r("tuc"), r("pA", 0, 16), -float(O), A.add, GH - 1.0, A.min)
+        take(ENG["rkd"], r("rkd"), r("mk2", off=r("tuc")))
+        ts(r("dr", 256, 512), r("nbm"), float(O), A.add)
+        tolist("pB", 0, "y0", "rkd", 256)
+        tolist("pC", 0, "y0", "dr", 256, at=256)
+        ts(r("t1", 0, 16), r("pB", 0, 16), float(CAP), A.is_gt, 2048.0, A.mult)
+        tt(r("t1", 16, 32), r("t1", 0, 16), r("pA", 0, 16), A.add)
+        cp(r("pu"), r("t1", 16, 32))
+        tt(r("pub", off=r("pu")), r("rr"), r("oldm"), A.add)
+        exchange(t + 1, r("pub", O, O + GH), "sent", total_e * (t + 1))
+        tt(w(t + 1, 0, S1, off=r("tu", 0, 16)), r("rr"), r("oldm"), A.add)
         if not final:
-            act(r("ds", 0, CAP), r("si", 0, CAP), scale=0.0, bias=K(JB))
-        lazy[0] = False
-        vals = r("msg", MSG * t + 8, MSG * t + 8 + CAP)
-        if not VIAW:
-            tolist("pD", 0, "y1", "dsh", CAP)
-            ts(r("ju", 0, 5), r("pD", 0, 5), -1.0, A.add)
-            if NEW:
-                moves("v")
-                steps()
-                tt(r("nw"), r("rr"), r("oldm"), A.add)
-                cp(vals, r("nw", off=r("ju", 0, 5)))
-            else:
-                cp(r("osel"), r("oldm", off=r("ju", 0, 5)))
-                moves("v")
-                steps()
-                tt(vals, r("rr", off=r("ju", 0, 5)), r("osel"), A.add)
-        mm(r("pB", 32, 37), r("ih"), r("mo", 0, 5), True, False)
-        tolist("pB", 32, "y0", "dsh", CAP, first=False)
-        tt(ids, r("pB", 32, 37), r("d15", 0, 5), A.min)
-        tt(r("msg", MSG * t + 8 + CAP, MSG * t + 13 + CAP), r("pB", 32, 37), r("d15", 0, 5), A.min)
-        if VIAW:
-            cp(r("ju", 0, 5), ids)
-            moves("v")
-            steps()
-            tt(r("w", 0, S1, off=r("tu", 0, 16)), r("rr"), r("oldm"), A.add)
-            cp(vals, r("w", O, S1, off=r("ju", 0, 5)))
-        at = lambda s: (MSG - 8) * (3 * t + s)
-        exchange(t, lambda s: r("msg", MSG * t + 8 * (s == 1), MSG * t + MSG - 8 * (s != 1)), lambda d, s: r("land", at(s), at(s + 1)), "sent", total_e * (t + 1))
-        if not final:
-            iota(mk(2560, 2560 + S1), [[0, S1]], 0, 0, "post")
-            iota(r("sl", 768 * t + 768, 768 * t + 1280), [[0, 512]], 0, 0, "post")
-        sort(3)
-        if NEW:
-            cp(r("w", 0, S1, off=r("tu", 0, 16)), r("nw"))
-        elif not VIAW:
-            tt(r("w", 0, S1, off=r("tu", 0, 16)), r("rr"), r("oldm"), A.add)
-        sort(4)
-        sort(5)
-        if final:
-            dma(T.yx[:, :], r("w", O, S1))
-        came = {slot(rank, d): float(GH * d) for d in range(N - 1)}
-        ts(r("gou", 16, 21), r("land", at(2), at(2) + 5), came[2], A.add)
-        cp(r("w", S1, off=r("gou", 16, 21)), r("land", at(2) + 8, at(3)))
-        ts(r("gou", 0, 5), r("land", at(0), at(0) + 5), came[0], A.add)
-        ts(r("gou", 5, 10), r("land", at(2) - 8, at(2) - 3), came[1], A.add)
-        cp(r("w", S1, off=r("gou", 0, 10)), r("land", at(0) + 8, at(2) - 8))
-        for n, (j0, j1, e) in enumerate(CHUNKS):
-            if n == SV:
-                act(r("sv"), r("w", 0, S1, off=r("su")))
-                mm(r("pS"), r("ipos"), r("sv"))
-            take(e, r("gb", 16 * j0, 16 * j1), wn(r("nbu", j0, j1)))
-        cp(r("sf"), r("pA", 0, 32))
-        lazy[0] = True
-        if not final:
-            mm(r("pG"), r("mb"), r("sl16"))
-            act(r("slb"), r("pG"))
-        lazy[0] = False
-        z = lambda n, k, o=0: r(n, o + 32 * k, o + 32 * k + 32)
+            for k in range(4):
+                keep(mk(512 * k, 512 * k + 512, t + 1), r("mkp"), [[0, 512]], A.is_equal, 0.0, 0, 0)
+            iota(sl(u=t + 1), [[0, 512]], 0, 0)
+            dma(w(t + 2, 0, S1), w(t + 1, 0, S1), after=w(t + 1, S1, WS))
+        else:
+            dma(T.yx[:, :], w(RO, O, S1), after=w(RO, S1, WS))
+        if t == 0:
+            for b in range(4):
+                places(b)
+        cp(r("tu", 16, 32), r("pC", 0, 16))
+        cp(mk(0, 2560, off=r("tu", 16, 32)), r("mv1"))
+        cum(r("mks", 0, S1), mk(0, S1))
+        for h in (1, 0):
+            act(r("rec", 256 * h, 256 * h + 256), r("plt", off=r("tu", 16 * h, 16 * h + 16)))
+        act(r("junk"), r("rec", 256, 512), AF.Sign, accum_out=c("acc", 0))
+        ts(r("uq", 0, 2), r("cf", 0, 2), c("acc", 0), A.mult)
+        mm(r("pC", 0, 2), r("bd"), r("uq", 0, 2))
+        lin(r("af", 8, 10), r("ns", 0, 2), 1 / 16, -4.0)
+        for k in range(2):
+            ts(c("ai", k), c("pC", k), c("af", 8 + k), A.min, (64 + 7.5) / 16, A.add)
+        ts(c("af", 0), c("ns", 1), c("ns", 0), A.subtract, float(V), A.add)
+        ts(c("af", 1), c("ns", 2), c("ns", 1), A.subtract, float(V), A.add)
+        ts(c("af", 2), c("ns", 0), B0 - 1.0, A.add)
+        ts(y("tq", 0), y("jl", 0), -1.0, A.mult, c("af", 2), A.add)
+        ts(c("af", 4), c("ai", 0), 16.0, A.mult)
+        ts(c("af", 6), c("ai", 0), 16.0, A.mult, c("af", 0), A.add)
+        ts(c("af", 7), c("ai", 1), 16.0, A.mult, c("af", 1), A.add)
+        ts(c("af", 5), c("ai", 1), 16.0, A.mult, c("af", 4), A.add)
+        ts(y("tq", 1), y("jl", 0), c("af", 4), A.is_ge, c("af", 6), A.mult)
+        ts(y("tq", 2), y("jl", 0), c("af", 5), A.is_ge, c("af", 7), A.mult)
+        tt(y("tq", 3), y("tq", 0), y("tq", 1), A.add)
+        tt(y("tq", 4), y("tq", 3), y("tq", 2), A.add)
+        cp(y("tpu", 0), y("tq", 4))
+        cp(r("tbh"), r("bag", off=y("tpu", 0)))
+        act(r("tb"), r("bag", off=y("tpu", 0)))
+        tolist("pC", 0, "y0", "tbh", PT)
+        cp(y("tbu", 0), r("pC", 0, 34))
+        take(ENG["ri"], r("ri"), r("mks", 0, S1, off=y("tbu", 0)))
+        for h, e in enumerate(RANK):
+            take(e, r("rk", 256 * h, 256 * h + 256), r("mks", off=r("tu", 16 * h, 16 * h + 16)))
+        tolist("pG", 0, "yrk", "rk", 512)
+        ts(r("rku"), r("pG", 0, 32), 512.0, A.add)
+        tolist("pG", 0, "yrk", "ri", PT)
+        ts(y("riu", 0), r("pG", 0, 34), 512.0, A.add, 512.0, A.min)
+        act(sl(768, off=r("rku", 0, 16)), r("rec", 0, 256), AF.Silu)
+        act(sl(768, off=r("rku", 16, 32)), r("rec", 256, 512), AF.Silu)
+        ts(r("sl16"), sl(), K(US), A.mult, K(MN), A.min)
+        tolist("pD", 0, "y0", "sl16", 512)
+        cp(r("su"), r("pD", 0, 32))
+        for a, b in ((0, CUTU), (CUTU, 32)):
+            cp(r("nbu", 16 * a, 16 * b), r("nbi", off=r("su", a, b)))
+        take(ENG["sv"], r("sv"), w(t + 1, 0, S1, off=r("su")))
+        mm(r("pS"), r("ih"), r("sv"))
         tolist("pB", 0, "ycl", "sl16", 512)
-        tolist("pC", 0, "ypos", "sl16", 512)
-        ts(r("v18"), r("pB", 0, 32), 4.0, A.is_ge, 18.0, A.mult)
         for k in range(3):
             ts(z("ne", k), r("pB", 0, 32), 4.0 + k, A.not_equal)
+        scan(r("sa"), r("rm"), r("ne"), A.mult, A.add)
+        tolist("pD", 32, "y123", "sl16", 512)
+        lin(r("sf"), r("pD", 0, 64))
+        tolist("pA", 0, "ypos", "sl16", 512)
+        ts(r("v18"), r("pB", 0, 32), 4.0, A.is_ge, 18.0, A.mult)
         for k in range(3):
             ts(z("rq", k), z("ne", k), 83.0 - 2 * k, A.mult, 16.0 + 2 * k, A.add)
-            tt(z("pp", k), r("pC", 0, 32), z("ne", k), A.max)
-            tt(z("pn", k), r("pC", 0, 32), z("ne", k), A.subtract)
-        scan(r("sa"), r("rm", 0, 96), r("ne"), A.mult, A.add)
-        scan(r("sb"), r("ne"), r("neg"), A.add, A.add)
-        ts(r("nq", 0, 3), r("ns", 0, 3), K(K0), A.mult, -32.0, A.add)
-        ts(r("nq", 4, 7), r("ns", 0, 3), -1536.0, A.add, K(K0), A.mult)
-        ts(c("lg", 5), c("ns", 2), B0 + 2 * V - 1.0, A.add)
+            ts(z("rq", 3 + k), z("ne", k), 2 * k - 83.0, A.mult, 99.0, A.add)
+            tt(z("pp", k), r("pA", 0, 32), z("ne", k), A.max)
+        lin(r("nq", 0, 3), r("ns", 0, 3), K(K0), -32.0)
         tt(r("nqh", 0, 3), r("nq", 0, 3), r("sa", 31, 96, 32), A.add)
-        tt(r("nqh", 4, 7), r("nq", 4, 7), r("sb", 31, 96, 32), A.add)
-        for n, (j0, j1, e) in enumerate(CHUNKS):
-            o = r("pE", j0, j1) if n < len(CHUNKS) - 1 else r("pF", j0, j1)
-            mm(o, r("bd16"), r("sv", j0, j1), True, False)
-            for i in range(16):
-                mm(o, r("bdm"), r("gb", 16 * j0 + i, 16 * j1, 16), False, False)
-            for i in range(16):
-                tt(r("mx", 512 * i + j0, 512 * i + j1), r("gb", 16 * j0 + i, 16 * j1, 16), r("pS", j0, j1), A.max)
-                mm(o, r("bd2"), r("mx", 512 * i + j0, 512 * i + j1), False, i == 15)
-        jl = CHUNKS[-1][0]
-        act(r("sg", 0, jl), r("pE", 0, jl), AF.Sign, bias=K(THB))
-        act(r("sg", jl, 512), r("pF", jl, 512), AF.Sign, bias=K(THB))
-        mm(r("pA", 0, 32), r("ih"), r("v18"), True, False)
-        tolist("pA", 0, "y01b", "sg", 512, first=False)
-        for k in range(3):
-            tt(z("fl", k, 96), r("pA", 0, 32), z("rq", k), A.is_equal)
-        scan(r("s1", 96, 192), r("rm", 0, 96), r("fl", 96, 192), A.mult, A.add)
-        cum(r("s2"), r("fl", 96, 192))
-        Lc, Dn, Nn = (lambda k: c("pC", k)), (lambda k: c("pC", 4 + k)), r("pG", 100, 103)
-        mm(r("pC", 0, 3), r("bdh"), r("nqh", 0, 3), True, False)
-        mm(r("pC", 0, 3), r("bdh"), r("s1", 127, 192, 32), False, True)
-        mm(r("pC", 4, 7), r("bdh"), r("nqh", 4, 7), True, False)
-        mm(r("pC", 4, 7), r("bdh"), r("s2", 31, 96, 32), False, True)
-        tt(r("zz"), r("fl", 96, 192), r("pp"), A.max)
-        for k in range(3):
-            ts(z("ho", k), z("zz", k), 4096.0, A.mult, Lc(k), A.is_lt)
-        cum(r("hs"), r("ho"))
-        tt(r("zn"), r("pn"), r("fl", 96, 192), A.subtract)
-        for k in range(3):
-            ts(z("xh", k), z("zn", k), 4096.0, A.mult, Dn(k), A.subtract)
-        mm(r("pD", 0, 224, 7), r("ih"), r("d1h"))
-        for k in range(3):
-            mm(r("pD", 1 + k, 224, 7), r("ih"), z("xh", k))
-        for k in range(3):
-            mm(r("pD", 4 + k, 224, 7), r("ub"), z("ho", k), True, False)
-            mm(r("pD", 4 + k, 224, 7), r("bdh"), z("hs", k), False, True)
-        mm(c("pD", 300), r("bdh"), c("hs", 95))
-        scan(r("o7"), r("rm7"), r("pD", 0, 224), A.mult, A.max)
-        ts(r("o4u"), r("o7", 6, 224, 7), -1024.0, A.add)
-        act(w4(512, 1024), r("si", 0, 512), scale=K(K5), bias=K(TG))
-        act(w4(1024, 1536), r("si", 0, 512), AF.Relu, scale=K(RS), bias=K(RB))
-        act(w4(0, 1536, off=r("o4u")), sl() if final else r("slb"), AF.Silu)
-        lazy[0] = True
-        cp(c("lg", 4), c("pD", 300))
-        for k in range(3):
-            ts(z("fl", k), r("pA", 0, 32), 16.0 + 2 * k, A.is_equal)
-        scan(r("s1", 0, 96), r("rm", 0, 96), r("fl", 0, 96), A.mult, A.add)
-        mm(r("pG", 0, 96), r("bdn"), r("s1", 96, 192), True, False)
-        mm(r("pG", 0, 96), r("ujn"), r("fl", 96, 192), False, False)
-        mm(r("pG", 0, 96), r("uj"), r("fl", 0, 96), False, False)
-        mm(r("pG", 0, 96), r("bdh"), r("s1", 0, 96), False, True)
-        if not final:
-            mm(Nn, r("bdh"), r("nqh", 0, 3), True, False)
-            mm(Nn, r("bdh"), r("s1", 31, 96, 32), False, True)
-        for k in range(3):
-            ts(z("vv", k), z("pG", k), Lc(k), A.add, B0 + V * k - 8193.0, A.add)
-        tt(z("npl", 0), z("vv", 0), z("vv", 1), A.max)
-        tt(z("npl", 1), z("vv", 2), r("jl"), A.max)
-        tt(z("npl", 2), z("npl", 0), z("npl", 1), A.max)
-
-        def tails():
-            for k in (1, 2):
-                ts(z("yy", k), r("d15"), Dn(k), A.add, Lc(k), A.is_ge)
-                ts(z("yy", 2 + k), r("d15"), Dn(k), A.add, float(B0 + V * k), A.add)
-            ts(z("yy", 0), r("d15"), Dn(0), A.add, float(B0), A.add)
-            tt(r("yy", 160, 224), r("yy", 32, 96), r("yy", 96, 160), A.mult)
-            tt(z("yy", 7), z("yy", 0), z("yy", 5), A.max)
-            tt(z("yy", 8), z("yy", 7), z("yy", 6), A.max)
-            ts(r("tpu"), z("yy", 8), c("lg", 5), A.min)
-            cp(r("tb"), r("bag", off=r("tpu")))
-            tolist("pB", 0, "y0", "tb", 512)
-
-        def leavers():
-            ts(z("lv", 0), z("npl", 2), float(B0), A.is_lt, 4096.0, A.mult)
-            tt(z("lv", 1), z("lv", 0), r("sf"), A.add)
-            tt(z("lv", 2), z("lv", 1), r("d2k"), A.min)
-            cp(r("lvu"), z("lv", 2))
-
-        def records():
-            if not final:
-                mm(r("pS"), r("i0"), r("sl16"), True, False)
-            for a in range(16):
-                mm(r("pS", a, 512, 16), r("selt", 128 * a, 128 * a + 128), z("npl", 2), final, final or a == 15)
-            act(r("nrec"), r("pS"), AF.Relu, scale=K(RS), bias=K(RF if final else RB))
-
-        def holes():
-            scan(r("ts4"), r("m4"), w4(512, 1024), A.mult, A.add)
-            mm(r("pF", 0, 32), r("ih"), r("cl"), True, False)
-            tolist("pF", 0, "y45", "ts4", 512, first=False)
-            cp(r("ixu"), r("pF", 0, 32))
-
-        def stayers():
-            ts(z("st", 0), r("pF", 0, 32), c("lg", 4), A.is_ge, 4096.0, A.mult)
-            tt(z("st", 1), z("st", 0), r("pB", 0, 32), A.add)
-            tt(z("st", 2), z("st", 1), r("d2k"), A.min)
-            cp(r("stu"), z("st", 2))
+        for k in range(2):
+            ts(y("bb", k), y("jl", 0), c("af", 4 + k), A.is_ge, float(NB), A.mult)
+            ts(y("rx", k), y("c16", 0), c("af", 4 + k), A.not_equal)
+        tt(y("rx", 2), y("rx", 0), y("rx", 1), A.mult)
         if final:
             for h in range(4):
                 ts(r("plf", O + 448 * h, O + 448 * h + 448), r("plt", O + 448 * h, O + 448 * h + 448), K(MG), A.add, MAGIC, A.subtract)
-            lazy[0] = False
-            tails()
-            records()
-            holes()
-            act(r("slb"), w4(1024, 1536, off=r("ixu")), bias=K(MG))
-            act(r("hf"), r("slb"), bias=-MAGIC)
-            leavers()
-            stayers()
+            ts(r("slr"), sl(), K(MG), A.add, MAGIC, A.subtract)
+        for j0, j1, e in CHUNKS:
+            take(e, r("gb", 16 * j0, 16 * j1), w(t + 1, O, WS, off=r("nbu", j0, j1)))
+        jl = CHUNKS[-1][0]
+        for o in (r("pE", 0, jl), r("pF", jl, 512)):
+            mm(o, r("msk"), r("sl16", o[2], o[3]), True, False)
+            mm(o, r("bd16"), r("sv", o[2], o[3]), False, False)
+        for n, (j0, j1, e) in enumerate(CHUNKS):
+            o = r("pE", j0, j1) if n < len(CHUNKS) - 1 else r("pF", j0, j1)
+            for i in range(16):
+                mm(o, r("bdn"), r("gb", 16 * j0 + i, 16 * j1, 16), False, False)
+            for i in range(16):
+                tt(r("mx", 512 * i + j0, 512 * i + j1), r("gb", 16 * j0 + i, 16 * j1, 16), r("pS", j0, j1), A.max)
+                mm(o, r("bd2"), r("mx", 512 * i + j0, 512 * i + j1), False, i == 15 and n >= len(CHUNKS) - 2)
+        act(r("sg", 0, jl), r("pE", 0, jl), AF.Sign, bias=K(THB))
+        act(r("sg", jl, 512), r("pF", jl, 512), AF.Sign, bias=K(THB))
+        for a, b, e in ((0, 18, "s"), (18, 34, "v")):
+            take(e, r("tg", 16 * a, 16 * b), r("sg", off=r("riu", a, b)))
+        mm(r("pA", 0, 32), r("ih"), r("v18"), True, False)
+        tolist("pA", 0, "y01", "sg", 512, first=False)
+        for k, x in enumerate((y("bb", 0), y("bb", 1), y("dl", 0))):
+            mm(r("pD", 0, 34), r("ih"), x, k == 0, False)
+        tolist("pB", 0, "ynl", "tg", PT)
+        scan(y("tx", 0), y("rx", 2), r("pB", 0, 34), A.mult, A.add)
+        cp(y("tx", 1), r("pB", 0, 34))
+        tt(y("tx", 2), r("pB", 0, 34), y("dl", 0), A.mult)
+        mm(r("pD", 0, 34), r("bd"), y("tx", 0), False, False)
+        mm(r("pD", 0, 34), r("us"), y("tx", 1), False, False)
+        mm(r("pD", 0, 34), r("ineg"), y("tx", 2), False, True)
+        cp(y("itu", 0), r("pD", 0, 34))
+        act(r("nl", 512, off=y("itu", 0)), r("tb"), AF.Silu)
+        for k in range(3):
+            tt(z("fl", k), r("pA", 0, 32), z("rq", k), A.is_equal)
+        scan(r("s1", 0, 96), r("rm"), r("fl", 0, 96), A.mult, A.add)
+        Lc, Nn = (lambda k: c("pC", k)), r("pG", 100, 103)
+        mm(r("pC", 0, 3), r("bd"), r("nqh", 0, 3), True, False)
+        mm(r("pC", 0, 3), r("bd"), r("s1", 31, 96, 32), False, True)
+        tt(r("zz"), r("fl", 0, 96), r("pp"), A.max)
+        for k in range(3):
+            ts(z("ho", k), z("zz", k), 4096.0, A.mult, Lc(k), A.is_lt)
+        scan(r("hs"), r("rm"), r("ho"), A.mult, A.add)
+        mm(r("pE", 0, 128, 4), r("ih"), r("d1h"))
+        for k in range(3):
+            o = r("pE", 1 + k, 128, 4)
+            mm(o, r("ic", 128 * k, 128 * k + 128), z("ho", k), True, False)
+            mm(o, r("us"), z("ho", k), False, False)
+            mm(o, r("bd"), z("hs", k), False, True)
+        scan(r("o3"), r("rm4"), r("pE", 0, 128), A.mult, A.max)
+        ts(r("ihu"), r("o3", 3, 128, 4), -1024.0, A.add)
+        cp(r("occ"), r("nl", off=r("ihu")))
+        for k in range(3):
+            tt(z("fl", 3 + k), r("pA", 0, 32), z("rq", 3 + k), A.is_equal)
+        scan(r("s1", 96, 192), r("rm"), r("fl", 96, 192), A.mult, A.add)
+        mm(r("pG", 0, 96), r("i8k"), r("fl", 96, 192), True, False)
+        mm(r("pG", 0, 96), r("usn"), r("fl", 96, 192), False, False)
+        mm(r("pG", 0, 96), r("bdn"), r("s1", 96, 192), False, True)
+        mm(Nn, r("bd"), r("nqh", 0, 3), True, False)
+        mm(Nn, r("bd"), r("s1", 31, 96, 32), False, False)
+        mm(Nn, r("bd"), r("s1", 127, 192, 32), False, True)
+        for k in range(3):
+            ts(r("vv", 1 + k, 128, 4), z("pG", k), c("pG", 100 + k), A.add, B0 + V * k - 8192.0, A.add)
+        scan(r("o4"), r("rm4"), r("vv"), A.mult, A.max)
+        npl = r("o4", 3, 128, 4)
+        if not final:
+            cp(r("jou"), npl)
+            if ENG["jou"] == "v":
+                cp(r("bag", off=r("jou")), sl())
+            else:
+                act(r("bag", off=r("jou")), sl(), AF.Silu)
+            ts(z("hv", 0), r("o3", 3, 128, 4), 1536.0, A.is_gt)
+            tt(z("hv", 1), z("hv", 0), z("sf", 1), A.mult)
+            tt(z("hv", 2), z("hv", 1), r("jl", 0, 32), A.max)
+            cp(r("hou"), z("hv", 2))
+            draw(t + 1, Nn)
+            cp(r("bag", off=r("hou")), r("occ"))
+        ts(z("lv", 0), npl, float(B0), A.is_lt, 4096.0, A.mult)
+        tt(z("lv", 1), z("lv", 0), z("sf", 0), A.add)
+        tt(z("lv", 2), z("lv", 1), r("d2k"), A.min)
+        cp(r("lvu"), z("lv", 2))
+        lin(r("pq"), r("pA", 0, 32), -V / 2, 8.0 * V - B0)
+        tt(r("posl"), npl, r("pq"), A.add)
+        mm(r("pS"), r("mcl"), r("sg", 0, 512), True, False)
+        if not final:
+            mm(r("pS"), r("i0"), r("sl16"), False, False)
+        for a in range(16):
+            mm(r("pS", a, 512, 16), r("selt", 128 * a, 128 * a + 128), r("posl"), False, a == 15)
+        act(r("nrec"), r("pS"), AF.Relu, scale=K(RS), bias=K(RF if final else RN))
+        tolist("pF", 0, "y0", "occ", 512)
+        cp(r("stu"), r("pF", 0, 32))
+        if final:
             cp(r("plf", off=r("lvu")), r("nrec"))
-            cp(r("plf", off=r("stu")), r("hf"))
+            cp(r("plf", off=r("stu")), r("slr"))
             op("y", lambda q, a, k: q.dma_start(T.yp[:, :], T.plf[9:128:16, O:S1]), [], {}, [r("plf", p=(0, 8))], [], ("dma%d" % nd[0], 16, True), "dma")
         else:
-            cp(r("jou"), z("npl", 2))
-            tails()
-            leavers()
-            act(r("bag", off=r("jou")), sl(), AF.Silu)
-            draw(t + 1, Nn)
-            records()
-            lazy[0] = False
-            holes()
-            lazy[0] = True
-            stayers()
-            lazy[0] = False
-            cp(r("hg"), w4(1024, 1536, off=r("ixu")))
-            tolist("pE", 0, "y123", "hg", 512)
-            cp(r("hou"), r("pE", 0, 32))
-            cp(r("bag", off=r("hou")), r("tb"))
             act(r("plt", off=r("lvu")), r("nrec"), AF.Silu)
-            lazy[0] = True
-            mm(r("pD"), r("i0"), r("tb"), True, False)
-            mm(r("pD"), r("mh"), r("hg"), False, True)
-            act(r("hf"), r("pD"))
+            mm(r("pB"), r("i0"), r("occ"), True, False)
+            mm(r("pB"), r("mh0"), r("sl16"), False, False)
+            mm(r("pB"), r("y123", 6, 134), r("sl16"), False, True)
+            act(r("hf"), r("pB"))
             act(r("plt", off=r("stu")), r("hf"), AF.Silu)
-            lazy[0] = False
-    key = slot(rank, 0)
-    if key not in ORDERS:
+    if not ORDERS:
         order = schedule(ops)
-        ORDERS[key] = (order, depend([ops[k] for k in order], False))
-    emit(g, T, [ops[k] for k in ORDERS[key][0]], ORDERS[key][1])
+        ORDERS[0] = (order, depend([ops[k] for k in order], False))
+    emit(g, T, [ops[k] for k in ORDERS[0][0]], ORDERS[0][1])

from concourse.bass import DstId, RemoteDMATransfer
from concourse.mybir import AluOpType as A, ActivationFunctionType as AF, AxisListType as AX

V, GH, CAP, RO, N = 1792, 512, 80, 3, 4
W = V + (N - 1) * GH
O = 256
S1 = O + V
WS = O + W
B0 = 544
PL = B0 + 3 * V
PT = 544
NB = 576
BIG = 65536.0
MAGIC = 12582912.0
SC = 16.0
F, B, H, I, U = "float32", "bfloat16", "float16", "int32", "uint16"
MOVES = (((0, 64, "s"), (64, 128, "v"), (128, 192, "s"), (192, 256, "v")),
         ((0, 64, "s"), (64, 96, "v"), (96, 160, "s"), (160, 208, "v"), (208, 256, "s")))
SUMS = tuple(tuple((a, b) for a, b, e in m) for m in MOVES)
CHUNKS = ((0, 80, "s"), (80, 192, "v"), (192, 320, "s"), (320, 384, "s"), (384, 448, "s"), (448, 512, "s"))
RANK, CUTM, CUTU, SELV = "vs", 6, 6, 2
ENG = {"ri": "s", "jou": "s", "sv": "s", "rkd": "v"}
QUEUES = {
    "s": ["-si -bag -bag@ plt gm#1 gm#0 oldm -mks rec#0 junk rk rec#1 sl@ sv tb gb ri sg tg nl@ bag@ nrec plt@#0 hf",
          "oldm gm -plt@#1 rk rec junk sl@ sv tb gb ri sg tg nl@ bag@ nrec plt@#0 hf",
          "oldm gm -plt@#1 rk rec#0 junk rec#1 sl@ tb sv gb#0 gb#3 gb ri sg tg nl@ nrec"],
    "v": ["dr#0 -mk mk@#0 nbm mk2 rkd gm#0 tu#1 gm#1 mk@#1 t1 mks pu rr rk pub@ rku sl16 -mkp w@ tpu su tbh nbu#1 nbu#0 gb"
          " mx#0:64 tbu mx riu tg itu ihu occ bag@",
          "dr#0 nbm mk@#0 mk2 gm#0 tu#1 rkd gm#1 mk@#1 t1 mks pu rr rk pub@ rku sl16 w@ tpu su tbh nbu gb"
          " mx#0:80 tbu mx riu tg itu ihu occ bag@",
          "dr#0 nbm mk@#0 mk2 gm#1 tu#1 rkd mk@#1 gm#0 mks t1 rr pu rk pub@ plf#0 rku plf#3 w@ plf#2 sl16 su tpu plf#1 nbu#0 tbh"
          " nbu#1 slr gb tbu mx#0:16 mx#64:80 mx riu tg itu ihu occ plf@"],
    "g": ["-si#0 -xg -pint -si#1 -selt -nbi -sl -plt", "", ""],
}


def _sb(c, d):
    return ("sbuf", [128, c], d)


BUF = {
    "w": _sb(4 * WS, B), "pub": _sb(4096, B), "nbi": _sb(2048, I), "bag": _sb(PL + 256, F), "plt": _sb(3072, F), "plf": _sb(3072, F),
    "si": _sb(2048, F), "mk": _sb(2 * 2560, B), "mkp": _sb(512, B), "mks": _sb(2560, B), "mk2": _sb(GH, B), "tuc": _sb(16, U), "bd0": _sb(128, B), "nl": _sb(512 + 4544, F),
    "sl": _sb(2 * 768, F), "sl16": _sb(512, H), "slr": _sb(512, F),
    "gb": _sb(8192, B), "gm": _sb(4096, B), "mx": _sb(8192, B), "selt": _sb(2048, B), "nz": _sb(512, B), "xg": _sb(128, F),
    "plci": _sb(112, I), "plcj": _sb(224, I), "plch": _sb(224, H), "plcu": _sb(112, U), "junk": _sb(256, F),
    "acc": _sb(4, F), "cf": _sb(4, F), "uq": _sb(4, H), "pq": _sb(32, F), "posl": _sb(32, H), "id16": _sb(112, H), "r0": _sb(16, F),
    "prm": _sb(16, I), "prmf": _sb(8, F), "par": _sb(8, F), "col": _sb(80, F), "pint": _sb(8, I),
    "yb": _sb(144, B), "y0": _sb(144, B), "y123": _sb(144, B), "y01": _sb(144, B), "yrk": _sb(144, B),
    "ycl": _sb(144, B), "ypos": _sb(144, B), "ynl": _sb(144, B),
    "bd": _sb(128, B), "bdn": _sb(128, B), "bd2": _sb(128, B), "bd16": _sb(128, B), "msk": _sb(128, B), "mcl": _sb(128, B),
    "i16": _sb(128, B), "ineg": _sb(128, B), "ibias": _sb(128, B), "ih": _sb(128, B),
    "i0": _sb(128, B), "i8k": _sb(128, B), "ic": _sb(384, B), "mh0": _sb(128, B),
    "e8": _sb(128, F), "us": _sb(128, B), "usn": _sb(128, B), "ones": _sb(256, B), "mv0": _sb(256, B), "mv1": _sb(256, B),
    "rm": _sb(96, B), "rm4": _sb(128, B),
    "jl": _sb(48, F), "c16": _sb(48, F), "dl": _sb(48, H), "u0": _sb(16, F), "d2k": _sb(32, F),
    "oc": _sb(4, F), "eq": _sb(16, F), "le": _sb(16, F), "ge": _sb(16, F), "xu": _sb(16, F),
    "ns": _sb(4, F), "cnt": _sb(8, H), "cnf": _sb(8, F), "sc": _sb(16, F), "bi": _sb(4, I), "bm": _sb(4, I), "bf": _sb(4, F),
    "pr": _sb(16, I), "ps": _sb(16, I), "posu": _sb(16, U),
    "dr": _sb(512, H), "rec": _sb(512, F), "tu": _sb(32, U), "nbm": _sb(256, U), "nbu": _sb(512, U),
    "t1": _sb(32, F), "oldm": _sb(256, B), "rr": _sb(256, B), "rkd": _sb(256, B), "rk": _sb(512, B), "pu": _sb(16, U), "rku": _sb(32, U),
    "su": _sb(32, U), "sf": _sb(64, F), "sv": _sb(512, B), "sg": _sb(528, B),
    "ne": _sb(96, H), "rq": _sb(192, F), "pp": _sb(96, F), "v18": _sb(32, H), "sa": _sb(96, H), "nq": _sb(8, F), "nqh": _sb(8, H),
    "ai": _sb(4, I), "af": _sb(16, F), "tq": _sb(240, F), "bb": _sb(96, H), "rx": _sb(144, F), "tpu": _sb(48, U),
    "tb": _sb(PT, F), "tbh": _sb(PT, H), "d1h": _sb(32, H),
    "tbu": _sb(48, U), "ri": _sb(PT, B), "riu": _sb(48, U), "tg": _sb(PT, B), "tx": _sb(144, H), "itu": _sb(48, U),
    "fl": _sb(192, H), "s1": _sb(192, H), "zz": _sb(96, F), "ho": _sb(96, H), "hs": _sb(96, H), "o3": _sb(128, F), "ihu": _sb(32, U),
    "vv": _sb(128, F), "o4": _sb(128, F), "lv": _sb(96, F), "jou": _sb(32, U), "lvu": _sb(32, U), "hv": _sb(96, F), "hou": _sb(32, U),
    "occ": _sb(512, H), "hf": _sb(512, F), "nrec": _sb(512, F), "stu": _sb(32, U), "lg": _sb(16, F),
    "pS": ("psum", [128, 512], F), "pE": ("psum", [128, 512], F), "pF": ("psum", [128, 512], F), "pG": ("psum", [128, 512], F),
    "pA": ("psum", [128, 512], F), "pB": ("psum", [128, 512], F), "pC": ("psum", [128, 512], F), "pD": ("psum", [128, 512], F),
}
SCRATCH = {}
PLACE = {}
for _n, (_w, _s, _d) in BUF.items():
    if _w == "sbuf" and _s[1] <= 288:
        _at = SCRATCH.get("tiles_" + _d, (0, [0, 0]))[1][1]
        PLACE[_n] = ("tiles_" + _d, _at)
        SCRATCH["tiles_" + _d] = _sb(_at + (_s[1] + 15) // 16 * 16, _d)
    else:
        PLACE[_n] = (_n, 0)
        SCRATCH[_n] = (_w, _s, _d)
DMAS = 16
SEMAPHORES = ["cv", "cs", "ct", "cg", "sent0", "sent"] + ["came%d" % k for k in range(4)] + ["dma%d" % k for k in range(DMAS)]


def r(name, c0=0, c1=None, step=1, p=(0, 128), off=None):
    if c1 is None:
        c1 = BUF[name][1][1]
    buf, at = PLACE[name]
    return ("ref", buf, at + c0, at + c1, step, p, off)


def c(name, k):
    return r(name, k, k + 1)


def is_ref(a):
    return isinstance(a, tuple) and len(a) == 7 and a[0] == "ref"


def width(a):
    return 16 * width(a[6]) if a[6] is not None else (a[3] - a[2] + a[4] - 1) // a[4]


def depend(ops, banks):
    def meet(a, b):
        return SCRATCH[a[1]][0] == "psum" or (a[2] < b[3] and b[2] < a[3] and not (a[4] == b[4] > 1 and (a[2] - b[2]) % a[4]))
    acc = {}
    deps = []
    for k, o in enumerate(ops):
        d = set()
        both = [(a, False) for a in o["rd"]] + [(a, True) for a in o["wr"]]
        for a, wr in both:
            psum = SCRATCH[a[1]][0] == "psum"
            for j, b, bw in acc.get(a[1], []):
                e = ops[j]["q"]
                if not meet(a, b) or (e == "t" and o["q"] == "t" and (not banks or o["kind"] == ops[j]["kind"] == "free")):
                    continue
                if wr or bw or (psum and e != o["q"]):
                    d.add(j)
        for a, wr in both:
            l = acc.setdefault(a[1], [])
            if wr and SCRATCH[a[1]][0] == "psum":
                if o["kind"] != "free" or not banks:
                    l[:] = [x for x in l if x[0] == k]
            elif wr and a[4] == 1 and a[6] is None and a[5] == (0, 128):
                l[:] = [x for x in l if x[0] == k or not (a[2] <= x[1][2] and x[1][3] <= a[3])]
            l.append((k, a, wr))
        deps.append(d)
    return deps


CY, WAKE, GATHER, SCATTER, SEND = 0.9, 200.0, 1.4, 2.8, 2000.0


def cost(q, kind, args, rd, wr):
    two = lambda a: SCRATCH[a[1]][2] in (B, H, U)
    if kind == "send":
        x = SEND if rd[0][1] == "w" else 0.0
        return 900.0 + x, SEND + x + 640 + 4.3 * width(rd[0])
    if kind == "land":
        return 0.0, 0.0
    if kind == "dma":
        a = (wr + rd)[0]
        x = width(a) * (2 if two(a) else 4) * 0.45 * (a[5][1] - a[5][0]) / 128
        return 100 + (x if q == "y" else 0), 1500 + x
    n = width(args[1] if kind == "red" else wr[0])
    if q == "t":
        x = max(64, n) * CY / 2 * (1 if two(args[2]) else 4)
    elif q == "g":
        x = 150 + 2 * CY * n
    elif wr[0][6] is not None:
        x = 60 + SCATTER * CY * n
    elif any(a[6] is not None for a in rd):
        x = 60 + GATHER * CY * n
    elif q == "s":
        x = 65 + CY * n + (1300 if kind == "table" else 0)
    elif kind == "tt":
        x = CY * max(64, n * (2 if all(SCRATCH[a[1]][0] == "sbuf" for a in args[1:3]) else 1))
    else:
        x = CY * max(64, n * (0.5 if kind != "red" and all(two(a) for a in rd + wr if width(a) == n) else 1))
    return x, x


def schedule(ops):
    n = len(ops)
    before = [{} for _ in ops]
    last = {}
    rounds = [{}]
    for k, (o, d) in enumerate(zip(ops, depend(ops, True))):
        for j in d:
            before[k][j] = ops[j]["cost"][1] + (0.0 if o["q"] == ops[j]["q"] == "t" else WAKE)
        if o["kind"] in ("send", "land", "post") and "send" in last:
            j = last["send"]
            before[k][j] = max(before[k].get(j, 0.0), ops[j]["cost"][o["kind"] == "land"])
        if o["kind"] == "dma" and o["q"] in last:
            j = last[o["q"]]
            before[k][j] = max(before[k].get(j, 0.0), ops[j]["cost"][0])
        last[o["q"] if o["kind"] == "dma" else o["kind"]] = k
        if o["wr"] and o["kind"] != "dma":
            a = o["wr"][0]
            name = max((at, x) for x, (b, at) in PLACE.items() if b == a[1] and at <= a[2])[1] + ("@" if a[6] else "")
            if name == "dr" and o["rd"][0][6] is not None:
                rounds.append({})
            rounds[-1].setdefault(o["q"] + name, []).append(k)
    for q, lists in QUEUES.items():
        chain = []
        for t, names in enumerate(lists):
            for x in names.split():
                name, _, part = x.lstrip("-").partition("#")
                calls = rounds[t + (x[0] != "-")].get(q + name, [])
                if part:
                    a, _, b = part.partition(":")
                    calls = calls[int(a):int(b) if b else int(a) + 1]
                chain += [k for k in calls if k not in chain]
        for j, k in zip(chain, chain[1:]):
            before[k][j] = max(before[k].get(j, 0.0), ops[j]["cost"][0])
    order = []
    waiting = [len(b) for b in before]
    after = [[] for _ in ops]
    for k in range(n):
        for j in before[k]:
            after[j].append(k)
    order = [k for k in range(n) if not waiting[k]]
    for j in order:
        for k in after[j]:
            waiting[k] -= 1
            if not waiting[k]:
                order.append(k)
    left = [o["cost"][1] for o in ops]
    for k in reversed(order):
        for j, x in before[k].items():
            left[j] = max(left[j], x + left[k])
    pos = {k: i for i, k in enumerate(order)}
    busy = {q: ([], []) for q in "vstgye"}
    start = [0.0] * n
    for k in sorted(range(n), key=lambda k: (-left[k], pos[k])):
        hold = ops[k]["cost"][0]
        t = max([start[j] + x for j, x in before[k].items()] + [0.0])
        a, b = busy[ops[k]["q"]]
        lo, hi = 0, len(b)
        while lo < hi:
            if b[(lo + hi) // 2] <= t:
                lo = (lo + hi) // 2 + 1
            else:
                hi = (lo + hi) // 2
        while lo < len(a) and t + hold > a[lo]:
            t = max(t, b[lo])
            lo += 1
        a.insert(lo, t)
        b.insert(lo, t + hold)
        start[k] = t
    return sorted(range(n), key=lambda k: (start[k], pos[k]))


ORDERS = {}


def emit(g, T, ops, deps):
    def ap(a):
        if not is_ref(a):
            return a
        _, name, c0, c1, step, p, off = a
        t = T[name]
        x = t[p[0]:p[1], c0:c1] if step == 1 else t[p[0]:p[1], c0:c1:step]
        return x.indirect(ap(off)) if off is not None else x
    known = {q: {} for q in "vstgye"}
    after = [None] * len(ops)
    waits = []
    for k, o in enumerate(ops):
        kn = known[o["q"]]
        need = {}
        for j in sorted(deps[k], reverse=True):
            key = ops[j]["ev"] or ops[j]["q"]
            if kn.get(key, -1) >= j:
                continue
            need[key] = j
            for x, y in after[j].items():
                if kn.get(x, -1) < y:
                    kn[x] = y
        waits.append(sorted(need.values()))
        after[k] = dict(kn)
        after[k][o["ev"] or o["q"]] = k
    marked = set(j for w in waits for j in w)
    Q = {"v": g.vector, "s": g.scalar, "t": g.tensor, "g": g, "y": g.sync, "e": None}
    count = {q: 0 for q in "vstg"}
    val = {}
    top = {}
    for k, o in enumerate(ops):
        q = Q[o["q"]]
        for j in waits[k]:
            q.wait_ge(*val[j])
        ins = o["fn"](q, [ap(a) for a in o["args"]], {x: ap(y) for x, y in o["kw"].items()})
        if o["ev"]:
            val[k] = (T.sem[o["ev"][0]], o["ev"][1])
            top[o["ev"][0]] = o["ev"][1]
            if o["ev"][2]:
                ins.then_inc(*val[k])
        elif k in marked:
            count[o["q"]] += 1
            val[k] = (T.sem["c" + o["q"]], count[o["q"]])
            top["c" + o["q"]] = count[o["q"]]
            ins.then_inc(val[k][0], 1)
    for s, v in top.items():
        g.sync.wait_ge(T.sem[s], v)


def rank_program(g, core, T, topo):
    rank = T.rank_of(core)
    if rank is None:
        return
    ops = []

    def op(q, fn, args, kw, rd, wr, ev=None, kind=None):
        rd = [a for a in rd if is_ref(a)]
        x = cost(q, kind, args, rd, wr)
        rd += [a[6] for a in rd + wr if a[6] is not None]
        ops.append({"q": q, "fn": fn, "args": args, "kw": kw, "rd": rd, "wr": wr, "ev": ev, "kind": kind, "cost": x})

    def ts(o, i, s1, o1, s2=None, o2=None):
        if o2 is None:
            op("v", lambda q, a, k: q.tensor_scalar(a[0], a[1], a[2], None, o1), [o, i, s1], {}, [i, s1], [o], kind="ts")
        else:
            op("v", lambda q, a, k: q.tensor_scalar(a[0], a[1], a[2], a[3], o1, o2), [o, i, s1, s2], {}, [i, s1, s2], [o], kind="ts")

    def tt(o, x, y, f):
        op("v", lambda q, a, k: q.tensor_tensor(a[0], a[1], a[2], f), [o, x, y], {}, [x, y], [o], kind="tt")

    def cp(o, i):
        op("v", lambda q, a, k: q.tensor_copy(a[0], a[1]), [o, i], {}, [i], [o])

    def ms(o, v):
        op("v", lambda q, a, k: q.memset(a[0], v), [o], {}, [], [o])

    def red(o, i):
        op("v", lambda q, a, k: q.tensor_reduce(a[0], a[1], AX.X, A.add), [o, i], {}, [i], [o], kind="red")

    def scan(o, d0, d1, o0, o1):
        op("v", lambda q, a, k: q.tensor_tensor_scan(a[0], a[1], a[2], 0.0, o0, o1), [o, d0, d1], {}, [d0, d1], [o])

    def cum(o, d):
        scan(o, d, d, A.add, A.max)

    def act(o, i, f=AF.Identity, **kw):
        op("s", lambda q, a, k: q.activation(a[0], a[1], f, **k), [o, i], kw, [i, kw.get("bias"), kw.get("scale")],
           [o] + ([kw["accum_out"]] if "accum_out" in kw else []), kind="table" if f == AF.Silu and o[6] is None else None)

    def lin(o, i, scale=1.0, bias=0.0):
        act(o, i, scale=scale, bias=bias)

    def take(e, o, i):
        (cp if e == "v" else act)(o, i)

    def mm(o, l, x, st=True, sp=True):
        op("t", lambda q, a, k: q.matmul(a[0], a[1], a[2], st, sp), [o, l, x], {}, [l, x], [o], kind=None if st or sp else "free")

    def iota(o, pat, base, cm, kind="post"):
        fl = {"allow_small_or_imprecise_dtypes": True} if SCRATCH[o[1]][2] != I else {}
        op("g", lambda q, a, k: q.iota(a[0], pat, base, cm, **fl), [o], {}, [], [o], kind=kind)

    def keep(o, i, pat, how, fill, base, cm):
        op("g", lambda q, a, k: q.affine_select(a[0], a[1], pat, how, fill, base, cm), [o, i], {}, [i], [o], kind="post")
    nd = [0]

    def dma(o, i, q="y", after=None):
        nd[0] += 1
        op(q, lambda e, a, k: e.dma_start(a[0], a[1]), [o, i], {}, [i, after], [o] if is_ref(o) else [], ("dma%d" % (nd[0] - 1), 16, True), "dma")

    def tolist(ps, c0, y, src, n, first=True, at=0):
        for a in range(16):
            mm(r(ps, c0, c0 + n // 16), r(y, 15 - a, 143 - a), r(src, at + a, at + n, 16), first and a == 0, a == 15)

    peers = [T.cores[(rank + d) % N] for d in range(1, N)]
    mine = topo.cores_of(core)
    far = [p for p in peers if p not in mine]
    far_e = topo.engines(core, far[0])
    share = len(far_e) // len(far)
    masks = {p: sum(1 << e for e in far_e[k * share:(k + 1) * share]) for k, p in enumerate(far)}
    near_n = 0
    for p in peers:
        if p in mine:
            near_e = [e for e in topo.engines(core, p) if e not in far_e]
            masks[p] = sum(1 << e for e in near_e)
            near_n = len(near_e)
    total_e = near_n + share * len(far)

    def w(t, a, b, **k):
        return r("w", WS * t + a, WS * t + b, **k)

    def exchange(k, src, lsem, lval):
        def fn(q, a, kw):
            tr = []
            for d, p in enumerate(peers):
                rid, pid = topo.addr(p, core)
                tr.append(RemoteDMATransfer(dst_ids=[DstId(rid=rid, pnc=pid)], dma_engine_mask=masks[p],
                                            remote_sem=T.sem["came%d" % k], src=a[0], dst=a[1 + d]))
            return q.remote_dma_fused(tr, local_sem=T.sem[lsem])
        op("g", fn, [src] + [w(k, S1 + d * GH, S1 + (d + 1) * GH) for d in range(N - 1)], {}, [src], [], (lsem, lval, False), "send")
        op("e", lambda q, a, kw: None, [], {}, [], [w(k, S1, WS)], ("came%d" % k, total_e, False), "land")

    (P, AK, G15, G16, P16, K0, K1, K2, K3, K4, K5, K6, K7, K8, K9, K01, K02, K12, K23, K45, K26, K78, K123, RS, RB, R0, RF, RN, MN, US,
     WC, WP, THB, MG, CL, QM, QQ, QR, Q13, BS, BD, KB, WN, MA, MB, MC,
     X0, X1, X2, X3, X4, X5, X6, X7, X8, X9, X10, X11, X12, X13, X14, X15, X16, X17, X18, X19, X20, X21, X22) = range(69)
    FLAG = {K0: ("eq", 0), K1: ("eq", 1), K2: ("eq", 2), K3: ("eq", 3), K4: ("eq", 4), K5: ("eq", 5), K6: ("eq", 6), K7: ("eq", 7),
            K8: ("eq", 8), K9: ("eq", 9), K01: ("le", 1), K02: ("le", 2)}
    K = lambda k: c(*FLAG.get(k, ("col", k)))

    dma(w(0, O, O + GH), T.x[:, 0:GH])
    ms(w(0, 0, O), 0.0)
    dma(r("plci"), T.plc[:, :], "s")
    dma(r("prm", 4, 7, p=(0, 8)), T.sd[:, :], "s")
    dma(r("prm", 0, 2, p=(0, 8)), T.th[:, :], "s")
    dma(r("nbi", O, S1), T.nb[:, :])
    dma(w(0, O + GH, S1), T.x[:, GH:V])
    iota(r("si", 0, 256), [[1, 256]], 0, 0, None)
    iota(c("pint", 0), [[0, 1]], 0, 1, None)
    iota(r("xg"), [[16, 8], [0, 16]], 0, 0, None)
    iota(r("si", 1280, V), [[1, 512]], 1280, 0, None)
    exchange(0, w(0, O, O + GH), "sent0", total_e)
    dma(r("pub", O, O + GH), T.x[:, 0:GH], after=w(0, S1, WS))
    dma(w(1, 0, S1), w(0, 0, S1))
    ms(r("bag", B0 + 2 * V - PT, B0 + 2 * V), 0.0)
    ms(r("bag", B0 - 16, B0), 0.0)
    ms(r("bag", B0 + V - 16, B0 + V), 0.0)
    ms(r("ones"), 1.0)
    iota(r("nbi", 0, O), [[2, O]], V, 0)
    if SELV < 4:
        ms(r("nz"), 1.0)
        ms(r("nz", 0, 512, 16), 0.0)
    for b in range(SELV, 4):
        keep(r("selt", 512 * b, 512 * b + 512), r("nz"), [[-1, 4], [-16, 8], [0, 16]], A.is_equal, 0.0, -4 * b, 1)
    iota(r("plt", S1, S1 + 512), [[0, 512]], 0, 0)
    iota(r("sl", 0, 512), [[0, 512]], 0, 0)
    act(r("si", V, 2048), r("si", 0, 256), AF.Silu, bias=float(V))
    ts(r("si", 256, 512), r("si", 0, 256), 256.0, A.add)
    ts(c("pint", 1), c("pint", 0), 15, A.bitwise_and)
    cp(K(P), c("pint", 0))
    ts(r("si", 512, 768), r("si", 0, 256), 512.0, A.add)
    cp(K(AK), c("pint", 1))
    ts(r("si", 768, 1280), r("si", 0, 512), 768.0, A.add)
    ts(r("eq"), r("si", 0, 16), K(AK), A.is_equal)
    ts(r("le"), r("si", 0, 16), K(AK), A.is_ge)
    ts(r("ge"), r("si", 0, 16), K(AK), A.is_le)
    ts(K(G16), K(P), K(AK), A.subtract)
    ts(K(P16), K(P), 16.0, A.mult)
    ts(r("e8", p=(0, 8)), r("xg", p=(0, 8)), r("col", P16, P16 + 1, p=(0, 8)), A.is_equal)
    ts(r("bd"), r("xg"), K(G16), A.is_equal)
    if SELV:
        cp(r("bd0"), r("bd"))
        ms(r("bd0", 0, 128, 16), 0.0)
    for a in range(4 * SELV):
        ts(r("selt", 128 * a, 128 * a + 128), r("bd0"), c("eq", a), A.mult)
    ts(r("xu"), r("si", 0, 16), 1 / 16, A.mult)
    ts(K(KB), K(K2), -1024.0, A.mult)
    for o in [r("mk", 512 * k, 512 * k + 512) for k in range(4)] + [r("mkp")]:
        ts(o, w(0, O, O + GH), 0.0, A.mult, K(KB), A.add)
    cp(r("plcu"), r("plci"))
    act(r("bag", B0, PL, off=r("plcu")), r("si", O, S1), AF.Silu)
    act(r("bag", PL, PL + 256), r("si", 0, 256))
    cp(r("prmf", 2, 5, p=(0, 8)), r("prm", 4, 7, p=(0, 8)))
    cp(r("prmf", 0, 2, p=(0, 8)), r("prm", 0, 2, p=(0, 8)))
    ts(r("junk", 0, 112), r("plci"), float(V), A.is_ge)
    ts(r("junk", 112, 224), r("plci"), float(2 * V), A.is_ge)
    red(c("cnf", 0), r("junk", 0, 112))
    red(c("cnf", 1), r("junk", 112, 224))
    ts(c("cnt", 0), c("cnf", 0), -1.0, A.mult, 112.0, A.add)
    ts(c("cnt", 1), c("cnf", 0), c("cnf", 1), A.subtract)
    cp(c("cnt", 2), c("cnf", 1))
    for h, m in enumerate((8128, 63)):
        ts(r("plcj", 112 * h, 112 * h + 112), r("plci"), m, A.bitwise_and)
    cp(r("plch"), r("plcj"))
    ts(K(G15), K(P), K(AK), A.subtract, 15.0, A.add)
    ts(c("oc", 0), c("ge", 4), -1.0, A.mult, 1.0, A.add)
    ts(c("oc", 1), c("ge", 4), c("ge", 8), A.subtract)
    cp(c("oc", 2), c("ge", 8))
    ts(K(CL), c("ge", 4), c("ge", 8), A.add)
    ts(K(QM), c("ge", 8), 1.0, A.add)
    ts(K(QQ), c("ge", 8), 64.0, A.mult, 64.0, A.add)
    ts(K(QR), c("ge", 8), -0.5, A.mult, 1.0, A.add)
    ts(K(Q13), c("ge", 8), 13.0, A.mult, 13.0, A.add)
    ts(K(BS), K(CL), float(V), A.mult, float(B0), A.add)
    ts(K(BD), K(CL), 64.0 - V, A.mult, 3.0 * V, A.add)
    ts(K(X7), K(CL), -4.0, A.mult, K(AK), A.add)
    ts(r("u0"), r("xu"), K(X7), A.add, 1024.0, A.mult)
    mm(r("pC", 4, 9), r("e8", p=(0, 8)), r("prmf", 0, 5, p=(0, 8)))
    tt(r("sc", 4, 7), r("pC", 6, 9), r("oc", 0, 3), A.mult)
    cp(r("par", 0, 2), r("pC", 4, 6))
    red(c("sc", 8), r("sc", 4, 7))
    mm(r("pB", 0, 3), r("bd"), r("cnt", 0, 3))
    for t in range(RO):
        ts(c("sc", 9 + t), c("sc", 8), 41.0 * t, A.add, K(QM), A.mult)

    def draw(t, sizes):
        ts(c("bi", 0), sizes[:2] + (sizes[2], sizes[2] + 1) + sizes[4:], K(Q13), A.mult, c("sc", 9 + t), A.add)
        tt(r("sc", 0, 3), sizes, r("oc", 0, 3), A.mult)
        cp(r("ns", 0, 3), sizes)
        ts(c("bm", 0), c("bi", 0), 63, A.bitwise_and)
        red(c("sc", 3), r("sc", 0, 3))
        cp(c("bf", 0), c("bm", 0))
        ts(c("bf", 1), c("sc", 3), K(QQ), A.max, K(QR), A.mult)
        ts(c("bf", 2), c("sc", 3), K(QQ), A.is_lt, K(BD), A.mult)
        ts(r("pr"), r("u0"), c("bf", 0), A.add, c("bf", 1), A.mult)
        ts(r("ps"), r("pr"), 12, A.arith_shift_right)
        ts(r("posu"), r("ps"), c("bf", 2), A.add, K(BS), A.add)
    draw(0, r("pB", 0, 3))
    ts(r("mv0"), r("ones"), K(K0), A.mult)
    ts(r("mv1"), r("ones"), K(K1), A.mult)
    lin(r("nl", 0, 512), r("si", 0, 512), 2.0, 2048.0)
    lin(r("plt", 0, O), r("si", 0, O), K(K0))
    lin(K(X10), K(K0), -0.5)
    lin(r("mks", S1, S1 + 512), r("si", 0, 512), K(X10))
    keep(r("rm"), r("ones", 0, 96), [[0, 3], [1, 32]], A.not_equal, 0.0, 0, 0)
    keep(r("rm4"), r("ones", 0, 128), [[0, 32], [1, 4]], A.not_equal, 0.0, 0, 0)
    lin(K(K12), K(K1), 1.0, K(K2))
    lin(K(K78), K(K7), 1.0, K(K8))
    lin(K(X0), K(K12), 1.0, K(K78))
    lin(K(X17), K(K9), 1.0, K(K3))
    lin(K(X12), K(X0), SC, K(X17))
    lin(K(RS), K(X12), 1.0, K(K0))
    lin(K(X1), K(K2), -4096 * SC)
    lin(K(X18), K(K1), -2048 * SC, K(X1))
    lin(K(X3), K(K6), SC, K(X18))
    lin(K(X2), K(K7), -(B0 + V - 1) * SC, K(X3))
    lin(K(RB), K(K8), -(B0 + 2 * V - 1) * SC, K(X2))
    lin(K(R0), K(RS), float(B0), K(RB))
    lin(K(RN), K(X12), float(V + B0), K(RB))
    lin(K(RF), K(K9), -float(B0), K(RN))
    lin(K(X8), K(K7), -1.0, K(K6))
    lin(K(X9), K(K8), -1.0, K(K7))
    lin(c("cf", 0), K(X8), 1 / 16)
    lin(c("cf", 1), K(X9), 1 / 16)
    lin(K(MG), K(K9), -float(B0), MAGIC)
    lin(K(US), K(X0), 1 / SC - 1, 1.0)
    lin(K(MN), K(K78), -2047.0, 2048.0)
    lin(K(WC), K(K6), 4 / SC, K(K78))
    lin(K(K123), K(K12), 1.0, K(K3))
    lin(K(X14), K(K3), 1.0, K(K6))
    lin(K(X13), K(X0), SC, K(X14))
    lin(K(X4), K(K123), 1 / 4096)
    lin(K(X5), K(K6), -B0 / 4096 / SC, K(X4))
    lin(K(WP), K(K78), -V / 4096, K(X5))
    lin(K(K23), K(K2), 1.0, K(K3))
    lin(K(K45), K(K4), 1.0, K(K5))
    lin(K(K26), c("le", 6), -BIG, 0.5)
    lin(K(X6), K(K01), BIG, K(K26))
    ts(c("lg", 0), c("par", 0), c("par", 1), A.min, K(K23), A.mult)
    ts(c("lg", 1), c("par", 0), c("par", 1), A.max, K(K45), A.mult)
    lin(c("lg", 2), c("par", 0), K(K0), c("lg", 0))
    lin(c("lg", 3), c("par", 1), K(K1), c("lg", 1))
    lin(c("lg", 4), c("lg", 2), -1.0, K(X6))
    lin(K(THB), c("lg", 3), -1.0, c("lg", 4))
    lin(K(X19), K(K7), -BIG)
    lin(K(MA), K(K6), BIG / SC, K(X19))
    lin(K(MB), K(X9), BIG)
    lin(K(MC), K(K8), BIG)
    lin(r("msk"), r("bd"), 0.0)
    for k, m in ((2, MA), (6, MA), (3, MB), (4, MB), (5, MC)):
        lin(r("msk", k, 128, 16), r("bd", k, 128, 16), K(m))
    lin(K(X20), K(K5), 1.0, K(X14))
    lin(K(X11), K(K2), -1.0, K(X20))
    lin(K(X21), K(K4), -1.0, K(X11))
    lin(K(X16), K(K7), 1.0, K(X21))
    lin(K(WN), K(X16), 0.5)
    lin(K(X15), K(K7), 2.0)
    lin(r("sg", 512, 528), r("ones", 0, 16), K(X15))
    ts(r("yb"), r("si", 0, 144), K(G15), A.is_equal)
    ts(r("y0"), r("yb"), K(K0), A.mult)
    ts(r("yrk"), r("yb"), K(K02), A.mult, -1.0, A.mult)
    for nme, k in (("y01", K01), ("y123", K123), ("ycl", WC), ("ypos", WP), ("ynl", WN)):
        lin(r(nme), r("yb"), K(k))
    ts(r("ih"), r("si", 0, 128), K(P), A.is_equal)
    for nme, v in (("i16", 1 / 16), ("ineg", -1.0), ("ibias", -15 / 32), ("i0", K(K0))):
        ts(r(nme), r("ih"), v, A.mult)
    lin(r("mh0"), r("ih"), K(X13))
    for o, v in [(r("i8k"), 8192.0)] + [(r("ic", 128 * k, 128 * k + 128), 1536.0 + NB * k) for k in range(3)]:
        keep(o, w(0, 0, 128), [[-1, 128]], A.not_equal, v, 0, 1)
    for nme, v in (("bd2", 2.0), ("bd16", -16.0), ("bdn", -1.0)):
        lin(r(nme), r("bd"), v)
    keep(r("usn"), r("bd"), [[-1, 128]], A.is_gt, 0.0, 0, 1)
    keep(r("us"), r("bdn"), [[-1, 128]], A.is_gt, 0.0, 0, 1)
    lin(K(X22), K(K01), V / 2)
    lin(r("mcl"), r("bd"), K(X22))
    lin(r("mcl", 0, 128, 16), r("bd", 0, 128, 16), 0.0)
    lin(r("jl", 0, 34), r("si", 0, PT, 16), 1.0, K(AK))
    lin(r("d2k"), r("jl", 0, 32), 1.0, 2048.0)
    ts(r("d1h"), r("jl", 0, 32), 1024.0, A.add)
    ts(r("dl", 0, 34), r("jl", 0, 34), 2.0, A.mult, 3.0 * NB, A.add)
    iota(r("c16", 0, 34), [[16, 34]], 0, 0)
    lin(r("vv", 0, 128, 4), r("jl", 0, 32))
    ts(r("id16"), r("si", 0, 112), 16.0, A.mult, float(O - B0), A.add)
    lin(r("r0"), r("si", 0, 16), K(K0), K(R0))

    def places(b):
        o = lambda a: r(("pS", "pE")[b % 2], 112 * a, 112 * a + 112)
        for a in range(4):
            mm(o(a), r("i0"), r("id16"), True, False)
            for h in range(2):
                mm(o(a), r("selt", 128 * (4 * b + a), 128 * (4 * b + a) + 128), r("plch", 112 * h, 112 * h + 112), False, h == 1)
        for a in range(4):
            act(r("plt", O + 4 * b + a, S1, 16), o(a), AF.Relu, scale=K(RS), bias=c("r0", 4 * b + a))

    for t in range(RO):
        final = t == RO - 1
        mk = lambda a, b, u=t, **k: r("mk", 2560 * (u % 2) + a, 2560 * (u % 2) + b, **k)
        sl = lambda n=512, a=0, u=t, **k: r("sl", 768 * (u % 2) + a, 768 * (u % 2) + n, **k)
        z = lambda n, k, o=0: r(n, o + 32 * k, o + 32 * k + 32)
        y = lambda n, k: r(n, 48 * k, 48 * k + 34)
        cp(r("dr", 0, 256), r("bag", off=r("posu")))
        tolist("pA", 0, "y0", "dr", 256)
        cp(r("tu", 0, 16), r("pA", 0, 16))
        for a, b in ((0, CUTM), (CUTM, 16)):
            cp(r("nbm", 16 * a, 16 * b), r("nbi", off=r("tu", a, b)))
        act(r("oldm"), w(t, 0, S1, off=r("tu", 0, 16)), bias=-192.0)
        for j0, j1, e in MOVES[t > 0]:
            take(e, r("gm", 16 * j0, 16 * j1), w(t, O, WS, off=r("nbm", j0, j1)))
        mm(r("pF", 0, 256), r("ibias"), r("ones"), True, False)
        mm(r("pF", 0, 256), r("ineg"), r("oldm"), False, False)
        for j0, j1 in SUMS[t > 0]:
            for i in range(16):
                mm(r("pF", j0, j1), r("i16"), r("gm", 16 * j0 + i, 16 * j1, 16), False, i == 15 and (j0, j1) == SUMS[t > 0][-1])
        ts(r("rr"), r("pF", 0, 256), 188 - 15 / 32, A.max, 196 - 15 / 32, A.min)
        cp(mk(0, 2048, off=r("tu", 0, 16)), r("mv0"))
        cum(r("mk2"), mk(O, O + GH))
        ts(r("tuc"), r("pA", 0, 16), -float(O), A.add, GH - 1.0, A.min)
        take(ENG["rkd"], r("rkd"), r("mk2", off=r("tuc")))
        ts(r("dr", 256, 512), r("nbm"), float(O), A.add)
        tolist("pB", 0, "y0", "rkd", 256)
        tolist("pC", 0, "y0", "dr", 256, at=256)
        ts(r("t1", 0, 16), r("pB", 0, 16), float(CAP), A.is_gt, 2048.0, A.mult)
        tt(r("t1", 16, 32), r("t1", 0, 16), r("pA", 0, 16), A.add)
        cp(r("pu"), r("t1", 16, 32))
        tt(r("pub", off=r("pu")), r("rr"), r("oldm"), A.add)
        exchange(t + 1, r("pub", O, O + GH), "sent", total_e * (t + 1))
        tt(w(t + 1, 0, S1, off=r("tu", 0, 16)), r("rr"), r("oldm"), A.add)
        if not final:
            for k in range(4):
                keep(mk(512 * k, 512 * k + 512, t + 1), r("mkp"), [[0, 512]], A.is_equal, 0.0, 0, 0)
            iota(sl(u=t + 1), [[0, 512]], 0, 0)
            dma(w(t + 2, 0, S1), w(t + 1, 0, S1), after=w(t + 1, S1, WS))
        else:
            dma(T.yx[:, :], w(RO, O, S1), after=w(RO, S1, WS))
        if t == 0:
            for b in range(4):
                places(b)
        cp(r("tu", 16, 32), r("pC", 0, 16))
        cp(mk(0, 2560, off=r("tu", 16, 32)), r("mv1"))
        cum(r("mks", 0, S1), mk(0, S1))
        for h in (1, 0):
            act(r("rec", 256 * h, 256 * h + 256), r("plt", off=r("tu", 16 * h, 16 * h + 16)))
        act(r("junk"), r("rec", 256, 512), AF.Sign, accum_out=c("acc", 0))
        ts(r("uq", 0, 2), r("cf", 0, 2), c("acc", 0), A.mult)
        mm(r("pC", 0, 2), r("bd"), r("uq", 0, 2))
        lin(r("af", 8, 10), r("ns", 0, 2), 1 / 16, -4.0)
        for k in range(2):
            ts(c("ai", k), c("pC", k), c("af", 8 + k), A.min, (64 + 7.5) / 16, A.add)
        ts(c("af", 0), c("ns", 1), c("ns", 0), A.subtract, float(V), A.add)
        ts(c("af", 1), c("ns", 2), c("ns", 1), A.subtract, float(V), A.add)
        ts(c("af", 2), c("ns", 0), B0 - 1.0, A.add)
        ts(y("tq", 0), y("jl", 0), -1.0, A.mult, c("af", 2), A.add)
        ts(c("af", 4), c("ai", 0), 16.0, A.mult)
        ts(c("af", 6), c("ai", 0), 16.0, A.mult, c("af", 0), A.add)
        ts(c("af", 7), c("ai", 1), 16.0, A.mult, c("af", 1), A.add)
        ts(c("af", 5), c("ai", 1), 16.0, A.mult, c("af", 4), A.add)
        ts(y("tq", 1), y("jl", 0), c("af", 4), A.is_ge, c("af", 6), A.mult)
        ts(y("tq", 2), y("jl", 0), c("af", 5), A.is_ge, c("af", 7), A.mult)
        tt(y("tq", 3), y("tq", 0), y("tq", 1), A.add)
        tt(y("tq", 4), y("tq", 3), y("tq", 2), A.add)
        cp(y("tpu", 0), y("tq", 4))
        cp(r("tbh"), r("bag", off=y("tpu", 0)))
        act(r("tb"), r("bag", off=y("tpu", 0)))
        tolist("pC", 0, "y0", "tbh", PT)
        cp(y("tbu", 0), r("pC", 0, 34))
        take(ENG["ri"], r("ri"), r("mks", 0, S1, off=y("tbu", 0)))
        for h, e in enumerate(RANK):
            take(e, r("rk", 256 * h, 256 * h + 256), r("mks", off=r("tu", 16 * h, 16 * h + 16)))
        tolist("pG", 0, "yrk", "rk", 512)
        ts(r("rku"), r("pG", 0, 32), 512.0, A.add)
        tolist("pG", 0, "yrk", "ri", PT)
        ts(y("riu", 0), r("pG", 0, 34), 512.0, A.add, 512.0, A.min)
        act(sl(768, off=r("rku", 0, 16)), r("rec", 0, 256), AF.Silu)
        act(sl(768, off=r("rku", 16, 32)), r("rec", 256, 512), AF.Silu)
        ts(r("sl16"), sl(), K(US), A.mult, K(MN), A.min)
        tolist("pD", 0, "y0", "sl16", 512)
        cp(r("su"), r("pD", 0, 32))
        for a, b in ((0, CUTU), (CUTU, 32)):
            cp(r("nbu", 16 * a, 16 * b), r("nbi", off=r("su", a, b)))
        take(ENG["sv"], r("sv"), w(t + 1, 0, S1, off=r("su")))
        mm(r("pS"), r("ih"), r("sv"))
        tolist("pB", 0, "ycl", "sl16", 512)
        for k in range(3):
            ts(z("ne", k), r("pB", 0, 32), 4.0 + k, A.not_equal)
        scan(r("sa"), r("rm"), r("ne"), A.mult, A.add)
        tolist("pD", 32, "y123", "sl16", 512)
        lin(r("sf"), r("pD", 0, 64))
        tolist("pA", 0, "ypos", "sl16", 512)
        ts(r("v18"), r("pB", 0, 32), 4.0, A.is_ge, 18.0, A.mult)
        for k in range(3):
            ts(z("rq", k), z("ne", k), 83.0 - 2 * k, A.mult, 16.0 + 2 * k, A.add)
            ts(z("rq", 3 + k), z("ne", k), 2 * k - 83.0, A.mult, 99.0, A.add)
            tt(z("pp", k), r("pA", 0, 32), z("ne", k), A.max)
        lin(r("nq", 0, 3), r("ns", 0, 3), K(K0), -32.0)
        tt(r("nqh", 0, 3), r("nq", 0, 3), r("sa", 31, 96, 32), A.add)
        for k in range(2):
            ts(y("bb", k), y("jl", 0), c("af", 4 + k), A.is_ge, float(NB), A.mult)
            ts(y("rx", k), y("c16", 0), c("af", 4 + k), A.not_equal)
        tt(y("rx", 2), y("rx", 0), y("rx", 1), A.mult)
        if final:
            for h in range(4):
                ts(r("plf", O + 448 * h, O + 448 * h + 448), r("plt", O + 448 * h, O + 448 * h + 448), K(MG), A.add, MAGIC, A.subtract)
            ts(r("slr"), sl(), K(MG), A.add, MAGIC, A.subtract)
        for j0, j1, e in CHUNKS:
            take(e, r("gb", 16 * j0, 16 * j1), w(t + 1, O, WS, off=r("nbu", j0, j1)))
        jl = CHUNKS[-1][0]
        for o in (r("pE", 0, jl), r("pF", jl, 512)):
            mm(o, r("msk"), r("sl16", o[2], o[3]), True, False)
            mm(o, r("bd16"), r("sv", o[2], o[3]), False, False)
        for n, (j0, j1, e) in enumerate(CHUNKS):
            o = r("pE", j0, j1) if n < len(CHUNKS) - 1 else r("pF", j0, j1)
            for i in range(16):
                mm(o, r("bdn"), r("gb", 16 * j0 + i, 16 * j1, 16), False, False)
            for i in range(16):
                tt(r("mx", 512 * i + j0, 512 * i + j1), r("gb", 16 * j0 + i, 16 * j1, 16), r("pS", j0, j1), A.max)
                mm(o, r("bd2"), r("mx", 512 * i + j0, 512 * i + j1), False, i == 15 and n >= len(CHUNKS) - 2)
        act(r("sg", 0, jl), r("pE", 0, jl), AF.Sign, bias=K(THB))
        act(r("sg", jl, 512), r("pF", jl, 512), AF.Sign, bias=K(THB))
        for a, b, e in ((0, 18, "s"), (18, 34, "v")):
            take(e, r("tg", 16 * a, 16 * b), r("sg", off=r("riu", a, b)))
        mm(r("pA", 0, 32), r("ih"), r("v18"), True, False)
        tolist("pA", 0, "y01", "sg", 512, first=False)
        for k, x in enumerate((y("bb", 0), y("bb", 1), y("dl", 0))):
            mm(r("pD", 0, 34), r("ih"), x, k == 0, False)
        tolist("pB", 0, "ynl", "tg", PT)
        scan(y("tx", 0), y("rx", 2), r("pB", 0, 34), A.mult, A.add)
        cp(y("tx", 1), r("pB", 0, 34))
        tt(y("tx", 2), r("pB", 0, 34), y("dl", 0), A.mult)
        mm(r("pD", 0, 34), r("bd"), y("tx", 0), False, False)
        mm(r("pD", 0, 34), r("us"), y("tx", 1), False, False)
        mm(r("pD", 0, 34), r("ineg"), y("tx", 2), False, True)
        cp(y("itu", 0), r("pD", 0, 34))
        act(r("nl", 512, off=y("itu", 0)), r("tb"), AF.Silu)
        for k in range(3):
            tt(z("fl", k), r("pA", 0, 32), z("rq", k), A.is_equal)
        scan(r("s1", 0, 96), r("rm"), r("fl", 0, 96), A.mult, A.add)
        Lc, Nn = (lambda k: c("pC", k)), r("pG", 100, 103)
        mm(r("pC", 0, 3), r("bd"), r("nqh", 0, 3), True, False)
        mm(r("pC", 0, 3), r("bd"), r("s1", 31, 96, 32), False, True)
        tt(r("zz"), r("fl", 0, 96), r("pp"), A.max)
        for k in range(3):
            ts(z("ho", k), z("zz", k), 4096.0, A.mult, Lc(k), A.is_lt)
        scan(r("hs"), r("rm"), r("ho"), A.mult, A.add)
        mm(r("pE", 0, 128, 4), r("ih"), r("d1h"))
        for k in range(3):
            o = r("pE", 1 + k, 128, 4)
            mm(o, r("ic", 128 * k, 128 * k + 128), z("ho", k), True, False)
            mm(o, r("us"), z("ho", k), False, False)
            mm(o, r("bd"), z("hs", k), False, True)
        scan(r("o3"), r("rm4"), r("pE", 0, 128), A.mult, A.max)
        ts(r("ihu"), r("o3", 3, 128, 4), -1024.0, A.add)
        cp(r("occ"), r("nl", off=r("ihu")))
        for k in range(3):
            tt(z("fl", 3 + k), r("pA", 0, 32), z("rq", 3 + k), A.is_equal)
        scan(r("s1", 96, 192), r("rm"), r("fl", 96, 192), A.mult, A.add)
        mm(r("pG", 0, 96), r("i8k"), r("fl", 96, 192), True, False)
        mm(r("pG", 0, 96), r("usn"), r("fl", 96, 192), False, False)
        mm(r("pG", 0, 96), r("bdn"), r("s1", 96, 192), False, True)
        mm(Nn, r("bd"), r("nqh", 0, 3), True, False)
        mm(Nn, r("bd"), r("s1", 31, 96, 32), False, False)
        mm(Nn, r("bd"), r("s1", 127, 192, 32), False, True)
        for k in range(3):
            ts(r("vv", 1 + k, 128, 4), z("pG", k), c("pG", 100 + k), A.add, B0 + V * k - 8192.0, A.add)
        scan(r("o4"), r("rm4"), r("vv"), A.mult, A.max)
        npl = r("o4", 3, 128, 4)
        if not final:
            cp(r("jou"), npl)
            if ENG["jou"] == "v":
                cp(r("bag", off=r("jou")), sl())
            else:
                act(r("bag", off=r("jou")), sl(), AF.Silu)
            ts(z("hv", 0), r("o3", 3, 128, 4), 1536.0, A.is_gt)
            tt(z("hv", 1), z("hv", 0), z("sf", 1), A.mult)
            tt(z("hv", 2), z("hv", 1), r("jl", 0, 32), A.max)
            cp(r("hou"), z("hv", 2))
            draw(t + 1, Nn)
            cp(r("bag", off=r("hou")), r("occ"))
        ts(z("lv", 0), npl, float(B0), A.is_lt, 4096.0, A.mult)
        tt(z("lv", 1), z("lv", 0), z("sf", 0), A.add)
        tt(z("lv", 2), z("lv", 1), r("d2k"), A.min)
        cp(r("lvu"), z("lv", 2))
        lin(r("pq"), r("pA", 0, 32), -V / 2, 8.0 * V - B0)
        tt(r("posl"), npl, r("pq"), A.add)
        mm(r("pS"), r("mcl"), r("sg", 0, 512), True, False)
        if not final:
            mm(r("pS"), r("i0"), r("sl16"), False, False)
        for a in range(16):
            mm(r("pS", a, 512, 16), r("selt", 128 * a, 128 * a + 128), r("posl"), False, a == 15)
        act(r("nrec"), r("pS"), AF.Relu, scale=K(RS), bias=K(RF if final else RN))
        tolist("pF", 0, "y0", "occ", 512)
        cp(r("stu"), r("pF", 0, 32))
        if final:
            cp(r("plf", off=r("lvu")), r("nrec"))
            cp(r("plf", off=r("stu")), r("slr"))
            op("y", lambda q, a, k: q.dma_start(T.yp[:, :], T.plf[9:128:16, O:S1]), [], {}, [r("plf", p=(0, 8))], [], ("dma%d" % nd[0], 16, True), "dma")
        else:
            act(r("plt", off=r("lvu")), r("nrec"), AF.Silu)
            mm(r("pB"), r("i0"), r("occ"), True, False)
            mm(r("pB"), r("mh0"), r("sl16"), False, False)
            mm(r("pB"), r("y123", 6, 134), r("sl16"), False, True)
            act(r("hf"), r("pB"))
            act(r("plt", off=r("stu")), r("hf"), AF.Silu)
    if not ORDERS:
        order = schedule(ops)
        ORDERS[0] = (order, depend([ops[k] for k in order], False))
    emit(g, T, [ops[k] for k in ORDERS[0][0]], ORDERS[0][1])
